import numpy as np
import ml_dtypes


def mxq(x, axis, fmt="e4m3"):
    dtype, down = {"e4m3": (ml_dtypes.float8_e4m3fn, 7), "e5m2": (ml_dtypes.float8_e5m2, 14)}[fmt]
    v = np.moveaxis(np.asarray(x, np.float32).astype(ml_dtypes.bfloat16).astype(np.float64), axis, -1)
    blocks = v.reshape(v.shape[:-1] + (-1, 32))
    amax = np.abs(blocks).max(-1, keepdims=True)
    byte = np.maximum(np.where(amax > 0, np.frexp(amax)[1] - 1 + 127, 0) - down, 1)
    scale = np.exp2(byte - 127.0)
    codes = (blocks / scale).astype(np.float32).astype(dtype).astype(np.float64)
    return np.moveaxis((codes * scale).reshape(v.shape), -1, axis)


WIDE = False


def mx_kscale(k):
    if not WIDE:
        return np.ones(k)
    levels = np.array([10, -10, 5, -5, 0])
    if k % 512:
        return np.exp2(np.random.permutation(np.resize(levels, k // 32))).repeat(32)
    a = np.empty((k // 512, 16))
    for p in range(k // 512):
        a[p, :8] = np.random.permutation(np.resize(levels, 8))
        for g in range(8):
            far = levels[np.abs(levels - a[p, g]) >= 10]
            a[p, g + 8] = far[np.random.randint(len(far))]
    return np.exp2(a.ravel()).repeat(32)


BF16 = ml_dtypes.bfloat16


def bf(x):
    return np.asarray(x, np.float32).astype(BF16)


def f64(x):
    return np.asarray(x).astype(np.float64)


E2M1 = np.array([0.0, 0.5, 1.0, 1.5, 2.0, 3.0, 4.0, 6.0, -0.0, -0.5, -1.0, -1.5, -2.0, -3.0, -4.0, -6.0])


def pack_weight(w, fmt):
    k, n = w.shape
    w = f64(bf(w)).reshape(k // 32, 32, n)
    amax = np.abs(w).max(1)
    if fmt == "e4m3":
        byte = np.frexp(amax)[1] - 1 + 127 - 7
    else:
        mant, ex = np.frexp(amax / 6.0)
        byte = np.where(mant > 0.5, ex, ex - 1) + 127
    byte = np.clip(np.where(amax > 0, byte, 1), 1, 254)
    scaled = (w * np.exp2(127.0 - byte)[:, None, :]).reshape(k, n).astype(np.float32)
    by_word = np.ascontiguousarray(scaled.reshape(k // 512, 128, 4, n).transpose(0, 1, 3, 2))
    if fmt == "e4m3":
        words = by_word.astype(ml_dtypes.float8_e4m3fn).view(np.uint8)
    else:
        c = by_word.astype(ml_dtypes.float4_e2m1fn).view(np.uint8) & 0xF
        words = c[..., 0::2] | (c[..., 1::2] << 4)
    return np.ascontiguousarray(words), np.ascontiguousarray(byte.astype(np.uint8).reshape(k // 512, 16, n))


def unpack_weight(words, scales, fmt):
    g, p, n, _ = words.shape
    if fmt == "e4m3":
        vals = np.ascontiguousarray(words).view(ml_dtypes.float8_e4m3fn).astype(np.float64)
    else:
        nib = np.empty((g, p, n, 4), np.uint8)
        nib[..., 0::2] = words & 0xF
        nib[..., 1::2] = words >> 4
        vals = E2M1[nib]
    vals = vals * np.repeat(np.exp2(scales.astype(np.float64) - 127.0), 8, axis=1)[..., None]
    return vals.transpose(0, 1, 3, 2).reshape(g * 512, n)
def pack4(w):
    words, scales = pack_weight(w, "e2m1")
    return words.reshape(words.shape[0], 128, -1), scales


def unpack4(words, scales):
    return unpack_weight(words.reshape(words.shape[0], 128, -1, 2), scales, "e2m1")


M, K, C, F, R = 1024, 1536, 1024, 2048, 512


def draw0():
    s = mx_kscale(K)
    t = mx_kscale(C)
    u = mx_kscale(M)
    x = np.random.standard_normal((M, K)) * s * u[:, None]
    w = np.random.standard_normal((K, C)) / np.sqrt(K) / s[:, None] * t
    prior = 0.5 * np.random.standard_normal((M, C)) * u[:, None] * t
    basis = 0.5 * np.random.standard_normal((C, F)) / np.sqrt(C) / t[:, None]
    depth = (1 + 0.1 * np.random.standard_normal(M)) / u
    pop = np.random.standard_normal((R, M)) / np.sqrt(M) / u
    basis_words, basis_scales = pack4(basis)
    return {"x": bf(x), "w": bf(w), "prior": bf(prior),
            "basis_words": basis_words, "basis_scales": basis_scales,
            "depth": bf(depth), "pop": bf(pop)}


def core(x, w, prior, basis_words, basis_scales, depth, pop):
    h = (mxq(f64(x), 1, "e4m3") @ mxq(f64(w), 0, "e4m3")) + f64(prior)
    logmag = mxq(h, 1, "e4m3") @ unpack4(basis_words, basis_scales)
    mag = np.exp(f64(depth)[:, None] * logmag)
    load = mxq(f64(pop), 1, "e4m3") @ mxq(h, 0, "e4m3")
    return mag, load


def e4m3fn_bytes(y):
    return np.clip(np.asarray(y, np.float64), -448.0, 448.0).astype(np.float32).astype(ml_dtypes.float8_e4m3fn).view(np.uint8)


def e4m3fn_values(b):
    return np.asarray(b, np.uint8).view(ml_dtypes.float8_e4m3fn).astype(np.float64)


def setup_inputs():
    d = draw0()
    x0 = np.asarray(d['pop']).astype(np.float64)
    s = (np.max(np.abs(x0), axis=(0,), keepdims=True) / 448.0).astype(np.float32)
    out = {}
    for k, v in d.items():
        if k == 'pop':
            out['pop_bytes'] = e4m3fn_bytes(x0 / s.astype(np.float64))
            out['pop_scale'] = s
        else:
            out[k] = v
    return out


def reference(x, w, prior, basis_words, basis_scales, depth, pop_bytes, pop_scale):
    return core(x, w, prior, basis_words, basis_scales, depth, e4m3fn_values(pop_bytes) * pop_scale.astype(np.float64))

@@ -1,0 +1,502 @@
+from contextlib import ExitStack
+
+import concourse.mybir as mybir
+from concourse.masks import make_identity
+
+M, K, C, F, R = 1024, 1536, 1024, 2048, 512
+FLOPS = 2 * (M * K * C + M * C * F + R * M * C)
+
+F32 = mybir.dt.float32
+BF16 = mybir.dt.bfloat16
+U32 = mybir.dt.uint32
+I32 = mybir.dt.int32
+U8 = mybir.dt.uint8
+E4M3 = mybir.dt.float8_e4m3fn_x4
+E2M1 = mybir.dt.float4_e2m1fn_x4
+FP8 = mybir.dt.float8_e4m3fn
+ADD = mybir.AluOpType.add
+MULT = mybir.AluOpType.mult
+EXP = mybir.ActivationFunctionType.Exp
+
+P = 128
+HALF = 512
+V_COLS = (256, 224)
+
+
+def tile_hrtf_weights_synthesis_s8_kernel(
+    tc, x, w, prior, basis_words, basis_scales, depth, pop_bytes, pop_scale, mag, load
+):
+    nc = tc.nc
+    with ExitStack() as ctx:
+        keep = ctx.enter_context(tc.tile_pool(name="keep", bufs=1))
+        stage = ctx.enter_context(tc.tile_pool(name="stage", bufs=4))
+        outs = ctx.enter_context(tc.tile_pool(name="outs", bufs=3))
+        psum = ctx.enter_context(tc.psum_pool(name="psum", bufs=8))
+        ctx.enter_context(tc.manual_schedule())
+
+        def bank():
+            b = psum.tile([P, 512], F32, name="bank")
+            return b
+
+        def kept(name, shape, dt):
+            t = keep.tile(shape, dt, name=name, align_bytes=64)
+            return t
+
+        ident = kept("ident", [P, P], F32)
+        dummy = kept("dummy", [P, 1], F32)
+        zeros = kept("zeros", [P, 512], BF16)
+        x_raw = [
+            outs.tile([P, 2, K], BF16, name="x_raw%d" % i, tag="big", bufs=4, align_bytes=64) for i in range(4)
+        ]
+        w_raw = [
+            [
+                outs.tile([P, 4, HALF], BF16, name="w_raw%d%d" % (h, q), tag="small", bufs=6, align_bytes=64)
+                for q in range(3)
+            ]
+            for h in range(2)
+        ]
+        pr = [[kept("pr%d%d" % (g, z), [P, 2, C], BF16) for z in range(2)] for g in range(2)]
+        b_words = kept("b_words", [P, 2, 2 * F], U8)
+        b_scales = kept("b_scales", [P, 2, F], U8)
+        depth_bf = kept("depth_bf", [P, 2, 4], BF16)
+        depth_f = kept("depth_f", [P, 8], F32)
+        pop_raw = kept("pop_raw", [P, 4, M], U8)
+        pop_sc = kept("pop_sc", [P, M], F32)
+        pop_bf = kept("pop_bf", [P, 4, M], BF16)
+        x_c = [kept("x_c%d" % i, [P, 3, 256], U32) for i in range(4)]
+        x_s = [kept("x_s%d" % i, [P, 3, 256], U8) for i in range(4)]
+        w_c = [[kept("w_c%d%d" % (h, q), [P, HALF], U32) for q in range(3)] for h in range(2)]
+        w_s = [[kept("w_s%d%d" % (h, q), [P, HALF], U8) for q in range(3)] for h in range(2)]
+        hb = [kept("hb%d" % g, [P, 4, C], BF16) for g in range(2)]
+        ht_c = [kept("ht_c%d" % i, [P, 2, P], U32) for i in range(8)]
+        ht_s = [kept("ht_s%d" % i, [P, 2, P], U8) for i in range(8)]
+        h_c = [kept("h_c%d" % g, [P, C], U32) for g in range(2)]
+        h_s = [kept("h_s%d" % g, [P, C], U8) for g in range(2)]
+        p_c = [kept("p_c%d" % g, [P, R], U32) for g in range(2)]
+        p_s = [kept("p_s%d" % g, [P, R], U8) for g in range(2)]
+
+        nc.vector.memset(zeros[:], 0.0)
+        nc.vector.memset(dummy[:], 0.0)
+        nc.scalar.activation(out=dummy[:], in_=dummy[:], func=EXP)
+        make_identity(nc, ident[:])
+        nc.gpsimd.memset(b_scales[:].rearrange("p g n -> p (g n)").bitcast(I32), 0)
+
+        def load_x(i):
+            g, t0 = i // 2, 2 * (i % 2)
+            src = x[g * 512:(g + 1) * 512, :].rearrange("(p t) k -> p t k", t=4)
+            for a in range(2):
+                nc.sync.dma_start(out=x_raw[i][:, a, :], in_=src[:, t0 + a, :])
+
+        def load_w(h, q):
+            src = w[q * 512:(q + 1) * 512, h * HALF:(h + 1) * HALF]
+            nc.sync.dma_start(out=w_raw[h][q][:], in_=src.rearrange("(p j) c -> p j c", j=4))
+
+        def load_prior(g, z):
+            src = prior[g * 512:(g + 1) * 512, :].rearrange("(p t) c -> p t c", t=4)
+            nc.sync.dma_start(out=pr[g][z][:], in_=src[:, 2 * z:2 * z + 2, :])
+
+        load_x(0)
+        load_w(0, 0)
+        load_w(0, 1)
+        load_x(1)
+        load_x(2)
+        load_w(0, 2)
+        load_x(3)
+        load_w(1, 0)
+        load_w(1, 1)
+        load_prior(0, 0)
+        load_prior(0, 1)
+        load_w(1, 2)
+        load_prior(1, 0)
+        load_prior(1, 1)
+        nc.sync.dma_start(
+            out=b_words[:].rearrange("p g n -> p (g n)").bitcast(I32).rearrange("p (g n) -> p g n", g=2),
+            in_=basis_words.bitcast(I32).rearrange("g p n -> p g n"),
+        )
+        b_scales_i = b_scales[:].rearrange("p g n -> p (g n)").bitcast(I32).rearrange("p (g n) -> p g n", g=2)
+        for quad in range(4):
+            nc.sync.dma_start(
+                out=b_scales_i[32 * quad:32 * quad + 4],
+                in_=basis_scales.bitcast(I32)[:, 4 * quad:4 * quad + 4, :].rearrange("g r n -> r g n"),
+            )
+        nc.sync.dma_start(out=depth_bf[:], in_=depth.rearrange("(g p t) -> p g t", p=P, t=4))
+        nc.sync.dma_start(out=pop_raw[:], in_=pop_bytes.rearrange("(p a) k -> p a k", a=4))
+        nc.sync.dma_start(out=pop_sc[:], in_=pop_scale.rearrange("o k -> (o k)").partition_broadcast(P))
+
+        def words(tile_ap):
+            return tile_ap.bitcast(F32)
+
+        x_banks = {}
+
+        def warm(n, rhs):
+            b = bank()
+            for k in range(n):
+                nc.tensor.matmul(b[:], lhsT=zeros[:, 0:P], rhs=rhs, start=True, stop=True)
+
+        def x_turn(i):
+            for q in range(3):
+                b = bank()
+                x_banks[i, q] = b
+            for a in range(2):
+                xw = words(x_raw[i][:, a, :])
+                for q in range(3):
+                    for u in range(2):
+                        col = (2 * a + u) * P
+                        nc.tensor.transpose(
+                            x_banks[i, q][:, col:col + P], xw[:, 256 * q + u:256 * (q + 1):2], ident[:]
+                        )
+                if i < 3:
+                    warm(1, zeros[:])
+
+        def copy(engine, out, in_):
+            if engine == "S":
+                nc.scalar.copy(out=out, in_=in_)
+            else:
+                nc.vector.tensor_copy(out=out, in_=in_)
+
+        x_grouped = {}
+
+        def x_empty(i, q, engine):
+            if i not in x_grouped:
+                xg = stage.tile([P, 3, 2, P, 4], BF16, name="xg", bufs=2, align_bytes=64)
+                x_grouped[i] = xg
+            copy(
+                engine,
+                words(x_grouped[i][:, q].rearrange("p a m t -> p (a m t)")).rearrange("p (a m u) -> p a m u", a=2, u=2),
+                x_banks[i, q][:].rearrange("p (a u m) -> p a m u", a=2, u=2),
+            )
+
+        def x_quant(i, q0, q1):
+            nc.vector.quantize_mx(
+                out=x_c[i][:, q0:q1, :].rearrange("p q m -> p (q m)").bitcast(E4M3),
+                scales=x_s[i][:, q0:q1, :].rearrange("p q m -> p (q m)"),
+                in_=x_grouped[i][:, q0:q1].rearrange("p q a m t -> p (q a m t)"),
+            )
+
+        w_grouped = {}
+
+        def w_group(h, q, engine):
+            if (h, q) not in w_grouped:
+                wg = stage.tile([P, HALF, 4], BF16, name="wg", bufs=3, align_bytes=64)
+                w_grouped[h, q] = wg
+            cols = slice(0, V_COLS[h]) if engine == "V" else slice(V_COLS[h], HALF)
+            copy(engine, w_grouped[h, q][:, cols, :], w_raw[h][q][:, :, cols].rearrange("p j c -> p c j"))
+
+        def w_quant(h, q):
+            nc.vector.quantize_mx(
+                out=w_c[h][q][:].bitcast(E4M3),
+                scales=w_s[h][q][:],
+                in_=w_grouped[h, q][:].rearrange("p c j -> p (c j)"),
+            )
+
+        h_banks = {}
+
+        def h_pass(i, h, q):
+            if q == 0:
+                b = bank()
+                h_banks[i, h] = b
+            cols = slice((i % 2) * P, (i % 2 + 1) * P)
+            nc.tensor.matmul_mx(
+                out=h_banks[i, h][:],
+                lhsT=x_c[i // 2][:, q, cols].bitcast(E4M3),
+                lhsT_scale=x_s[i // 2][:, q, cols],
+                rhs=w_c[h][q][:].bitcast(E4M3),
+                rhs_scale=w_s[h][q][:],
+                start=(q == 0),
+                stop=(q == 2),
+            )
+
+        def h_add(i, h):
+            g, t = i // 4, i % 4
+            nc.vector.tensor_tensor(
+                out=hb[g][:, t, h * HALF:(h + 1) * HALF].rearrange("q (u p e) -> q u p e", u=2, e=2),
+                in0=h_banks[i, h][:].rearrange("q (p u e) -> q u p e", u=2, e=2),
+                in1=pr[g][t // 2][:, t % 2, h * HALF:(h + 1) * HALF].rearrange("q (p u e) -> q u p e", u=2, e=2),
+                op=ADD,
+            )
+
+        ht_banks = {}
+
+        def ht_turn(i):
+            g, t = i // 4, i % 4
+            b = bank()
+            ht_banks[i] = b
+            hw = words(hb[g][:, t, :])
+            for v in range(4):
+                nc.tensor.transpose(b[:, v * P:(v + 1) * P], hw[:, v * P:(v + 1) * P], ident[:])
+
+        ht_grouped = {}
+
+        def ht_empty(i, engine):
+            hg = stage.tile([P, 2, P, 4], BF16, name="hg", align_bytes=64)
+            ht_grouped[i] = hg
+            copy(
+                engine,
+                words(hg[:].rearrange("p a m t -> p (a m t)")).rearrange("p (a m u) -> p a m u", a=2, u=2),
+                ht_banks[i][:].rearrange("p (a u m) -> p a m u", a=2, u=2),
+            )
+
+        def ht_quant(i):
+            nc.vector.quantize_mx(
+                out=ht_c[i][:].rearrange("p a m -> p (a m)").bitcast(E4M3),
+                scales=ht_s[i][:].rearrange("p a m -> p (a m)"),
+                in_=ht_grouped[i][:].rearrange("p a m t -> p (a m t)"),
+            )
+
+        mag_rows = mag.rearrange("(g p t) f -> g t p f", p=P, t=4)
+        mag_banks = {}
+
+        def mag_mm(i, f):
+            b = bank()
+            mag_banks[i, f] = b
+            for a in range(2):
+                nc.tensor.matmul_mx(
+                    out=b[:],
+                    lhsT=ht_c[i][:, a, :].bitcast(E4M3),
+                    lhsT_scale=ht_s[i][:, a, :],
+                    rhs=b_words[:, a, 1024 * f:1024 * (f + 1)].bitcast(E2M1),
+                    rhs_scale=b_scales[:, a, 512 * f:512 * (f + 1)],
+                    start=(a == 0),
+                    stop=(a == 1),
+                )
+
+        mag_tiles = {}
+
+        def mag_exp(i, f):
+            if f == 0:
+                mo = outs.tile([P, F], F32, name="mo", tag="big", bufs=4, align_bytes=64)
+                mag_tiles[i] = mo
+            nc.scalar.activation(
+                out=mag_tiles[i][:, 512 * f:512 * (f + 1)], in_=mag_banks[i, f][:], func=EXP, scale=depth_f[:, i:i + 1]
+            )
+
+        def mag_store(i, c0, c1):
+            cols = slice(c0, c1)
+            nc.sync.dma_start(out=mag_rows[i // 4, i % 4, :, cols], in_=mag_tiles[i][:, cols])
+
+        h_grouped = {}
+
+        def h_group(g, h, engine):
+            group = stage.tile([P, HALF, 4], BF16, name="group", bufs=3, align_bytes=64)
+            h_grouped[g, h] = group
+            cols = slice(HALF * h, HALF * (h + 1))
+            copy(engine, group[:], hb[g][:, :, cols].rearrange("p t c -> p c t"))
+
+        def h_quant(g, h):
+            cols = slice(HALF * h, HALF * (h + 1))
+            nc.vector.quantize_mx(
+                out=h_c[g][:, cols].bitcast(E4M3),
+                scales=h_s[g][:, cols],
+                in_=h_grouped[g, h][:].rearrange("p c t -> p (c t)"),
+            )
+
+        pop_banks = {}
+
+        def pop_product(a):
+            nc.vector.tensor_tensor(out=pop_bf[:, a, :], in0=pop_raw[:, a, :].bitcast(FP8), in1=pop_sc[:], op=MULT)
+
+        def pop_turn(g, z):
+            b = bank()
+            pop_banks[g, z] = b
+            for a in range(2):
+                pw = words(pop_bf[:, 2 * z + a, :])
+                for u in range(2):
+                    col = (2 * a + u) * P
+                    nc.tensor.transpose(b[:, col:col + P], pw[:, 256 * g + u:256 * (g + 1):2], ident[:])
+
+        pop_grouped = {}
+
+        def pop_empty(g, z, engine):
+            if g not in pop_grouped:
+                group = stage.tile([P, 2, 2, P, 4], BF16, name="group", bufs=3, align_bytes=64)
+                pop_grouped[g] = group
+            copy(
+                engine,
+                words(pop_grouped[g][:, z].rearrange("p a r t -> p (a r t)")).rearrange("p (a r u) -> p a r u", a=2, u=2),
+                pop_banks[g, z][:].rearrange("p (a u r) -> p a r u", a=2, u=2),
+            )
+
+        def pop_quant(g):
+            nc.vector.quantize_mx(
+                out=p_c[g][:].bitcast(E4M3),
+                scales=p_s[g][:],
+                in_=pop_grouped[g][:].rearrange("p z a r t -> p (z a r t)"),
+            )
+
+        load_rows = load.rearrange("(p a) c -> a p c", a=4)
+        load_banks = {}
+
+        def load_mm(a, h):
+            b = bank()
+            load_banks[a, h] = b
+            for g in range(2):
+                nc.tensor.matmul_mx(
+                    out=b[:],
+                    lhsT=p_c[g][:, P * a:P * (a + 1)].bitcast(E4M3),
+                    lhsT_scale=p_s[g][:, P * a:P * (a + 1)],
+                    rhs=h_c[g][:, 512 * h:512 * (h + 1)].bitcast(E4M3),
+                    rhs_scale=h_s[g][:, 512 * h:512 * (h + 1)],
+                    start=(g == 0),
+                    stop=(g == 1),
+                )
+
+        load_tiles = {}
+
+        def load_empty(a, h, engine):
+            if a not in load_tiles:
+                lo = outs.tile([P, C], F32, name="lo", tag="small", bufs=6, align_bytes=64)
+                load_tiles[a] = lo
+            copy(
+                engine,
+                load_tiles[a][:, 512 * h:512 * (h + 1)].rearrange("q (p u e) -> q p u e", u=2, e=2),
+                load_banks[a, h][:].rearrange("q (u p e) -> q p u e", u=2, e=2),
+            )
+
+        def load_store(a, halves):
+            for h in range(halves):
+                cols = slice(C // halves * h, C // halves * (h + 1))
+                nc.sync.dma_start(out=load_rows[a, :, cols], in_=load_tiles[a][:, cols])
+
+
+        def x_step(i, vector_banks):
+            for q in range(3):
+                x_empty(i, q, "V" if q in vector_banks else "S")
+
+        def x_quants(i):
+            x_quant(i, 0, 2)
+            x_quant(i, 2, 3)
+
+        def w_step(h, q):
+            w_group(h, q, "V")
+            w_group(h, q, "S")
+
+        def h_passes(tiles, h, passes):
+            for q in passes:
+                for i in tiles:
+                    h_pass(i, h, q)
+
+        def h_all(i, h):
+            h_passes((i,), h, range(3))
+
+        def mag_step(i, run=2):
+            for f in range(4):
+                mag_mm(i, f)
+                mag_exp(i, f)
+                if (f + 1) % run == 0:
+                    mag_store(i, 512 * (f + 1 - run), 512 * (f + 1))
+
+        def load_step(a, engines):
+            for h in range(2):
+                load_mm(a, h)
+                load_empty(a, h, engines[h])
+            load_store(a, 1)
+
+        warm(8, zeros[:])
+        x_turn(0)
+        w_step(0, 0)
+        w_step(0, 1)
+        x_step(0, (1,))
+        w_quant(0, 0)
+        x_quants(0)
+        w_quant(0, 1)
+        warm(2, w_raw[0][0][:, 0, :])
+        warm(2, w_raw[0][1][:, 0, :])
+        x_turn(1)
+        x_step(1, (0,))
+        x_turn(2)
+        x_quant(1, 0, 2)
+        w_group(0, 2, "V")
+        x_step(2, (2,))
+        w_group(0, 2, "S")
+        x_quants(2)
+        x_quant(1, 2, 3)
+        w_quant(0, 2)
+        h_passes(range(4), 0, (0,))
+        x_turn(3)
+        x_step(3, ())
+        h_passes(range(4), 0, (1, 2))
+        w_step(1, 0)
+        x_quant(3, 0, 2)
+        w_step(1, 1)
+        x_quant(3, 2, 3)
+        h_all(4, 0)
+        h_all(5, 0)
+        h_add(0, 0)
+        w_quant(1, 0)
+        h_add(1, 0)
+        w_quant(1, 1)
+        h_add(2, 0)
+        w_step(1, 2)
+        h_add(3, 0)
+        w_quant(1, 2)
+        h_all(6, 0)
+        h_add(4, 0)
+        h_add(5, 0)
+        h_passes((0, 1), 1, (0, 1))
+        h_all(7, 0)
+        h_passes((2,), 1, (0, 1))
+        h_passes((0, 1, 2), 1, (2,))
+        h_all(3, 1)
+        for i in range(4):
+            h_add(i, 1)
+        h_all(4, 1)
+        h_all(5, 1)
+        h_add(4, 1)
+        h_add(5, 1)
+        for i in range(4):
+            ht_turn(i)
+        for i in range(4):
+            ht_empty(i, "SSVS"[i])
+        h_add(6, 0)
+        ht_quant(0)
+        ht_quant(1)
+        h_add(7, 0)
+        ht_quant(2)
+        ht_quant(3)
+        nc.vector.tensor_copy(out=depth_f[:], in_=depth_bf[:].rearrange("p g t -> p (g t)"))
+        h_all(6, 1)
+        h_all(7, 1)
+        pop_product(0)
+        h_group(0, 0, "S")
+        mag_step(0)
+        h_add(6, 1)
+        h_add(7, 1)
+        mag_step(1)
+        h_group(0, 1, "V")
+        h_quant(0, 0)
+        pop_product(1)
+        h_quant(0, 1)
+        for i in range(4, 8):
+            ht_turn(i)
+        ht_empty(4, "S")
+        ht_empty(5, "V")
+        pop_product(2)
+        ht_empty(6, "S")
+        ht_empty(7, "V")
+        ht_quant(4)
+        ht_quant(5)
+        mag_step(2)
+        pop_product(3)
+        ht_quant(6)
+        ht_quant(7)
+        h_group(1, 0, "V")
+        mag_step(3)
+        for z in range(2):
+            for g in range(2):
+                pop_turn(g, z)
+        for z in range(2):
+            for g in range(2):
+                pop_empty(g, z, "VS"[g])
+        mag_step(4)
+        h_quant(1, 0)
+        pop_quant(0)
+        h_group(1, 1, "V")
+        pop_quant(1)
+        h_quant(1, 1)
+        mag_step(5)
+        mag_step(6)
+        load_step(0, "VV")
+        load_step(1, "VV")
+        load_step(2, "VS")
+        load_step(3, "VS")
+        mag_step(7, run=1)

@@ -20,7 +20,6 @@ EXP = mybir.ActivationFunctionType.Exp
 
 P = 128
 HALF = 512
-V_COLS = (256, 224)
 
 
 def tile_hrtf_weights_synthesis_s8_kernel(
@@ -31,11 +30,21 @@ def tile_hrtf_weights_synthesis_s8_kernel(
         keep = ctx.enter_context(tc.tile_pool(name="keep", bufs=1))
         stage = ctx.enter_context(tc.tile_pool(name="stage", bufs=4))
         outs = ctx.enter_context(tc.tile_pool(name="outs", bufs=3))
-        psum = ctx.enter_context(tc.psum_pool(name="psum", bufs=8))
+        psum = ctx.enter_context(tc.psum_pool(name="psum", bufs=1))
         ctx.enter_context(tc.manual_schedule())
 
-        def bank():
-            b = psum.tile([P, 512], F32, name="bank")
+        free_banks = list(range(8))
+        bank_of = {}
+
+        def take_bank(key):
+            number = free_banks.pop(0)
+            b = psum.tile([P, 512], F32, name="bank%d" % number)
+            bank_of[key] = (b, number)
+            return b
+
+        def give_bank(key):
+            b, number = bank_of[key]
+            free_banks.append(number)
             return b
 
         def kept(name, shape, dt):
@@ -46,7 +55,7 @@ def tile_hrtf_weights_synthesis_s8_kernel(
         dummy = kept("dummy", [P, 1], F32)
         zeros = kept("zeros", [P, 512], BF16)
         x_raw = [
-            outs.tile([P, 2, K], BF16, name="x_raw%d" % i, tag="big", bufs=4, align_bytes=64) for i in range(4)
+            outs.tile([P, K], BF16, name="x_raw%d" % i, tag="big", bufs=8, align_bytes=64) for i in range(8)
         ]
         w_raw = [
             [
@@ -55,19 +64,21 @@ def tile_hrtf_weights_synthesis_s8_kernel(
             ]
             for h in range(2)
         ]
-        pr = [[kept("pr%d%d" % (g, z), [P, 2, C], BF16) for z in range(2)] for g in range(2)]
+        pr_half = [kept("pr_half%d" % h, [P, 4, HALF], BF16) for h in range(2)]
+        pr_pair = [kept("pr_pair%d" % z, [P, 2, C], BF16) for z in range(2)]
         b_words = kept("b_words", [P, 2, 2 * F], U8)
         b_scales = kept("b_scales", [P, 2, F], U8)
         depth_bf = kept("depth_bf", [P, 2, 4], BF16)
         depth_f = kept("depth_f", [P, 8], F32)
         pop_raw = kept("pop_raw", [P, 4, M], U8)
-        pop_sc = kept("pop_sc", [P, M], F32)
-        pop_bf = kept("pop_bf", [P, 4, M], BF16)
+        pop_sc = kept("pop_sc", [P, 2, 4], F32)
+        one = kept("one", [P, 1], F32)
+        pop_bf = [kept("pop_bf%d" % a, [P, M], BF16) for a in range(4)]
         x_c = [kept("x_c%d" % i, [P, 3, 256], U32) for i in range(4)]
         x_s = [kept("x_s%d" % i, [P, 3, 256], U8) for i in range(4)]
         w_c = [[kept("w_c%d%d" % (h, q), [P, HALF], U32) for q in range(3)] for h in range(2)]
         w_s = [[kept("w_s%d%d" % (h, q), [P, HALF], U8) for q in range(3)] for h in range(2)]
-        hb = [kept("hb%d" % g, [P, 4, C], BF16) for g in range(2)]
+        hb = [[kept("hb%d%d" % (g, h), [P, 4 * HALF], BF16) for h in range(2)] for g in range(2)]
         ht_c = [kept("ht_c%d" % i, [P, 2, P], U32) for i in range(8)]
         ht_s = [kept("ht_s%d" % i, [P, 2, P], U8) for i in range(8)]
         h_c = [kept("h_c%d" % g, [P, C], U32) for g in range(2)]
@@ -77,76 +88,88 @@ def tile_hrtf_weights_synthesis_s8_kernel(
 
         nc.vector.memset(zeros[:], 0.0)
         nc.vector.memset(dummy[:], 0.0)
+        nc.vector.memset(one[:], 1.0)
         nc.scalar.activation(out=dummy[:], in_=dummy[:], func=EXP)
         make_identity(nc, ident[:])
         nc.gpsimd.memset(b_scales[:].rearrange("p g n -> p (g n)").bitcast(I32), 0)
 
         def load_x(i):
-            g, t0 = i // 2, 2 * (i % 2)
+            g, t = i // 4, i % 4
             src = x[g * 512:(g + 1) * 512, :].rearrange("(p t) k -> p t k", t=4)
-            for a in range(2):
-                nc.sync.dma_start(out=x_raw[i][:, a, :], in_=src[:, t0 + a, :])
+            nc.sync.dma_start(out=x_raw[i][:], in_=src[:, t, :])
 
         def load_w(h, q):
             src = w[q * 512:(q + 1) * 512, h * HALF:(h + 1) * HALF]
             nc.sync.dma_start(out=w_raw[h][q][:], in_=src.rearrange("(p j) c -> p j c", j=4))
 
-        def load_prior(g, z):
-            src = prior[g * 512:(g + 1) * 512, :].rearrange("(p t) c -> p t c", t=4)
-            nc.sync.dma_start(out=pr[g][z][:], in_=src[:, 2 * z:2 * z + 2, :])
+        def load_prior_half(h):
+            src = prior[0:512, h * HALF:(h + 1) * HALF]
+            nc.sync.dma_start(out=pr_half[h][:], in_=src.rearrange("(p t) c -> p t c", t=4))
+
+        def load_prior_pair(z):
+            src = prior[512:1024, :].rearrange("(p t) c -> p t c", t=4)
+            nc.sync.dma_start(out=pr_pair[z][:], in_=src[:, 2 * z:2 * z + 2, :])
+
+        def prior_of(i, h):
+            if i < 4:
+                return pr_half[h][:, i, :]
+            return pr_pair[(i - 4) // 2][:, i % 2, h * HALF:(h + 1) * HALF]
+
+        def load_basis():
+            b_scales_i = b_scales[:].rearrange("p g n -> p (g n)").bitcast(I32).rearrange("p (g n) -> p g n", g=2)
+            for quad in range(4):
+                nc.sync.dma_start(
+                    out=b_scales_i[32 * quad:32 * quad + 4],
+                    in_=basis_scales.bitcast(I32)[:, 4 * quad:4 * quad + 4, :].rearrange("g r n -> r g n"),
+                )
+            nc.sync.dma_start(out=depth_bf[:], in_=depth.rearrange("(g p t) -> p g t", p=P, t=4))
+            nc.sync.dma_start(
+                out=b_words[:].rearrange("p g n -> p (g n)").bitcast(I32).rearrange("p (g n) -> p g n", g=2),
+                in_=basis_words.bitcast(I32).rearrange("g p n -> p g n"),
+            )
+
+        def load_pop():
+            nc.sync.dma_start(out=pop_raw[:], in_=pop_bytes.rearrange("(p a) k -> p a k", a=4))
+            nc.sync.dma_start(out=pop_sc[:], in_=pop_scale.rearrange("o (g p t) -> p (o g) t", p=P, t=4))
 
         load_x(0)
-        load_w(0, 0)
-        load_w(0, 1)
         load_x(1)
+        load_w(0, 0)
         load_x(2)
-        load_w(0, 2)
         load_x(3)
+        load_w(0, 1)
+        load_x(4)
+        load_x(5)
+        load_w(0, 2)
         load_w(1, 0)
+        load_prior_half(0)
         load_w(1, 1)
-        load_prior(0, 0)
-        load_prior(0, 1)
         load_w(1, 2)
-        load_prior(1, 0)
-        load_prior(1, 1)
-        nc.sync.dma_start(
-            out=b_words[:].rearrange("p g n -> p (g n)").bitcast(I32).rearrange("p (g n) -> p g n", g=2),
-            in_=basis_words.bitcast(I32).rearrange("g p n -> p g n"),
-        )
-        b_scales_i = b_scales[:].rearrange("p g n -> p (g n)").bitcast(I32).rearrange("p (g n) -> p g n", g=2)
-        for quad in range(4):
-            nc.sync.dma_start(
-                out=b_scales_i[32 * quad:32 * quad + 4],
-                in_=basis_scales.bitcast(I32)[:, 4 * quad:4 * quad + 4, :].rearrange("g r n -> r g n"),
-            )
-        nc.sync.dma_start(out=depth_bf[:], in_=depth.rearrange("(g p t) -> p g t", p=P, t=4))
-        nc.sync.dma_start(out=pop_raw[:], in_=pop_bytes.rearrange("(p a) k -> p a k", a=4))
-        nc.sync.dma_start(out=pop_sc[:], in_=pop_scale.rearrange("o k -> (o k)").partition_broadcast(P))
+        load_prior_half(1)
+        load_basis()
+        load_prior_pair(0)
+        load_x(6)
+        load_x(7)
+        load_pop()
+        load_prior_pair(1)
 
         def words(tile_ap):
             return tile_ap.bitcast(F32)
 
-        x_banks = {}
-
-        def warm(n, rhs):
-            b = bank()
+        def warm(n):
+            b = take_bank("warm")
             for k in range(n):
-                nc.tensor.matmul(b[:], lhsT=zeros[:, 0:P], rhs=rhs, start=True, stop=True)
+                nc.tensor.matmul(b[:], lhsT=zeros[:, 0:P], rhs=zeros[:], start=True, stop=True)
+            give_bank("warm")
 
         def x_turn(i):
+            j, a = i // 2, i % 2
+            xw = words(x_raw[i][:])
             for q in range(3):
-                b = bank()
-                x_banks[i, q] = b
-            for a in range(2):
-                xw = words(x_raw[i][:, a, :])
-                for q in range(3):
-                    for u in range(2):
-                        col = (2 * a + u) * P
-                        nc.tensor.transpose(
-                            x_banks[i, q][:, col:col + P], xw[:, 256 * q + u:256 * (q + 1):2], ident[:]
-                        )
-                if i < 3:
-                    warm(1, zeros[:])
+                b = take_bank(("x", j, q)) if a == 0 else bank_of["x", j, q][0]
+                for u in range(2):
+                    col = (2 * a + u) * P
+                    nc.tensor.transpose(b[:, col:col + P], xw[:, 256 * q + u:256 * (q + 1):2], ident[:])
 
         def copy(engine, out, in_):
             if engine == "S":
@@ -158,29 +181,36 @@ def tile_hrtf_weights_synthesis_s8_kernel(
 
         def x_empty(i, q, engine):
             if i not in x_grouped:
-                xg = stage.tile([P, 3, 2, P, 4], BF16, name="xg", bufs=2, align_bytes=64)
+                xg = stage.tile([P, 3 * 1024], BF16, name="xg", bufs=2, align_bytes=64)
                 x_grouped[i] = xg
             copy(
                 engine,
-                words(x_grouped[i][:, q].rearrange("p a m t -> p (a m t)")).rearrange("p (a m u) -> p a m u", a=2, u=2),
-                x_banks[i, q][:].rearrange("p (a u m) -> p a m u", a=2, u=2),
+                words(x_grouped[i][:, 1024 * q:1024 * (q + 1)]).rearrange("p (a m u) -> p a m u", a=2, u=2),
+                give_bank(("x", i, q))[:].rearrange("p (a u m) -> p a m u", a=2, u=2),
             )
 
         def x_quant(i, q0, q1):
             nc.vector.quantize_mx(
                 out=x_c[i][:, q0:q1, :].rearrange("p q m -> p (q m)").bitcast(E4M3),
                 scales=x_s[i][:, q0:q1, :].rearrange("p q m -> p (q m)"),
-                in_=x_grouped[i][:, q0:q1].rearrange("p q a m t -> p (q a m t)"),
+                in_=x_grouped[i][:, 1024 * q0:1024 * q1],
             )
 
         w_grouped = {}
 
-        def w_group(h, q, engine):
+        def interleave(engine, out, in_):
+            copy(
+                engine,
+                out.rearrange("p (c i) t -> p c t i", i=4),
+                in_.rearrange("p t (c i) -> p c t i", i=4),
+            )
+
+        def w_group(h, q, engine, split):
             if (h, q) not in w_grouped:
                 wg = stage.tile([P, HALF, 4], BF16, name="wg", bufs=3, align_bytes=64)
                 w_grouped[h, q] = wg
-            cols = slice(0, V_COLS[h]) if engine == "V" else slice(V_COLS[h], HALF)
-            copy(engine, w_grouped[h, q][:, cols, :], w_raw[h][q][:, :, cols].rearrange("p j c -> p c j"))
+            cols = slice(0, split) if engine == "V" else slice(split, HALF)
+            interleave(engine, w_grouped[h, q][:, cols, :], w_raw[h][q][:, :, cols])
 
         def w_quant(h, q):
             nc.vector.quantize_mx(
@@ -189,15 +219,11 @@ def tile_hrtf_weights_synthesis_s8_kernel(
                 in_=w_grouped[h, q][:].rearrange("p c j -> p (c j)"),
             )
 
-        h_banks = {}
-
         def h_pass(i, h, q):
-            if q == 0:
-                b = bank()
-                h_banks[i, h] = b
+            b = take_bank(("h", i, h)) if q == 0 else bank_of["h", i, h][0]
             cols = slice((i % 2) * P, (i % 2 + 1) * P)
             nc.tensor.matmul_mx(
-                out=h_banks[i, h][:],
+                out=b[:],
                 lhsT=x_c[i // 2][:, q, cols].bitcast(E4M3),
                 lhsT_scale=x_s[i // 2][:, q, cols],
                 rhs=w_c[h][q][:].bitcast(E4M3),
@@ -209,21 +235,20 @@ def tile_hrtf_weights_synthesis_s8_kernel(
         def h_add(i, h):
             g, t = i // 4, i % 4
             nc.vector.tensor_tensor(
-                out=hb[g][:, t, h * HALF:(h + 1) * HALF].rearrange("q (u p e) -> q u p e", u=2, e=2),
-                in0=h_banks[i, h][:].rearrange("q (p u e) -> q u p e", u=2, e=2),
-                in1=pr[g][t // 2][:, t % 2, h * HALF:(h + 1) * HALF].rearrange("q (p u e) -> q u p e", u=2, e=2),
+                out=hb[g][h][:, t * HALF:(t + 1) * HALF].rearrange("q (u p e) -> q u p e", u=2, e=2),
+                in0=give_bank(("h", i, h))[:].rearrange("q (p u e) -> q u p e", u=2, e=2),
+                in1=prior_of(i, h).rearrange("q (p u e) -> q u p e", u=2, e=2),
                 op=ADD,
             )
 
-        ht_banks = {}
-
         def ht_turn(i):
             g, t = i // 4, i % 4
-            b = bank()
-            ht_banks[i] = b
-            hw = words(hb[g][:, t, :])
-            for v in range(4):
-                nc.tensor.transpose(b[:, v * P:(v + 1) * P], hw[:, v * P:(v + 1) * P], ident[:])
+            b = take_bank(("ht", i))
+            for h in range(2):
+                hw = words(hb[g][h][:, t * HALF:(t + 1) * HALF])
+                for u in range(2):
+                    col = (2 * h + u) * P
+                    nc.tensor.transpose(b[:, col:col + P], hw[:, u * P:(u + 1) * P], ident[:])
 
         ht_grouped = {}
 
@@ -233,7 +258,7 @@ def tile_hrtf_weights_synthesis_s8_kernel(
             copy(
                 engine,
                 words(hg[:].rearrange("p a m t -> p (a m t)")).rearrange("p (a m u) -> p a m u", a=2, u=2),
-                ht_banks[i][:].rearrange("p (a u m) -> p a m u", a=2, u=2),
+                give_bank(("ht", i))[:].rearrange("p (a u m) -> p a m u", a=2, u=2),
             )
 
         def ht_quant(i):
@@ -244,11 +269,9 @@ def tile_hrtf_weights_synthesis_s8_kernel(
             )
 
         mag_rows = mag.rearrange("(g p t) f -> g t p f", p=P, t=4)
-        mag_banks = {}
 
         def mag_mm(i, f):
-            b = bank()
-            mag_banks[i, f] = b
+            b = take_bank(("mag", i, f))
             for a in range(2):
                 nc.tensor.matmul_mx(
                     out=b[:],
@@ -263,24 +286,29 @@ def tile_hrtf_weights_synthesis_s8_kernel(
         mag_tiles = {}
 
         def mag_exp(i, f):
-            if f == 0:
-                mo = outs.tile([P, F], F32, name="mo", tag="big", bufs=4, align_bytes=64)
-                mag_tiles[i] = mo
+            if f % 2 == 0:
+                mo = outs.tile([P, F // 2], F32, name="mo", tag="big", bufs=8, align_bytes=64)
+                mag_tiles[i, f // 2] = mo
             nc.scalar.activation(
-                out=mag_tiles[i][:, 512 * f:512 * (f + 1)], in_=mag_banks[i, f][:], func=EXP, scale=depth_f[:, i:i + 1]
+                out=mag_tiles[i, f // 2][:, 512 * (f % 2):512 * (f % 2 + 1)],
+                in_=give_bank(("mag", i, f))[:],
+                func=EXP,
+                scale=depth_f[:, i:i + 1],
             )
 
-        def mag_store(i, c0, c1):
-            cols = slice(c0, c1)
-            nc.sync.dma_start(out=mag_rows[i // 4, i % 4, :, cols], in_=mag_tiles[i][:, cols])
+        def mag_store(i, f0, f1):
+            z = f0 // 2
+            nc.sync.dma_start(
+                out=mag_rows[i // 4, i % 4, :, 512 * f0:512 * f1],
+                in_=mag_tiles[i, z][:, 512 * f0 - 1024 * z:512 * f1 - 1024 * z],
+            )
 
         h_grouped = {}
 
         def h_group(g, h, engine):
             group = stage.tile([P, HALF, 4], BF16, name="group", bufs=3, align_bytes=64)
             h_grouped[g, h] = group
-            cols = slice(HALF * h, HALF * (h + 1))
-            copy(engine, group[:], hb[g][:, :, cols].rearrange("p t c -> p c t"))
+            interleave(engine, group[:], hb[g][h][:].rearrange("p (t c) -> p t c", t=4))
 
         def h_quant(g, h):
             cols = slice(HALF * h, HALF * (h + 1))
@@ -290,45 +318,47 @@ def tile_hrtf_weights_synthesis_s8_kernel(
                 in_=h_grouped[g, h][:].rearrange("p c t -> p (c t)"),
             )
 
-        pop_banks = {}
-
-        def pop_product(a):
-            nc.vector.tensor_tensor(out=pop_bf[:, a, :], in0=pop_raw[:, a, :].bitcast(FP8), in1=pop_sc[:], op=MULT)
+        def pop_widen(a):
+            nc.vector.tensor_scalar(
+                out=pop_bf[a][:].rearrange("r (u p e) -> r p u e", u=2, e=2),
+                in0=pop_raw[:, a, :].bitcast(FP8).rearrange("r (p u e) -> r p u e", u=2, e=2),
+                scalar1=one[:],
+                scalar2=None,
+                op0=MULT,
+            )
 
         def pop_turn(g, z):
-            b = bank()
-            pop_banks[g, z] = b
+            b = take_bank(("pop", g, z))
             for a in range(2):
-                pw = words(pop_bf[:, 2 * z + a, :])
+                pw = words(pop_bf[2 * z + a][:])
                 for u in range(2):
-                    col = (2 * a + u) * P
-                    nc.tensor.transpose(b[:, col:col + P], pw[:, 256 * g + u:256 * (g + 1):2], ident[:])
+                    col = (2 * u + a) * P
+                    nc.tensor.transpose(b[:, col:col + P], pw[:, 256 * u + P * g:256 * u + P * (g + 1)], ident[:])
 
         pop_grouped = {}
 
-        def pop_empty(g, z, engine):
+        def pop_empty(g, z):
             if g not in pop_grouped:
-                group = stage.tile([P, 2, 2, P, 4], BF16, name="group", bufs=3, align_bytes=64)
+                group = stage.tile([P, 2048], BF16, name="group", bufs=3, align_bytes=64)
                 pop_grouped[g] = group
-            copy(
-                engine,
-                words(pop_grouped[g][:, z].rearrange("p a r t -> p (a r t)")).rearrange("p (a r u) -> p a r u", a=2, u=2),
-                pop_banks[g, z][:].rearrange("p (a u r) -> p a r u", a=2, u=2),
+            nc.vector.tensor_tensor(
+                out=pop_grouped[g][:, 1024 * z:1024 * (z + 1)].rearrange("p (r u e) -> p r u e", u=2, e=2),
+                in0=give_bank(("pop", g, z))[:].bitcast(BF16).rearrange("p (u r e) -> p r u e", u=2, e=2),
+                in1=pop_sc[:, g, :].rearrange("p (u e) -> p u e", u=2).unsqueeze(1).to_broadcast([P, 256, 2, 2]),
+                op=MULT,
             )
 
         def pop_quant(g):
             nc.vector.quantize_mx(
                 out=p_c[g][:].bitcast(E4M3),
                 scales=p_s[g][:],
-                in_=pop_grouped[g][:].rearrange("p z a r t -> p (z a r t)"),
+                in_=pop_grouped[g][:],
             )
 
         load_rows = load.rearrange("(p a) c -> a p c", a=4)
-        load_banks = {}
 
         def load_mm(a, h):
-            b = bank()
-            load_banks[a, h] = b
+            b = take_bank(("load", a, h))
             for g in range(2):
                 nc.tensor.matmul_mx(
                     out=b[:],
@@ -349,154 +379,145 @@ def tile_hrtf_weights_synthesis_s8_kernel(
             copy(
                 engine,
                 load_tiles[a][:, 512 * h:512 * (h + 1)].rearrange("q (p u e) -> q p u e", u=2, e=2),
-                load_banks[a, h][:].rearrange("q (u p e) -> q p u e", u=2, e=2),
+                give_bank(("load", a, h))[:].rearrange("q (u p e) -> q p u e", u=2, e=2),
             )
 
-        def load_store(a, halves):
-            for h in range(halves):
-                cols = slice(C // halves * h, C // halves * (h + 1))
-                nc.sync.dma_start(out=load_rows[a, :, cols], in_=load_tiles[a][:, cols])
+        def load_store(a, h0, h1):
+            cols = slice(512 * h0, 512 * h1)
+            nc.sync.dma_start(out=load_rows[a, :, cols], in_=load_tiles[a][:, cols])
 
-
-        def x_step(i, vector_banks):
-            for q in range(3):
-                x_empty(i, q, "V" if q in vector_banks else "S")
-
-        def x_quants(i):
-            x_quant(i, 0, 2)
-            x_quant(i, 2, 3)
-
-        def w_step(h, q):
-            w_group(h, q, "V")
-            w_group(h, q, "S")
 
         def h_passes(tiles, h, passes):
             for q in passes:
                 for i in tiles:
                     h_pass(i, h, q)
 
-        def h_all(i, h):
-            h_passes((i,), h, range(3))
-
-        def mag_step(i, run=2):
-            for f in range(4):
+        def mag_step(i, banks=range(4), run=2):
+            for f in banks:
                 mag_mm(i, f)
                 mag_exp(i, f)
                 if (f + 1) % run == 0:
-                    mag_store(i, 512 * (f + 1 - run), 512 * (f + 1))
+                    mag_store(i, f + 1 - run, f + 1)
 
-        def load_step(a, engines):
-            for h in range(2):
-                load_mm(a, h)
-                load_empty(a, h, engines[h])
-            load_store(a, 1)
+        def w_share(h, q, split):
+            w_group(h, q, "V", split)
+            w_group(h, q, "S", split)
 
-        warm(8, zeros[:])
+        def x_empties(j, engines):
+            for q in range(3):
+                x_empty(j, q, engines[q])
+
+        def h_adds(tiles, h):
+            for i in tiles:
+                h_add(i, h)
+
+        warm(6)
         x_turn(0)
-        w_step(0, 0)
-        w_step(0, 1)
-        x_step(0, (1,))
-        w_quant(0, 0)
-        x_quants(0)
-        w_quant(0, 1)
-        warm(2, w_raw[0][0][:, 0, :])
-        warm(2, w_raw[0][1][:, 0, :])
         x_turn(1)
-        x_step(1, (0,))
+        x_empties(0, "VSS")
+        w_share(0, 0, 384)
+        x_quant(0, 0, 2)
+        w_quant(0, 0)
+        x_quant(0, 2, 3)
+        warm(3)
         x_turn(2)
-        x_quant(1, 0, 2)
-        w_group(0, 2, "V")
-        x_step(2, (2,))
-        w_group(0, 2, "S")
-        x_quants(2)
-        x_quant(1, 2, 3)
-        w_quant(0, 2)
-        h_passes(range(4), 0, (0,))
         x_turn(3)
-        x_step(3, ())
-        h_passes(range(4), 0, (1, 2))
-        w_step(1, 0)
-        x_quant(3, 0, 2)
-        w_step(1, 1)
-        x_quant(3, 2, 3)
-        h_all(4, 0)
-        h_all(5, 0)
-        h_add(0, 0)
+        h_passes((0, 1), 0, (0,))
+        x_empties(1, "VSS")
+        w_share(0, 1, 320)
+        x_quant(1, 0, 2)
+        w_quant(0, 1)
+        x_quant(1, 2, 3)
+        x_turn(4)
+        x_turn(5)
+        h_passes((2, 3), 0, (0,))
+        h_passes(range(4), 0, (1,))
+        x_empties(2, "SSS")
+        w_group(0, 2, "V", 512)
+        x_quant(2, 0, 2)
+        w_quant(0, 2)
+        w_share(1, 0, 128)
+        x_quant(2, 2, 3)
+        h_passes((4, 5), 0, (0, 1))
+        h_passes(range(6), 0, (2,))
         w_quant(1, 0)
+        h_add(0, 0)
+        w_share(1, 1, 128)
         h_add(1, 0)
-        w_quant(1, 1)
         h_add(2, 0)
-        w_step(1, 2)
+        w_quant(1, 1)
+        w_share(1, 2, 192)
+        h_passes(range(5), 1, (0, 1))
         h_add(3, 0)
         w_quant(1, 2)
-        h_all(6, 0)
-        h_add(4, 0)
-        h_add(5, 0)
-        h_passes((0, 1), 1, (0, 1))
-        h_all(7, 0)
-        h_passes((2,), 1, (0, 1))
-        h_passes((0, 1, 2), 1, (2,))
-        h_all(3, 1)
-        for i in range(4):
-            h_add(i, 1)
-        h_all(4, 1)
-        h_all(5, 1)
-        h_add(4, 1)
-        h_add(5, 1)
-        for i in range(4):
-            ht_turn(i)
-        for i in range(4):
-            ht_empty(i, "SSVS"[i])
-        h_add(6, 0)
-        ht_quant(0)
-        ht_quant(1)
-        h_add(7, 0)
-        ht_quant(2)
-        ht_quant(3)
-        nc.vector.tensor_copy(out=depth_f[:], in_=depth_bf[:].rearrange("p g t -> p (g t)"))
-        h_all(6, 1)
-        h_all(7, 1)
-        pop_product(0)
+        h_passes((5,), 1, (0, 1))
+        h_passes(range(6), 1, (2,))
         h_group(0, 0, "S")
-        mag_step(0)
-        h_add(6, 1)
-        h_add(7, 1)
-        mag_step(1)
-        h_group(0, 1, "V")
-        h_quant(0, 0)
-        pop_product(1)
-        h_quant(0, 1)
-        for i in range(4, 8):
+        nc.vector.tensor_copy(out=depth_f[:], in_=depth_bf[:].rearrange("p g t -> p (g t)"))
+        h_adds(range(4), 1)
+        for i in range(4):
             ht_turn(i)
-        ht_empty(4, "S")
-        ht_empty(5, "V")
-        pop_product(2)
-        ht_empty(6, "S")
-        ht_empty(7, "V")
+        for i in range(4):
+            ht_empty(i, "S")
+        ht_quant(0)
+        h_add(4, 0)
+        ht_quant(1)
+        h_add(4, 1)
+        ht_quant(2)
+        h_add(5, 0)
+        ht_quant(3)
+        h_add(5, 1)
+        h_quant(0, 0)
+        mag_step(0)
+        mag_step(1)
+        x_turn(6)
+        x_turn(7)
+        for a in range(4):
+            pop_widen(a)
+        x_empties(3, "VSV")
+        x_quant(3, 0, 2)
+        x_quant(3, 2, 3)
+        mag_step(2)
+        ht_turn(4)
+        ht_turn(5)
+        pop_turn(0, 0)
+        pop_turn(0, 1)
+        ht_empty(4, "V")
+        ht_empty(5, "S")
+        pop_empty(0, 0)
+        pop_empty(0, 1)
         ht_quant(4)
         ht_quant(5)
-        mag_step(2)
-        pop_product(3)
-        ht_quant(6)
-        ht_quant(7)
-        h_group(1, 0, "V")
-        mag_step(3)
-        for z in range(2):
-            for g in range(2):
-                pop_turn(g, z)
-        for z in range(2):
-            for g in range(2):
-                pop_empty(g, z, "VS"[g])
-        mag_step(4)
-        h_quant(1, 0)
         pop_quant(0)
+        mag_step(3)
+        h_group(0, 1, "S")
+        for i in (6, 7):
+            for h in range(2):
+                h_passes((i,), h, range(3))
+                h_add(i, h)
+        mag_step(4, banks=(0, 1))
+        ht_turn(6)
+        ht_turn(7)
+        pop_turn(1, 0)
+        pop_turn(1, 1)
+        h_group(1, 0, "V")
+        ht_empty(6, "S")
+        ht_empty(7, "S")
+        h_quant(0, 1)
+        pop_empty(1, 0)
+        h_quant(1, 0)
+        pop_empty(1, 1)
+        mag_step(4, banks=(2, 3))
+        ht_quant(6)
         h_group(1, 1, "V")
         pop_quant(1)
-        h_quant(1, 1)
+        ht_quant(7)
         mag_step(5)
+        h_quant(1, 1)
         mag_step(6)
-        load_step(0, "VV")
-        load_step(1, "VV")
-        load_step(2, "VS")
-        load_step(3, "VS")
-        mag_step(7, run=1)
+        for a in range(4):
+            for h in range(2):
+                load_mm(a, h)
+                load_empty(a, h, "V")
+            load_store(a, 0, 2)
+            mag_step(7, banks=(a,), run=2 if a < 2 else 1)

@@ -55,17 +55,12 @@ def tile_hrtf_weights_synthesis_s8_kernel(
         dummy = kept("dummy", [P, 1], F32)
         zeros = kept("zeros", [P, 512], BF16)
         x_raw = [
-            outs.tile([P, K], BF16, name="x_raw%d" % i, tag="big", bufs=8, align_bytes=64) for i in range(8)
+            outs.tile([P, 2 * K], BF16, name="x_raw%d" % j, tag="big", bufs=4, align_bytes=64) for j in range(4)
         ]
         w_raw = [
-            [
-                outs.tile([P, 4, HALF], BF16, name="w_raw%d%d" % (h, q), tag="small", bufs=6, align_bytes=64)
-                for q in range(3)
-            ]
-            for h in range(2)
+            outs.tile([P, 4, C], BF16, name="w_raw%d" % q, tag="small", bufs=3, align_bytes=64) for q in range(3)
         ]
-        pr_half = [kept("pr_half%d" % h, [P, 4, HALF], BF16) for h in range(2)]
-        pr_pair = [kept("pr_pair%d" % z, [P, 2, C], BF16) for z in range(2)]
+        pr = [kept("pr%d" % j, [P, 2, C], BF16) for j in range(4)]
         b_words = kept("b_words", [P, 2, 2 * F], U8)
         b_scales = kept("b_scales", [P, 2, F], U8)
         depth_bf = kept("depth_bf", [P, 2, 4], BF16)
@@ -79,8 +74,8 @@ def tile_hrtf_weights_synthesis_s8_kernel(
         w_c = [[kept("w_c%d%d" % (h, q), [P, HALF], U32) for q in range(3)] for h in range(2)]
         w_s = [[kept("w_s%d%d" % (h, q), [P, HALF], U8) for q in range(3)] for h in range(2)]
         hb = [[kept("hb%d%d" % (g, h), [P, 4 * HALF], BF16) for h in range(2)] for g in range(2)]
-        ht_c = [kept("ht_c%d" % i, [P, 2, P], U32) for i in range(8)]
-        ht_s = [kept("ht_s%d" % i, [P, 2, P], U8) for i in range(8)]
+        ht_c = [kept("ht_c%d" % j, [P, 4 * P], U32) for j in range(4)]
+        ht_s = [kept("ht_s%d" % j, [P, 4 * P], U8) for j in range(4)]
         h_c = [kept("h_c%d" % g, [P, C], U32) for g in range(2)]
         h_s = [kept("h_s%d" % g, [P, C], U8) for g in range(2)]
         p_c = [kept("p_c%d" % g, [P, R], U32) for g in range(2)]
@@ -93,34 +88,31 @@ def tile_hrtf_weights_synthesis_s8_kernel(
         make_identity(nc, ident[:])
         nc.gpsimd.memset(b_scales[:].rearrange("p g n -> p (g n)").bitcast(I32), 0)
 
-        def load_x(i):
+        def load_x(i, tiles):
             g, t = i // 4, i % 4
-            src = x[g * 512:(g + 1) * 512, :].rearrange("(p t) k -> p t k", t=4)
-            nc.sync.dma_start(out=x_raw[i][:], in_=src[:, t, :])
+            src = x[g * 512:(g + 1) * 512, :].rearrange("(p t) k -> p (t k)", t=4)
+            nc.sync.dma_start(
+                out=x_raw[i // 2][:, K * (i % 2):K * (i % 2 + tiles)], in_=src[:, K * t:K * (t + tiles)]
+            )
 
-        def load_w(h, q):
-            src = w[q * 512:(q + 1) * 512, h * HALF:(h + 1) * HALF]
-            nc.sync.dma_start(out=w_raw[h][q][:], in_=src.rearrange("(p j) c -> p j c", j=4))
+        def load_w(q):
+            src = w[q * 512:(q + 1) * 512, :]
+            nc.sync.dma_start(out=w_raw[q][:], in_=src.rearrange("(p j) c -> p j c", j=4))
 
-        def load_prior_half(h):
-            src = prior[0:512, h * HALF:(h + 1) * HALF]
-            nc.sync.dma_start(out=pr_half[h][:], in_=src.rearrange("(p t) c -> p t c", t=4))
-
-        def load_prior_pair(z):
-            src = prior[512:1024, :].rearrange("(p t) c -> p t c", t=4)
-            nc.sync.dma_start(out=pr_pair[z][:], in_=src[:, 2 * z:2 * z + 2, :])
+        def load_prior(j):
+            g, z = j // 2, j % 2
+            src = prior[g * 512:(g + 1) * 512, :].rearrange("(p t) c -> p t c", t=4)
+            nc.sync.dma_start(out=pr[j][:], in_=src[:, 2 * z:2 * z + 2, :])
 
         def prior_of(i, h):
-            if i < 4:
-                return pr_half[h][:, i, :]
-            return pr_pair[(i - 4) // 2][:, i % 2, h * HALF:(h + 1) * HALF]
+            return pr[i // 2][:, i % 2, h * HALF:(h + 1) * HALF]
 
         def load_basis():
             b_scales_i = b_scales[:].rearrange("p g n -> p (g n)").bitcast(I32).rearrange("p (g n) -> p g n", g=2)
-            for quad in range(4):
+            for r in range(4):
                 nc.sync.dma_start(
-                    out=b_scales_i[32 * quad:32 * quad + 4],
-                    in_=basis_scales.bitcast(I32)[:, 4 * quad:4 * quad + 4, :].rearrange("g r n -> r g n"),
+                    out=b_scales_i[r:P:32],
+                    in_=basis_scales.bitcast(I32)[:, r:16:4, :].rearrange("g quad n -> quad g n"),
                 )
             nc.sync.dma_start(out=depth_bf[:], in_=depth.rearrange("(g p t) -> p g t", p=P, t=4))
             nc.sync.dma_start(
@@ -132,26 +124,20 @@ def tile_hrtf_weights_synthesis_s8_kernel(
             nc.sync.dma_start(out=pop_raw[:], in_=pop_bytes.rearrange("(p a) k -> p a k", a=4))
             nc.sync.dma_start(out=pop_sc[:], in_=pop_scale.rearrange("o (g p t) -> p (o g) t", p=P, t=4))
 
-        load_x(0)
-        load_x(1)
-        load_w(0, 0)
-        load_x(2)
-        load_x(3)
-        load_w(0, 1)
-        load_x(4)
-        load_x(5)
-        load_w(0, 2)
-        load_w(1, 0)
-        load_prior_half(0)
-        load_w(1, 1)
-        load_w(1, 2)
-        load_prior_half(1)
+        load_x(0, 1)
+        load_x(1, 1)
+        load_x(2, 2)
+        load_w(0)
+        load_x(4, 2)
+        load_w(1)
+        load_w(2)
+        load_prior(0)
+        load_prior(1)
         load_basis()
-        load_prior_pair(0)
-        load_x(6)
-        load_x(7)
+        load_prior(2)
         load_pop()
-        load_prior_pair(1)
+        load_x(6, 2)
+        load_prior(3)
 
         def words(tile_ap):
             return tile_ap.bitcast(F32)
@@ -164,7 +150,7 @@ def tile_hrtf_weights_synthesis_s8_kernel(
 
         def x_turn(i):
             j, a = i // 2, i % 2
-            xw = words(x_raw[i][:])
+            xw = words(x_raw[j][:, K * a:K * (a + 1)])
             for q in range(3):
                 b = take_bank(("x", j, q)) if a == 0 else bank_of["x", j, q][0]
                 for u in range(2):
@@ -205,12 +191,15 @@ def tile_hrtf_weights_synthesis_s8_kernel(
                 in_.rearrange("p t (c i) -> p c t i", i=4),
             )
 
+        def depth_widen():
+            nc.scalar.copy(out=depth_f[:], in_=depth_bf[:].rearrange("p g t -> p (g t)"))
+
         def w_group(h, q, engine, split):
             if (h, q) not in w_grouped:
                 wg = stage.tile([P, HALF, 4], BF16, name="wg", bufs=3, align_bytes=64)
                 w_grouped[h, q] = wg
             cols = slice(0, split) if engine == "V" else slice(split, HALF)
-            interleave(engine, w_grouped[h, q][:, cols, :], w_raw[h][q][:, :, cols])
+            interleave(engine, w_grouped[h, q][:, cols, :], w_raw[q][:, :, h * HALF:(h + 1) * HALF][:, :, cols])
 
         def w_quant(h, q):
             nc.vector.quantize_mx(
@@ -253,19 +242,21 @@ def tile_hrtf_weights_synthesis_s8_kernel(
         ht_grouped = {}
 
         def ht_empty(i, engine):
-            hg = stage.tile([P, 2, P, 4], BF16, name="hg", align_bytes=64)
-            ht_grouped[i] = hg
+            if i % 2 == 0:
+                hg = stage.tile([P, 2048], BF16, name="hg", bufs=2, align_bytes=64)
+                ht_grouped[i // 2] = hg
             copy(
                 engine,
-                words(hg[:].rearrange("p a m t -> p (a m t)")).rearrange("p (a m u) -> p a m u", a=2, u=2),
+                words(ht_grouped[i // 2][:, 1024 * (i % 2):1024 * (i % 2 + 1)]).rearrange("p (a m u) -> p a m u", a=2, u=2),
                 give_bank(("ht", i))[:].rearrange("p (a u m) -> p a m u", a=2, u=2),
             )
 
-        def ht_quant(i):
+        def ht_quant(i, tiles=1):
+            j, a = i // 2, i % 2
             nc.vector.quantize_mx(
-                out=ht_c[i][:].rearrange("p a m -> p (a m)").bitcast(E4M3),
-                scales=ht_s[i][:].rearrange("p a m -> p (a m)"),
-                in_=ht_grouped[i][:].rearrange("p a m t -> p (a m t)"),
+                out=ht_c[j][:, 256 * a:256 * (a + tiles)].bitcast(E4M3),
+                scales=ht_s[j][:, 256 * a:256 * (a + tiles)],
+                in_=ht_grouped[j][:, 1024 * a:1024 * (a + tiles)],
             )
 
         mag_rows = mag.rearrange("(g p t) f -> g t p f", p=P, t=4)
@@ -273,10 +264,11 @@ def tile_hrtf_weights_synthesis_s8_kernel(
         def mag_mm(i, f):
             b = take_bank(("mag", i, f))
             for a in range(2):
+                cols = slice(P * (2 * (i % 2) + a), P * (2 * (i % 2) + a + 1))
                 nc.tensor.matmul_mx(
                     out=b[:],
-                    lhsT=ht_c[i][:, a, :].bitcast(E4M3),
-                    lhsT_scale=ht_s[i][:, a, :],
+                    lhsT=ht_c[i // 2][:, cols].bitcast(E4M3),
+                    lhsT_scale=ht_s[i // 2][:, cols],
                     rhs=b_words[:, a, 1024 * f:1024 * (f + 1)].bitcast(E2M1),
                     rhs_scale=b_scales[:, a, 512 * f:512 * (f + 1)],
                     start=(a == 0),
@@ -286,22 +278,19 @@ def tile_hrtf_weights_synthesis_s8_kernel(
         mag_tiles = {}
 
         def mag_exp(i, f):
-            if f % 2 == 0:
-                mo = outs.tile([P, F // 2], F32, name="mo", tag="big", bufs=8, align_bytes=64)
-                mag_tiles[i, f // 2] = mo
+            if f == 0:
+                mo = outs.tile([P, F], F32, name="mo", tag="big", bufs=4, align_bytes=64)
+                mag_tiles[i] = mo
             nc.scalar.activation(
-                out=mag_tiles[i, f // 2][:, 512 * (f % 2):512 * (f % 2 + 1)],
+                out=mag_tiles[i][:, 512 * f:512 * (f + 1)],
                 in_=give_bank(("mag", i, f))[:],
                 func=EXP,
                 scale=depth_f[:, i:i + 1],
             )
 
         def mag_store(i, f0, f1):
-            z = f0 // 2
-            nc.sync.dma_start(
-                out=mag_rows[i // 4, i % 4, :, 512 * f0:512 * f1],
-                in_=mag_tiles[i, z][:, 512 * f0 - 1024 * z:512 * f1 - 1024 * z],
-            )
+            cols = slice(512 * f0, 512 * f1)
+            nc.sync.dma_start(out=mag_rows[i // 4, i % 4, :, cols], in_=mag_tiles[i][:, cols])
 
         h_grouped = {}
 
@@ -373,18 +362,21 @@ def tile_hrtf_weights_synthesis_s8_kernel(
         load_tiles = {}
 
         def load_empty(a, h, engine):
-            if a not in load_tiles:
-                lo = outs.tile([P, C], F32, name="lo", tag="small", bufs=6, align_bytes=64)
-                load_tiles[a] = lo
+            if a // 2 not in load_tiles:
+                lo = outs.tile([P, 2 * C], F32, name="lo", tag="small", bufs=3, align_bytes=64)
+                load_tiles[a // 2] = lo
+            col = C * (a % 2) + 512 * h
             copy(
                 engine,
-                load_tiles[a][:, 512 * h:512 * (h + 1)].rearrange("q (p u e) -> q p u e", u=2, e=2),
+                load_tiles[a // 2][:, col:col + 512].rearrange("q (p u e) -> q p u e", u=2, e=2),
                 give_bank(("load", a, h))[:].rearrange("q (u p e) -> q p u e", u=2, e=2),
             )
 
         def load_store(a, h0, h1):
-            cols = slice(512 * h0, 512 * h1)
-            nc.sync.dma_start(out=load_rows[a, :, cols], in_=load_tiles[a][:, cols])
+            col = C * (a % 2)
+            nc.sync.dma_start(
+                out=load_rows[a, :, 512 * h0:512 * h1], in_=load_tiles[a // 2][:, col + 512 * h0:col + 512 * h1]
+            )
 
 
         def h_passes(tiles, h, passes):
@@ -411,113 +403,130 @@ def tile_hrtf_weights_synthesis_s8_kernel(
             for i in tiles:
                 h_add(i, h)
 
+        def h_both(tiles, q):
+            for i in tiles:
+                for h in range(2):
+                    h_pass(i, h, q)
+
         warm(6)
         x_turn(0)
         x_turn(1)
-        x_empties(0, "VSS")
-        w_share(0, 0, 384)
+        x_empties(0, "VSV")
         x_quant(0, 0, 2)
-        w_quant(0, 0)
         x_quant(0, 2, 3)
-        warm(3)
         x_turn(2)
         x_turn(3)
-        h_passes((0, 1), 0, (0,))
-        x_empties(1, "VSS")
-        w_share(0, 1, 320)
+        x_empties(1, "VSV")
+        w_share(0, 0, 256)
         x_quant(1, 0, 2)
-        w_quant(0, 1)
+        w_quant(0, 0)
+        w_share(1, 0, 192)
         x_quant(1, 2, 3)
+        warm(4)
         x_turn(4)
         x_turn(5)
-        h_passes((2, 3), 0, (0,))
-        h_passes(range(4), 0, (1,))
-        x_empties(2, "SSS")
-        w_group(0, 2, "V", 512)
-        x_quant(2, 0, 2)
-        w_quant(0, 2)
-        w_share(1, 0, 128)
-        x_quant(2, 2, 3)
-        h_passes((4, 5), 0, (0, 1))
-        h_passes(range(6), 0, (2,))
         w_quant(1, 0)
-        h_add(0, 0)
-        w_share(1, 1, 128)
-        h_add(1, 0)
-        h_add(2, 0)
+        h_passes(range(4), 0, (0,))
+        h_passes((0,), 1, (0,))
+        x_empties(2, "VSS")
+        w_share(0, 1, 320)
+        x_quant(2, 0, 2)
+        w_quant(0, 1)
+        h_passes((1,), 1, (0,))
+        h_passes((4, 5), 0, (0,))
+        w_share(1, 1, 192)
+        x_quant(2, 2, 3)
+        h_passes(range(6), 0, (1,))
+        w_share(0, 2, 320)
         w_quant(1, 1)
+        w_quant(0, 2)
+        h_passes((0, 1), 1, (1,))
         w_share(1, 2, 192)
-        h_passes(range(5), 1, (0, 1))
-        h_add(3, 0)
+        h_passes(range(6), 0, (2,))
+        h_add(0, 0)
         w_quant(1, 2)
-        h_passes((5,), 1, (0, 1))
-        h_passes(range(6), 1, (2,))
+        h_adds((1, 2, 3), 0)
         h_group(0, 0, "S")
-        nc.vector.tensor_copy(out=depth_f[:], in_=depth_bf[:].rearrange("p g t -> p (g t)"))
-        h_adds(range(4), 1)
-        for i in range(4):
-            ht_turn(i)
-        for i in range(4):
-            ht_empty(i, "S")
+        h_passes((0, 1), 1, (2,))
+        h_passes((2,), 1, range(3))
+        h_passes((3,), 1, range(3))
+        h_adds((0, 1), 1)
+        depth_widen()
+        ht_turn(0)
+        ht_turn(1)
+        h_add(2, 1)
+        ht_empty(0, "V")
+        ht_empty(1, "S")
+        h_passes((4,), 1, range(3))
+        h_passes((5,), 1, range(3))
+        h_add(3, 1)
         ht_quant(0)
-        h_add(4, 0)
+        pop_widen(0)
         ht_quant(1)
-        h_add(4, 1)
-        ht_quant(2)
-        h_add(5, 0)
-        ht_quant(3)
-        h_add(5, 1)
-        h_quant(0, 0)
         mag_step(0)
-        mag_step(1)
+        for a in range(1, 4):
+            pop_widen(a)
+        ht_turn(2)
+        ht_turn(3)
+        h_add(4, 0)
+        h_add(4, 1)
+        ht_empty(2, "V")
+        ht_empty(3, "S")
+        mag_step(1, banks=(0, 1))
         x_turn(6)
         x_turn(7)
-        for a in range(4):
-            pop_widen(a)
+        h_add(5, 0)
+        ht_quant(2, 2)
+        h_add(5, 1)
         x_empties(3, "VSV")
+        mag_step(1, banks=(2, 3))
+        pop_turn(0, 0)
+        pop_turn(0, 1)
         x_quant(3, 0, 2)
         x_quant(3, 2, 3)
+        pop_empty(0, 0)
+        pop_empty(0, 1)
         mag_step(2)
         ht_turn(4)
         ht_turn(5)
-        pop_turn(0, 0)
-        pop_turn(0, 1)
-        ht_empty(4, "V")
-        ht_empty(5, "S")
-        pop_empty(0, 0)
-        pop_empty(0, 1)
-        ht_quant(4)
-        ht_quant(5)
-        pop_quant(0)
-        mag_step(3)
-        h_group(0, 1, "S")
-        for i in (6, 7):
-            for h in range(2):
-                h_passes((i,), h, range(3))
-                h_add(i, h)
-        mag_step(4, banks=(0, 1))
-        ht_turn(6)
-        ht_turn(7)
         pop_turn(1, 0)
         pop_turn(1, 1)
-        h_group(1, 0, "V")
-        ht_empty(6, "S")
-        ht_empty(7, "S")
-        h_quant(0, 1)
+        h_quant(0, 0)
+        ht_empty(4, "S")
+        ht_empty(5, "S")
+        h_group(0, 1, "S")
+        pop_quant(0)
         pop_empty(1, 0)
-        h_quant(1, 0)
         pop_empty(1, 1)
-        mag_step(4, banks=(2, 3))
-        ht_quant(6)
-        h_group(1, 1, "V")
+        for i in (6, 7):
+            h_passes((i,), 0, range(3))
+            mag_step(3, banks=(2 * (i - 6), 2 * (i - 6) + 1))
+        ht_quant(4, 2)
+        h_adds((6, 7), 0)
         pop_quant(1)
-        ht_quant(7)
-        mag_step(5)
+        h_group(1, 0, "V")
+        for i in (6, 7):
+            h_passes((i,), 1, range(3))
+            h_add(i, 1)
+            mag_step(4, banks=(2 * (i - 6), 2 * (i - 6) + 1))
+        h_quant(1, 0)
+        h_group(1, 1, "V")
+        h_quant(0, 1)
         h_quant(1, 1)
-        mag_step(6)
+        mag_step(5)
+        ht_turn(6)
+        ht_turn(7)
+        ht_empty(6, "V")
+        ht_empty(7, "S")
+        ht_quant(6, 2)
         for a in range(4):
-            for h in range(2):
-                load_mm(a, h)
-                load_empty(a, h, "V")
-            load_store(a, 0, 2)
-            mag_step(7, banks=(a,), run=2 if a < 2 else 1)
+            load_mm(a, 0)
+            load_empty(a, 0, "SVSV"[a])
+            load_store(a, 0, 1)
+        for a in range(4):
+            load_mm(a, 1)
+            load_empty(a, 1, "V")
+            load_store(a, 1, 2)
+            mag_step(6, banks=(a,))
+        mag_step(7, banks=(0, 1))
+        mag_step(7, banks=(2, 3), run=1)

@@ -114,39 +114,57 @@ def tile_hrtf_weights_synthesis_s8_kernel(
                     out=b_scales_i[r:P:32],
                     in_=basis_scales.bitcast(I32)[:, r:16:4, :].rearrange("g quad n -> quad g n"),
                 )
-            nc.sync.dma_start(out=depth_bf[:], in_=depth.rearrange("(g p t) -> p g t", p=P, t=4))
             nc.sync.dma_start(
                 out=b_words[:].rearrange("p g n -> p (g n)").bitcast(I32).rearrange("p (g n) -> p g n", g=2),
                 in_=basis_words.bitcast(I32).rearrange("g p n -> p g n"),
             )
 
+        def load_depth():
+            nc.sync.dma_start(out=depth_bf[:], in_=depth.rearrange("(g p t) -> p g t", p=P, t=4))
+
         def load_pop():
             nc.sync.dma_start(out=pop_raw[:], in_=pop_bytes.rearrange("(p a) k -> p a k", a=4))
+
+        def load_pop_scale():
             nc.sync.dma_start(out=pop_sc[:], in_=pop_scale.rearrange("o (g p t) -> p (o g) t", p=P, t=4))
 
         load_x(0, 1)
         load_x(1, 1)
-        load_x(2, 2)
         load_w(0)
-        load_x(4, 2)
+        load_x(2, 1)
+        load_x(3, 1)
         load_w(1)
+        load_x(4, 1)
+        load_x(5, 1)
         load_w(2)
         load_prior(0)
+        load_pop()
         load_prior(1)
         load_basis()
-        load_prior(2)
-        load_pop()
+        load_depth()
         load_x(6, 2)
+        load_prior(2)
         load_prior(3)
+        load_pop_scale()
 
         def words(tile_ap):
             return tile_ap.bitcast(F32)
 
-        def warm(n):
+        def warm(n, rhs=None):
             b = take_bank("warm")
             for k in range(n):
-                nc.tensor.matmul(b[:], lhsT=zeros[:, 0:P], rhs=zeros[:], start=True, stop=True)
+                nc.tensor.matmul(b[:], lhsT=zeros[:, 0:P], rhs=zeros[:] if rhs is None else rhs, start=True, stop=True)
             give_bank("warm")
+
+        x_sorted = {}
+
+        def x_sort(i):
+            xs = stage.tile([P, K // 2], F32, name="xs", bufs=2, align_bytes=64)
+            x_sorted[i] = xs
+            nc.vector.tensor_copy(
+                out=xs[:].rearrange("m (u p) -> m u p", u=2),
+                in_=words(x_raw[i // 2][:, K * (i % 2):K * (i % 2 + 1)]).rearrange("m (p u) -> m u p", u=2),
+            )
 
         def x_turn(i):
             j, a = i // 2, i % 2
@@ -155,7 +173,11 @@ def tile_hrtf_weights_synthesis_s8_kernel(
                 b = take_bank(("x", j, q)) if a == 0 else bank_of["x", j, q][0]
                 for u in range(2):
                     col = (2 * a + u) * P
-                    nc.tensor.transpose(b[:, col:col + P], xw[:, 256 * q + u:256 * (q + 1):2], ident[:])
+                    if i in x_sorted:
+                        src = x_sorted[i][:, 384 * u + P * q:384 * u + P * (q + 1)]
+                    else:
+                        src = xw[:, 256 * q + u:256 * (q + 1):2]
+                    nc.tensor.transpose(b[:, col:col + P], src, ident[:])
 
         def copy(engine, out, in_):
             if engine == "S":
@@ -295,7 +317,7 @@ def tile_hrtf_weights_synthesis_s8_kernel(
         h_grouped = {}
 
         def h_group(g, h, engine):
-            group = stage.tile([P, HALF, 4], BF16, name="group", bufs=3, align_bytes=64)
+            group = stage.tile([P, HALF, 4], BF16, name="group", bufs=4, align_bytes=64)
             h_grouped[g, h] = group
             interleave(engine, group[:], hb[g][h][:].rearrange("p (t c) -> p t c", t=4))
 
@@ -316,6 +338,19 @@ def tile_hrtf_weights_synthesis_s8_kernel(
                 op0=MULT,
             )
 
+        pop_wide = {}
+
+        def pop_cast(a):
+            wide = stage.tile([P, M], BF16, name="wide", bufs=2, align_bytes=64)
+            pop_wide[a] = wide
+            nc.scalar.copy(out=wide[:], in_=pop_raw[:, a, :].bitcast(FP8))
+
+        def pop_sort(a):
+            nc.scalar.copy(
+                out=words(pop_bf[a][:]).rearrange("r (u p) -> r u p", u=2),
+                in_=words(pop_wide[a][:]).rearrange("r (p u) -> r u p", u=2),
+            )
+
         def pop_turn(g, z):
             b = take_bank(("pop", g, z))
             for a in range(2):
@@ -328,7 +363,7 @@ def tile_hrtf_weights_synthesis_s8_kernel(
 
         def pop_empty(g, z):
             if g not in pop_grouped:
-                group = stage.tile([P, 2048], BF16, name="group", bufs=3, align_bytes=64)
+                group = stage.tile([P, 2048], BF16, name="group", bufs=4, align_bytes=64)
                 pop_grouped[g] = group
             nc.vector.tensor_tensor(
                 out=pop_grouped[g][:, 1024 * z:1024 * (z + 1)].rearrange("p (r u e) -> p r u e", u=2, e=2),
@@ -408,102 +443,109 @@ def tile_hrtf_weights_synthesis_s8_kernel(
                 for h in range(2):
                     h_pass(i, h, q)
 
-        warm(6)
+        warm(4)
         x_turn(0)
         x_turn(1)
-        x_empties(0, "VSV")
+        x_empties(0, "VSS")
         x_quant(0, 0, 2)
         x_quant(0, 2, 3)
+        w_share(0, 0, 320)
+        w_share(1, 0, 224)
+        w_quant(0, 0)
+        warm(2)
+        warm(3, w_raw[0][:, 0, 0:512])
         x_turn(2)
         x_turn(3)
-        x_empties(1, "VSV")
-        w_share(0, 0, 256)
+        h_passes((0, 1), 0, (0,))
+        x_empties(1, "VSS")
+        w_quant(1, 0)
+        h_passes((0,), 1, (0,))
         x_quant(1, 0, 2)
-        w_quant(0, 0)
-        w_share(1, 0, 192)
+        w_share(0, 1, 384)
         x_quant(1, 2, 3)
-        warm(4)
+        w_quant(0, 1)
+        h_passes((2, 3), 0, (0,))
         x_turn(4)
         x_turn(5)
-        w_quant(1, 0)
-        h_passes(range(4), 0, (0,))
-        h_passes((0,), 1, (0,))
+        w_share(1, 1, 128)
         x_empties(2, "VSS")
-        w_share(0, 1, 320)
-        x_quant(2, 0, 2)
-        w_quant(0, 1)
-        h_passes((1,), 1, (0,))
-        h_passes((4, 5), 0, (0,))
-        w_share(1, 1, 192)
-        x_quant(2, 2, 3)
-        h_passes(range(6), 0, (1,))
-        w_share(0, 2, 320)
         w_quant(1, 1)
+        h_passes(range(4), 0, (1,))
+        h_passes((0,), 1, (1,))
+        x_quant(2, 0, 2)
+        w_share(0, 2, 320)
+        x_quant(2, 2, 3)
         w_quant(0, 2)
-        h_passes((0, 1), 1, (1,))
-        w_share(1, 2, 192)
+        h_passes((1,), 1, (0, 1))
+        h_passes((4, 5), 0, (0, 1))
+        w_share(1, 2, 256)
         h_passes(range(6), 0, (2,))
-        h_add(0, 0)
         w_quant(1, 2)
+        h_add(0, 0)
+        pop_cast(0)
+        pop_cast(1)
+        pop_sort(0)
+        pop_sort(1)
         h_adds((1, 2, 3), 0)
         h_group(0, 0, "S")
         h_passes((0, 1), 1, (2,))
         h_passes((2,), 1, range(3))
         h_passes((3,), 1, range(3))
         h_adds((0, 1), 1)
-        depth_widen()
         ht_turn(0)
         ht_turn(1)
         h_add(2, 1)
         ht_empty(0, "V")
         ht_empty(1, "S")
+        depth_widen()
         h_passes((4,), 1, range(3))
         h_passes((5,), 1, range(3))
         h_add(3, 1)
         ht_quant(0)
-        pop_widen(0)
+        pop_widen(2)
+        x_sort(6)
         ht_quant(1)
+        x_sort(7)
         mag_step(0)
-        for a in range(1, 4):
-            pop_widen(a)
-        ht_turn(2)
-        ht_turn(3)
         h_add(4, 0)
         h_add(4, 1)
-        ht_empty(2, "V")
-        ht_empty(3, "S")
-        mag_step(1, banks=(0, 1))
+        h_add(5, 0)
+        h_add(5, 1)
+        ht_turn(2)
+        ht_turn(3)
         x_turn(6)
         x_turn(7)
-        h_add(5, 0)
+        ht_empty(2, "S")
+        ht_empty(3, "S")
+        pop_widen(3)
         ht_quant(2, 2)
-        h_add(5, 1)
         x_empties(3, "VSV")
-        mag_step(1, banks=(2, 3))
-        pop_turn(0, 0)
-        pop_turn(0, 1)
+        mag_step(1)
         x_quant(3, 0, 2)
         x_quant(3, 2, 3)
-        pop_empty(0, 0)
-        pop_empty(0, 1)
-        mag_step(2)
         ht_turn(4)
         ht_turn(5)
-        pop_turn(1, 0)
-        pop_turn(1, 1)
-        h_quant(0, 0)
+        for z in range(2):
+            for g in range(2):
+                pop_turn(g, z)
         ht_empty(4, "S")
         ht_empty(5, "S")
-        h_group(0, 1, "S")
-        pop_quant(0)
+        pop_empty(0, 0)
         pop_empty(1, 0)
+        mag_step(2)
+        h_group(0, 1, "S")
+        pop_empty(0, 1)
+        ht_quant(4, 2)
         pop_empty(1, 1)
         for i in (6, 7):
             h_passes((i,), 0, range(3))
             mag_step(3, banks=(2 * (i - 6), 2 * (i - 6) + 1))
-        ht_quant(4, 2)
-        h_adds((6, 7), 0)
+        h_quant(0, 0)
+        pop_quant(0)
+        h_add(6, 0)
         pop_quant(1)
+        h_add(7, 0)
+        h_quant(0, 1)
         h_group(1, 0, "V")
         for i in (6, 7):
             h_passes((i,), 1, range(3))
@@ -511,11 +553,10 @@ def tile_hrtf_weights_synthesis_s8_kernel(
             mag_step(4, banks=(2 * (i - 6), 2 * (i - 6) + 1))
         h_quant(1, 0)
         h_group(1, 1, "V")
-        h_quant(0, 1)
-        h_quant(1, 1)
         mag_step(5)
         ht_turn(6)
         ht_turn(7)
+        h_quant(1, 1)
         ht_empty(6, "V")
         ht_empty(7, "S")
         ht_quant(6, 2)

@@ -19,7 +19,14 @@ MULT = mybir.AluOpType.mult
 EXP = mybir.ActivationFunctionType.Exp
 
 P = 128
-HALF = 512
+PASS = 512
+BANK = 512
+WORDS = PASS // 2
+TURNED = 2 * BANK
+K_PASSES = K // PASS
+BINS = F // BANK
+
+VECTOR_COLS = (320, 192)
 
 
 def tile_hrtf_weights_synthesis_s8_kernel(
@@ -28,8 +35,8 @@ def tile_hrtf_weights_synthesis_s8_kernel(
     nc = tc.nc
     with ExitStack() as ctx:
         keep = ctx.enter_context(tc.tile_pool(name="keep", bufs=1))
-        stage = ctx.enter_context(tc.tile_pool(name="stage", bufs=4))
-        outs = ctx.enter_context(tc.tile_pool(name="outs", bufs=3))
+        stage = ctx.enter_context(tc.tile_pool(name="stage", bufs=2))
+        shared = ctx.enter_context(tc.tile_pool(name="shared", bufs=4))
         psum = ctx.enter_context(tc.psum_pool(name="psum", bufs=1))
         ctx.enter_context(tc.manual_schedule())
 
@@ -38,29 +45,28 @@ def tile_hrtf_weights_synthesis_s8_kernel(
 
         def take_bank(key):
             number = free_banks.pop(0)
-            b = psum.tile([P, 512], F32, name="bank%d" % number)
-            bank_of[key] = (b, number)
-            return b
+            bank = psum.tile([P, BANK], F32, name="bank%d" % number)
+            bank_of[key] = (bank, number)
+            return bank
 
         def give_bank(key):
-            b, number = bank_of[key]
+            bank, number = bank_of[key]
             free_banks.append(number)
-            return b
+            return bank
 
         def kept(name, shape, dt):
-            t = keep.tile(shape, dt, name=name, align_bytes=64)
-            return t
+            tile = keep.tile(shape, dt, name=name, align_bytes=64)
+            return tile
 
         ident = kept("ident", [P, P], F32)
-        dummy = kept("dummy", [P, 1], F32)
-        zeros = kept("zeros", [P, 512], BF16)
-        x_raw = [
-            outs.tile([P, 2 * K], BF16, name="x_raw%d" % j, tag="big", bufs=4, align_bytes=64) for j in range(4)
-        ]
+        table_probe = kept("table_probe", [P, 1], F32)
+        zeros = kept("zeros", [P, BANK], BF16)
+        x_raw = [shared.tile([P, 2 * K], BF16, name="x_raw%d" % j, tag="x_mag", align_bytes=64) for j in range(4)]
         w_raw = [
-            outs.tile([P, 4, C], BF16, name="w_raw%d" % q, tag="small", bufs=3, align_bytes=64) for q in range(3)
+            shared.tile([P, 4, C], BF16, name="w_raw%d" % q, tag="w_load", bufs=K_PASSES, align_bytes=64)
+            for q in range(K_PASSES)
         ]
-        pr = [kept("pr%d" % j, [P, 2, C], BF16) for j in range(4)]
+        prior_sb = [kept("prior%d" % j, [P, 2, C], BF16) for j in range(4)]
         b_words = kept("b_words", [P, 2, 2 * F], U8)
         b_scales = kept("b_scales", [P, 2, F], U8)
         depth_bf = kept("depth_bf", [P, 2, 4], BF16)
@@ -68,116 +74,70 @@ def tile_hrtf_weights_synthesis_s8_kernel(
         pop_raw = kept("pop_raw", [P, 4, M], U8)
         pop_sc = kept("pop_sc", [P, 2, 4], F32)
         one = kept("one", [P, 1], F32)
-        pop_bf = [kept("pop_bf%d" % a, [P, M], BF16) for a in range(4)]
-        x_c = [kept("x_c%d" % i, [P, 3, 256], U32) for i in range(4)]
-        x_s = [kept("x_s%d" % i, [P, 3, 256], U8) for i in range(4)]
-        w_c = [[kept("w_c%d%d" % (h, q), [P, HALF], U32) for q in range(3)] for h in range(2)]
-        w_s = [[kept("w_s%d%d" % (h, q), [P, HALF], U8) for q in range(3)] for h in range(2)]
-        hb = [[kept("hb%d%d" % (g, h), [P, 4 * HALF], BF16) for h in range(2)] for g in range(2)]
-        ht_c = [kept("ht_c%d" % j, [P, 4 * P], U32) for j in range(4)]
-        ht_s = [kept("ht_s%d" % j, [P, 4 * P], U8) for j in range(4)]
-        h_c = [kept("h_c%d" % g, [P, C], U32) for g in range(2)]
-        h_s = [kept("h_s%d" % g, [P, C], U8) for g in range(2)]
-        p_c = [kept("p_c%d" % g, [P, R], U32) for g in range(2)]
-        p_s = [kept("p_s%d" % g, [P, R], U8) for g in range(2)]
+        pop_sorted = [kept("pop_sorted%d" % s, [P, M], BF16) for s in range(4)]
+        x_codes = [kept("x_codes%d" % j, [P, K_PASSES, 2 * P], U32) for j in range(4)]
+        x_scales = [kept("x_scales%d" % j, [P, K_PASSES, 2 * P], U8) for j in range(4)]
+        w_codes = [[kept("w_codes%d%d" % (h, q), [P, BANK], U32) for q in range(K_PASSES)] for h in range(2)]
+        w_scales = [[kept("w_scales%d%d" % (h, q), [P, BANK], U8) for q in range(K_PASSES)] for h in range(2)]
+        h_bf = [[kept("h_bf%d%d" % (g, h), [P, 4 * BANK], BF16) for h in range(2)] for g in range(2)]
+        ht_codes = [kept("ht_codes%d" % j, [P, 4 * P], U32) for j in range(4)]
+        ht_scales = [kept("ht_scales%d" % j, [P, 4 * P], U8) for j in range(4)]
+        h_codes = [kept("h_codes%d" % g, [P, C], U32) for g in range(2)]
+        h_scales = [kept("h_scales%d" % g, [P, C], U8) for g in range(2)]
+        pop_codes = [kept("pop_codes%d" % g, [P, R], U32) for g in range(2)]
+        pop_scales = [kept("pop_scales%d" % g, [P, R], U8) for g in range(2)]
 
         nc.vector.memset(zeros[:], 0.0)
-        nc.vector.memset(dummy[:], 0.0)
+        nc.vector.memset(table_probe[:], 0.0)
         nc.vector.memset(one[:], 1.0)
-        nc.scalar.activation(out=dummy[:], in_=dummy[:], func=EXP)
+        nc.scalar.activation(out=table_probe[:], in_=table_probe[:], func=EXP)
         make_identity(nc, ident[:])
-        nc.gpsimd.memset(b_scales[:].rearrange("p g n -> p (g n)").bitcast(I32), 0)
+        b_scales_i32 = b_scales[:].rearrange("p g n -> p (g n)").bitcast(I32)
+        nc.gpsimd.memset(b_scales_i32, 0)
 
-        def load_x(i, tiles):
-            g, t = i // 4, i % 4
-            src = x[g * 512:(g + 1) * 512, :].rearrange("(p t) k -> p (t k)", t=4)
+        def fetch_x(i, tiles):
+            g, t = divmod(i, 4)
+            src = x[g * PASS:(g + 1) * PASS, :].rearrange("(p t) k -> p (t k)", t=4)
             nc.sync.dma_start(
                 out=x_raw[i // 2][:, K * (i % 2):K * (i % 2 + tiles)], in_=src[:, K * t:K * (t + tiles)]
             )
 
-        def load_w(q):
-            src = w[q * 512:(q + 1) * 512, :]
-            nc.sync.dma_start(out=w_raw[q][:], in_=src.rearrange("(p j) c -> p j c", j=4))
+        def fetch_w(q):
+            src = w[q * PASS:(q + 1) * PASS, :]
+            nc.sync.dma_start(out=w_raw[q][:], in_=src.rearrange("(p t) c -> p t c", t=4))
 
-        def load_prior(j):
-            g, z = j // 2, j % 2
-            src = prior[g * 512:(g + 1) * 512, :].rearrange("(p t) c -> p t c", t=4)
-            nc.sync.dma_start(out=pr[j][:], in_=src[:, 2 * z:2 * z + 2, :])
+        def fetch_prior(j):
+            g, t = divmod(2 * j, 4)
+            src = prior[g * PASS:(g + 1) * PASS, :].rearrange("(p t) c -> p t c", t=4)
+            nc.sync.dma_start(out=prior_sb[j][:], in_=src[:, t:t + 2, :])
 
-        def prior_of(i, h):
-            return pr[i // 2][:, i % 2, h * HALF:(h + 1) * HALF]
-
-        def load_basis():
-            b_scales_i = b_scales[:].rearrange("p g n -> p (g n)").bitcast(I32).rearrange("p (g n) -> p g n", g=2)
-            for r in range(4):
+        def fetch_basis():
+            for row in range(4):
                 nc.sync.dma_start(
-                    out=b_scales_i[r:P:32],
-                    in_=basis_scales.bitcast(I32)[:, r:16:4, :].rearrange("g quad n -> quad g n"),
+                    out=b_scales_i32.rearrange("p (g n) -> p g n", g=2)[row:P:32],
+                    in_=basis_scales.bitcast(I32)[:, row:16:4, :].rearrange("g quad n -> quad g n"),
                 )
             nc.sync.dma_start(
                 out=b_words[:].rearrange("p g n -> p (g n)").bitcast(I32).rearrange("p (g n) -> p g n", g=2),
                 in_=basis_words.bitcast(I32).rearrange("g p n -> p g n"),
             )
 
-        def load_depth():
-            nc.sync.dma_start(out=depth_bf[:], in_=depth.rearrange("(g p t) -> p g t", p=P, t=4))
+        for q in range(K_PASSES):
+            fetch_x(2 * q, 1)
+            fetch_x(2 * q + 1, 1)
+            fetch_w(q)
+        fetch_prior(0)
+        nc.sync.dma_start(out=pop_raw[:], in_=pop_bytes.rearrange("(r s) k -> r s k", s=4))
+        fetch_prior(1)
+        fetch_basis()
+        nc.sync.dma_start(out=depth_bf[:], in_=depth.rearrange("(g p t) -> p g t", p=P, t=4))
+        fetch_x(6, 2)
+        fetch_prior(2)
+        fetch_prior(3)
+        nc.sync.dma_start(out=pop_sc[:], in_=pop_scale.rearrange("o (g p t) -> p (o g) t", p=P, t=4))
 
-        def load_pop():
-            nc.sync.dma_start(out=pop_raw[:], in_=pop_bytes.rearrange("(p a) k -> p a k", a=4))
-
-        def load_pop_scale():
-            nc.sync.dma_start(out=pop_sc[:], in_=pop_scale.rearrange("o (g p t) -> p (o g) t", p=P, t=4))
-
-        load_x(0, 1)
-        load_x(1, 1)
-        load_w(0)
-        load_x(2, 1)
-        load_x(3, 1)
-        load_w(1)
-        load_x(4, 1)
-        load_x(5, 1)
-        load_w(2)
-        load_prior(0)
-        load_pop()
-        load_prior(1)
-        load_basis()
-        load_depth()
-        load_x(6, 2)
-        load_prior(2)
-        load_prior(3)
-        load_pop_scale()
-
-        def words(tile_ap):
-            return tile_ap.bitcast(F32)
-
-        def warm(n, rhs=None):
-            b = take_bank("warm")
-            for k in range(n):
-                nc.tensor.matmul(b[:], lhsT=zeros[:, 0:P], rhs=zeros[:] if rhs is None else rhs, start=True, stop=True)
-            give_bank("warm")
-
-        x_sorted = {}
-
-        def x_sort(i):
-            xs = stage.tile([P, K // 2], F32, name="xs", bufs=2, align_bytes=64)
-            x_sorted[i] = xs
-            nc.vector.tensor_copy(
-                out=xs[:].rearrange("m (u p) -> m u p", u=2),
-                in_=words(x_raw[i // 2][:, K * (i % 2):K * (i % 2 + 1)]).rearrange("m (p u) -> m u p", u=2),
-            )
-
-        def x_turn(i):
-            j, a = i // 2, i % 2
-            xw = words(x_raw[j][:, K * a:K * (a + 1)])
-            for q in range(3):
-                b = take_bank(("x", j, q)) if a == 0 else bank_of["x", j, q][0]
-                for u in range(2):
-                    col = (2 * a + u) * P
-                    if i in x_sorted:
-                        src = x_sorted[i][:, 384 * u + P * q:384 * u + P * (q + 1)]
-                    else:
-                        src = xw[:, 256 * q + u:256 * (q + 1):2]
-                    nc.tensor.transpose(b[:, col:col + P], src, ident[:])
+        def words(ap):
+            return ap.bitcast(F32)
 
         def copy(engine, out, in_):
             if engine == "S":
@@ -185,342 +145,332 @@ def tile_hrtf_weights_synthesis_s8_kernel(
             else:
                 nc.vector.tensor_copy(out=out, in_=in_)
 
-        x_grouped = {}
+        def quantize(codes, scales, values):
+            nc.vector.quantize_mx(out=codes.bitcast(E4M3), scales=scales, in_=values)
 
-        def x_empty(i, q, engine):
-            if i not in x_grouped:
-                xg = stage.tile([P, 3 * 1024], BF16, name="xg", bufs=2, align_bytes=64)
-                x_grouped[i] = xg
+        def warm(count, moving):
+            bank = take_bank("warm")
+            for repeat in range(count):
+                nc.tensor.matmul(bank[:], lhsT=zeros[:, 0:P], rhs=moving, start=True, stop=True)
+            give_bank("warm")
+
+        def empty_turned(engine, out, bank):
             copy(
                 engine,
-                words(x_grouped[i][:, 1024 * q:1024 * (q + 1)]).rearrange("p (a m u) -> p a m u", a=2, u=2),
-                give_bank(("x", i, q))[:].rearrange("p (a u m) -> p a m u", a=2, u=2),
+                words(out).rearrange("p (a m u) -> p a m u", a=2, u=2),
+                bank[:].rearrange("p (a u m) -> p a m u", a=2, u=2),
             )
-
-        def x_quant(i, q0, q1):
-            nc.vector.quantize_mx(
-                out=x_c[i][:, q0:q1, :].rearrange("p q m -> p (q m)").bitcast(E4M3),
-                scales=x_s[i][:, q0:q1, :].rearrange("p q m -> p (q m)"),
-                in_=x_grouped[i][:, 1024 * q0:1024 * q1],
-            )
-
-        w_grouped = {}
 
         def interleave(engine, out, in_):
             copy(
                 engine,
-                out.rearrange("p (c i) t -> p c t i", i=4),
-                in_.rearrange("p t (c i) -> p c t i", i=4),
+                out.rearrange("p (c n) t -> p c t n", n=4),
+                in_.rearrange("p t (c n) -> p c t n", n=4),
             )
 
-        def depth_widen():
-            nc.scalar.copy(out=depth_f[:], in_=depth_bf[:].rearrange("p g t -> p (g t)"))
+        x_sorted = {}
+        x_grouped = {}
 
-        def w_group(h, q, engine, split):
-            if (h, q) not in w_grouped:
-                wg = stage.tile([P, HALF, 4], BF16, name="wg", bufs=3, align_bytes=64)
-                w_grouped[h, q] = wg
-            cols = slice(0, split) if engine == "V" else slice(split, HALF)
-            interleave(engine, w_grouped[h, q][:, cols, :], w_raw[q][:, :, h * HALF:(h + 1) * HALF][:, :, cols])
+        def x_words(i):
+            return words(x_raw[i // 2][:, K * (i % 2):K * (i % 2 + 1)])
+
+        def x_sort(i):
+            tile = stage.tile([P, K // 2], F32, name="x_sorted", align_bytes=64)
+            x_sorted[i] = tile
+            nc.vector.tensor_copy(
+                out=tile[:].rearrange("m (u n) -> m u n", u=2), in_=x_words(i).rearrange("m (n u) -> m u n", u=2)
+            )
+
+        def x_turn(i):
+            j, a = divmod(i, 2)
+            for q in range(K_PASSES):
+                bank = take_bank(("x", j, q)) if a == 0 else bank_of["x", j, q][0]
+                for u in range(2):
+                    if i in x_sorted:
+                        first = (K_PASSES * u + q) * P
+                        src = x_sorted[i][:, first:first + P]
+                    else:
+                        src = x_words(i)[:, WORDS * q + u:WORDS * (q + 1):2]
+                    col = (2 * a + u) * P
+                    nc.tensor.transpose(bank[:, col:col + P], src, ident[:])
+
+        def x_empty(j, engines):
+            tile = stage.tile([P, K_PASSES * TURNED], BF16, name="x_grouped", align_bytes=64)
+            x_grouped[j] = tile
+            for q in range(K_PASSES):
+                empty_turned(engines[q], tile[:, TURNED * q:TURNED * (q + 1)], give_bank(("x", j, q)))
+
+        def x_quant(j, q0, q1):
+            quantize(
+                x_codes[j][:, q0:q1, :].rearrange("p q m -> p (q m)"),
+                x_scales[j][:, q0:q1, :].rearrange("p q m -> p (q m)"),
+                x_grouped[j][:, TURNED * q0:TURNED * q1],
+            )
+
+        w_grouped = {}
+
+        def w_group(h, q):
+            tile = stage.tile([P, BANK, 4], BF16, name="w_grouped", bufs=3, align_bytes=64)
+            w_grouped[h, q] = tile
+            half = w_raw[q][:, :, h * BANK:(h + 1) * BANK]
+            for engine, cols in (("V", slice(0, VECTOR_COLS[h])), ("S", slice(VECTOR_COLS[h], BANK))):
+                interleave(engine, tile[:, cols, :], half[:, :, cols])
 
         def w_quant(h, q):
-            nc.vector.quantize_mx(
-                out=w_c[h][q][:].bitcast(E4M3),
-                scales=w_s[h][q][:],
-                in_=w_grouped[h, q][:].rearrange("p c j -> p (c j)"),
-            )
+            quantize(w_codes[h][q][:], w_scales[h][q][:], w_grouped[h, q][:].rearrange("p c t -> p (c t)"))
 
-        def h_pass(i, h, q):
-            b = take_bank(("h", i, h)) if q == 0 else bank_of["h", i, h][0]
-            cols = slice((i % 2) * P, (i % 2 + 1) * P)
-            nc.tensor.matmul_mx(
-                out=b[:],
-                lhsT=x_c[i // 2][:, q, cols].bitcast(E4M3),
-                lhsT_scale=x_s[i // 2][:, q, cols],
-                rhs=w_c[h][q][:].bitcast(E4M3),
-                rhs_scale=w_s[h][q][:],
-                start=(q == 0),
-                stop=(q == 2),
-            )
+        def h_passes(tiles, h, passes):
+            for q in passes:
+                for i in tiles:
+                    bank = take_bank(("h", i, h)) if q == 0 else bank_of["h", i, h][0]
+                    cols = slice((i % 2) * P, (i % 2 + 1) * P)
+                    nc.tensor.matmul_mx(
+                        out=bank[:],
+                        lhsT=x_codes[i // 2][:, q, cols].bitcast(E4M3),
+                        lhsT_scale=x_scales[i // 2][:, q, cols],
+                        rhs=w_codes[h][q][:].bitcast(E4M3),
+                        rhs_scale=w_scales[h][q][:],
+                        start=(q == 0),
+                        stop=(q == K_PASSES - 1),
+                    )
 
-        def h_add(i, h):
-            g, t = i // 4, i % 4
-            nc.vector.tensor_tensor(
-                out=hb[g][h][:, t * HALF:(t + 1) * HALF].rearrange("q (u p e) -> q u p e", u=2, e=2),
-                in0=give_bank(("h", i, h))[:].rearrange("q (p u e) -> q u p e", u=2, e=2),
-                in1=prior_of(i, h).rearrange("q (p u e) -> q u p e", u=2, e=2),
-                op=ADD,
-            )
+        def h_row(i, h):
+            return h_bf[i // 4][h][:, (i % 4) * BANK:(i % 4 + 1) * BANK]
 
-        def ht_turn(i):
-            g, t = i // 4, i % 4
-            b = take_bank(("ht", i))
-            for h in range(2):
-                hw = words(hb[g][h][:, t * HALF:(t + 1) * HALF])
-                for u in range(2):
-                    col = (2 * h + u) * P
-                    nc.tensor.transpose(b[:, col:col + P], hw[:, u * P:(u + 1) * P], ident[:])
+        def h_add(tiles, h):
+            for i in tiles:
+                nc.vector.tensor_tensor(
+                    out=h_row(i, h).rearrange("m (u p e) -> m u p e", u=2, e=2),
+                    in0=give_bank(("h", i, h))[:].rearrange("m (p u e) -> m u p e", u=2, e=2),
+                    in1=prior_sb[i // 2][:, i % 2, h * BANK:(h + 1) * BANK].rearrange(
+                        "m (p u e) -> m u p e", u=2, e=2
+                    ),
+                    op=ADD,
+                )
 
         ht_grouped = {}
 
-        def ht_empty(i, engine):
-            if i % 2 == 0:
-                hg = stage.tile([P, 2048], BF16, name="hg", bufs=2, align_bytes=64)
-                ht_grouped[i // 2] = hg
-            copy(
-                engine,
-                words(ht_grouped[i // 2][:, 1024 * (i % 2):1024 * (i % 2 + 1)]).rearrange("p (a m u) -> p a m u", a=2, u=2),
-                give_bank(("ht", i))[:].rearrange("p (a u m) -> p a m u", a=2, u=2),
-            )
+        def ht_turn(i):
+            bank = take_bank(("ht", i))
+            for h in range(2):
+                for u in range(2):
+                    col = (2 * h + u) * P
+                    nc.tensor.transpose(bank[:, col:col + P], words(h_row(i, h))[:, u * P:(u + 1) * P], ident[:])
 
-        def ht_quant(i, tiles=1):
-            j, a = i // 2, i % 2
-            nc.vector.quantize_mx(
-                out=ht_c[j][:, 256 * a:256 * (a + tiles)].bitcast(E4M3),
-                scales=ht_s[j][:, 256 * a:256 * (a + tiles)],
-                in_=ht_grouped[j][:, 1024 * a:1024 * (a + tiles)],
-            )
+        def ht_empty(i, engine):
+            j, a = divmod(i, 2)
+            if a == 0:
+                tile = stage.tile([P, 2 * TURNED], BF16, name="ht_grouped", align_bytes=64)
+                ht_grouped[j] = tile
+            empty_turned(engine, ht_grouped[j][:, TURNED * a:TURNED * (a + 1)], give_bank(("ht", i)))
+
+        def ht_quant(i, tiles):
+            j, a = divmod(i, 2)
+            cols = slice(2 * P * a, 2 * P * (a + tiles))
+            quantize(ht_codes[j][:, cols], ht_scales[j][:, cols], ht_grouped[j][:, TURNED * a:TURNED * (a + tiles)])
 
         mag_rows = mag.rearrange("(g p t) f -> g t p f", p=P, t=4)
-
-        def mag_mm(i, f):
-            b = take_bank(("mag", i, f))
-            for a in range(2):
-                cols = slice(P * (2 * (i % 2) + a), P * (2 * (i % 2) + a + 1))
-                nc.tensor.matmul_mx(
-                    out=b[:],
-                    lhsT=ht_c[i // 2][:, cols].bitcast(E4M3),
-                    lhsT_scale=ht_s[i // 2][:, cols],
-                    rhs=b_words[:, a, 1024 * f:1024 * (f + 1)].bitcast(E2M1),
-                    rhs_scale=b_scales[:, a, 512 * f:512 * (f + 1)],
-                    start=(a == 0),
-                    stop=(a == 1),
-                )
-
         mag_tiles = {}
 
-        def mag_exp(i, f):
-            if f == 0:
-                mo = outs.tile([P, F], F32, name="mo", tag="big", bufs=4, align_bytes=64)
-                mag_tiles[i] = mo
-            nc.scalar.activation(
-                out=mag_tiles[i][:, 512 * f:512 * (f + 1)],
-                in_=give_bank(("mag", i, f))[:],
-                func=EXP,
-                scale=depth_f[:, i:i + 1],
-            )
-
-        def mag_store(i, f0, f1):
-            cols = slice(512 * f0, 512 * f1)
-            nc.sync.dma_start(out=mag_rows[i // 4, i % 4, :, cols], in_=mag_tiles[i][:, cols])
+        def spectrum(i, banks=range(BINS), store_every=2):
+            for f in banks:
+                bank = take_bank(("mag", i, f))
+                for h in range(2):
+                    first = P * (2 * (i % 2) + h)
+                    nc.tensor.matmul_mx(
+                        out=bank[:],
+                        lhsT=ht_codes[i // 2][:, first:first + P].bitcast(E4M3),
+                        lhsT_scale=ht_scales[i // 2][:, first:first + P],
+                        rhs=b_words[:, h, 2 * BANK * f:2 * BANK * (f + 1)].bitcast(E2M1),
+                        rhs_scale=b_scales[:, h, BANK * f:BANK * (f + 1)],
+                        start=(h == 0),
+                        stop=(h == 1),
+                    )
+                if f == 0:
+                    tile = shared.tile([P, F], F32, name="mag_out", tag="x_mag", align_bytes=64)
+                    mag_tiles[i] = tile
+                nc.scalar.activation(
+                    out=mag_tiles[i][:, BANK * f:BANK * (f + 1)],
+                    in_=give_bank(("mag", i, f))[:],
+                    func=EXP,
+                    scale=depth_f[:, i:i + 1],
+                )
+                if (f + 1) % store_every == 0:
+                    cols = slice(BANK * (f + 1 - store_every), BANK * (f + 1))
+                    nc.sync.dma_start(out=mag_rows[i // 4, i % 4, :, cols], in_=mag_tiles[i][:, cols])
 
         h_grouped = {}
 
         def h_group(g, h, engine):
-            group = stage.tile([P, HALF, 4], BF16, name="group", bufs=4, align_bytes=64)
-            h_grouped[g, h] = group
-            interleave(engine, group[:], hb[g][h][:].rearrange("p (t c) -> p t c", t=4))
+            tile = stage.tile([P, BANK, 4], BF16, name="grouped", bufs=4, align_bytes=64)
+            h_grouped[g, h] = tile
+            interleave(engine, tile[:], h_bf[g][h][:].rearrange("p (t c) -> p t c", t=4))
 
         def h_quant(g, h):
-            cols = slice(HALF * h, HALF * (h + 1))
-            nc.vector.quantize_mx(
-                out=h_c[g][:, cols].bitcast(E4M3),
-                scales=h_s[g][:, cols],
-                in_=h_grouped[g, h][:].rearrange("p c t -> p (c t)"),
-            )
+            cols = slice(BANK * h, BANK * (h + 1))
+            quantize(h_codes[g][:, cols], h_scales[g][:, cols], h_grouped[g, h][:].rearrange("p c t -> p (c t)"))
 
-        def pop_widen(a):
+        pop_wide = {}
+        pop_grouped = {}
+
+        def pop_widen_vector(s):
             nc.vector.tensor_scalar(
-                out=pop_bf[a][:].rearrange("r (u p e) -> r p u e", u=2, e=2),
-                in0=pop_raw[:, a, :].bitcast(FP8).rearrange("r (p u e) -> r p u e", u=2, e=2),
+                out=pop_sorted[s][:].rearrange("r (u n e) -> r n u e", u=2, e=2),
+                in0=pop_raw[:, s, :].bitcast(FP8).rearrange("r (n u e) -> r n u e", u=2, e=2),
                 scalar1=one[:],
                 scalar2=None,
                 op0=MULT,
             )
 
-        pop_wide = {}
+        def pop_cast_scalar(s):
+            tile = stage.tile([P, M], BF16, name="pop_wide", align_bytes=64)
+            pop_wide[s] = tile
+            nc.scalar.copy(out=tile[:], in_=pop_raw[:, s, :].bitcast(FP8))
 
-        def pop_cast(a):
-            wide = stage.tile([P, M], BF16, name="wide", bufs=2, align_bytes=64)
-            pop_wide[a] = wide
-            nc.scalar.copy(out=wide[:], in_=pop_raw[:, a, :].bitcast(FP8))
-
-        def pop_sort(a):
+        def pop_sort_scalar(s):
             nc.scalar.copy(
-                out=words(pop_bf[a][:]).rearrange("r (u p) -> r u p", u=2),
-                in_=words(pop_wide[a][:]).rearrange("r (p u) -> r u p", u=2),
+                out=words(pop_sorted[s][:]).rearrange("r (u n) -> r u n", u=2),
+                in_=words(pop_wide[s][:]).rearrange("r (n u) -> r u n", u=2),
             )
 
         def pop_turn(g, z):
-            b = take_bank(("pop", g, z))
+            bank = take_bank(("pop", g, z))
             for a in range(2):
-                pw = words(pop_bf[2 * z + a][:])
                 for u in range(2):
+                    first = (2 * u + g) * P
                     col = (2 * u + a) * P
-                    nc.tensor.transpose(b[:, col:col + P], pw[:, 256 * u + P * g:256 * u + P * (g + 1)], ident[:])
-
-        pop_grouped = {}
+                    nc.tensor.transpose(
+                        bank[:, col:col + P], words(pop_sorted[2 * z + a][:])[:, first:first + P], ident[:]
+                    )
 
         def pop_empty(g, z):
-            if g not in pop_grouped:
-                group = stage.tile([P, 2048], BF16, name="group", bufs=4, align_bytes=64)
-                pop_grouped[g] = group
+            if z == 0:
+                tile = stage.tile([P, 2 * TURNED], BF16, name="grouped", bufs=4, align_bytes=64)
+                pop_grouped[g] = tile
             nc.vector.tensor_tensor(
-                out=pop_grouped[g][:, 1024 * z:1024 * (z + 1)].rearrange("p (r u e) -> p r u e", u=2, e=2),
+                out=pop_grouped[g][:, TURNED * z:TURNED * (z + 1)].rearrange("p (r u e) -> p r u e", u=2, e=2),
                 in0=give_bank(("pop", g, z))[:].bitcast(BF16).rearrange("p (u r e) -> p r u e", u=2, e=2),
-                in1=pop_sc[:, g, :].rearrange("p (u e) -> p u e", u=2).unsqueeze(1).to_broadcast([P, 256, 2, 2]),
+                in1=pop_sc[:, g, :].rearrange("p (u e) -> p u e", u=2).unsqueeze(1).to_broadcast([P, 2 * P, 2, 2]),
                 op=MULT,
             )
 
         def pop_quant(g):
-            nc.vector.quantize_mx(
-                out=p_c[g][:].bitcast(E4M3),
-                scales=p_s[g][:],
-                in_=pop_grouped[g][:],
-            )
+            quantize(pop_codes[g][:], pop_scales[g][:], pop_grouped[g][:])
 
-        load_rows = load.rearrange("(p a) c -> a p c", a=4)
+        load_rows = load.rearrange("(r s) c -> s r c", s=4)
+        load_tiles = {}
 
-        def load_mm(a, h):
-            b = take_bank(("load", a, h))
+        def loading(s, h, engine):
+            bank = take_bank(("load", s, h))
+            cols = slice(BANK * h, BANK * (h + 1))
             for g in range(2):
                 nc.tensor.matmul_mx(
-                    out=b[:],
-                    lhsT=p_c[g][:, P * a:P * (a + 1)].bitcast(E4M3),
-                    lhsT_scale=p_s[g][:, P * a:P * (a + 1)],
-                    rhs=h_c[g][:, 512 * h:512 * (h + 1)].bitcast(E4M3),
-                    rhs_scale=h_s[g][:, 512 * h:512 * (h + 1)],
+                    out=bank[:],
+                    lhsT=pop_codes[g][:, P * s:P * (s + 1)].bitcast(E4M3),
+                    lhsT_scale=pop_scales[g][:, P * s:P * (s + 1)],
+                    rhs=h_codes[g][:, cols].bitcast(E4M3),
+                    rhs_scale=h_scales[g][:, cols],
                     start=(g == 0),
                     stop=(g == 1),
                 )
-
-        load_tiles = {}
-
-        def load_empty(a, h, engine):
-            if a // 2 not in load_tiles:
-                lo = outs.tile([P, 2 * C], F32, name="lo", tag="small", bufs=3, align_bytes=64)
-                load_tiles[a // 2] = lo
-            col = C * (a % 2) + 512 * h
+            if s // 2 not in load_tiles:
+                tile = shared.tile([P, 2 * C], F32, name="load_out", tag="w_load", bufs=K_PASSES, align_bytes=64)
+                load_tiles[s // 2] = tile
+            first = C * (s % 2) + BANK * h
+            out = load_tiles[s // 2][:, first:first + BANK]
             copy(
                 engine,
-                load_tiles[a // 2][:, col:col + 512].rearrange("q (p u e) -> q p u e", u=2, e=2),
-                give_bank(("load", a, h))[:].rearrange("q (u p e) -> q p u e", u=2, e=2),
+                out.rearrange("r (p u e) -> r p u e", u=2, e=2),
+                give_bank(("load", s, h))[:].rearrange("r (u p e) -> r p u e", u=2, e=2),
             )
+            nc.sync.dma_start(out=load_rows[s, :, cols], in_=out)
 
-        def load_store(a, h0, h1):
-            col = C * (a % 2)
-            nc.sync.dma_start(
-                out=load_rows[a, :, 512 * h0:512 * h1], in_=load_tiles[a // 2][:, col + 512 * h0:col + 512 * h1]
-            )
+        all_passes = range(K_PASSES)
 
-
-        def h_passes(tiles, h, passes):
-            for q in passes:
-                for i in tiles:
-                    h_pass(i, h, q)
-
-        def mag_step(i, banks=range(4), run=2):
-            for f in banks:
-                mag_mm(i, f)
-                mag_exp(i, f)
-                if (f + 1) % run == 0:
-                    mag_store(i, f + 1 - run, f + 1)
-
-        def w_share(h, q, split):
-            w_group(h, q, "V", split)
-            w_group(h, q, "S", split)
-
-        def x_empties(j, engines):
-            for q in range(3):
-                x_empty(j, q, engines[q])
-
-        def h_adds(tiles, h):
-            for i in tiles:
-                h_add(i, h)
-
-        def h_both(tiles, q):
-            for i in tiles:
-                for h in range(2):
-                    h_pass(i, h, q)
-
-        warm(4)
+        warm(4, zeros[:])
         x_turn(0)
         x_turn(1)
-        x_empties(0, "VSS")
+        x_empty(0, "VSS")
         x_quant(0, 0, 2)
         x_quant(0, 2, 3)
-        w_share(0, 0, 320)
-        w_share(1, 0, 224)
+        w_group(0, 0)
+        w_group(1, 0)
         w_quant(0, 0)
-        warm(2)
-        warm(3, w_raw[0][:, 0, 0:512])
+        warm(2, zeros[:])
+        warm(3, w_raw[0][:, 0, 0:BANK])
+
         x_turn(2)
         x_turn(3)
         h_passes((0, 1), 0, (0,))
-        x_empties(1, "VSS")
+        x_empty(1, "VSS")
         w_quant(1, 0)
         h_passes((0,), 1, (0,))
         x_quant(1, 0, 2)
-        w_share(0, 1, 384)
+        w_group(0, 1)
         x_quant(1, 2, 3)
         w_quant(0, 1)
         h_passes((2, 3), 0, (0,))
+
         x_turn(4)
         x_turn(5)
-        w_share(1, 1, 128)
-        x_empties(2, "VSS")
+        w_group(1, 1)
+        x_empty(2, "VSS")
         w_quant(1, 1)
         h_passes(range(4), 0, (1,))
         h_passes((0,), 1, (1,))
         x_quant(2, 0, 2)
-        w_share(0, 2, 320)
+        w_group(0, 2)
         x_quant(2, 2, 3)
         w_quant(0, 2)
         h_passes((1,), 1, (0, 1))
         h_passes((4, 5), 0, (0, 1))
-        w_share(1, 2, 256)
+        w_group(1, 2)
         h_passes(range(6), 0, (2,))
         w_quant(1, 2)
-        h_add(0, 0)
-        pop_cast(0)
-        pop_cast(1)
-        pop_sort(0)
-        pop_sort(1)
-        h_adds((1, 2, 3), 0)
+
+        h_add((0,), 0)
+        for s in (0, 1):
+            pop_cast_scalar(s)
+        for s in (0, 1):
+            pop_sort_scalar(s)
+        h_add((1, 2, 3), 0)
         h_group(0, 0, "S")
         h_passes((0, 1), 1, (2,))
-        h_passes((2,), 1, range(3))
-        h_passes((3,), 1, range(3))
-        h_adds((0, 1), 1)
+        h_passes((2,), 1, all_passes)
+        h_passes((3,), 1, all_passes)
+        h_add((0, 1), 1)
+        h_passes((4,), 1, (0, 1))
         ht_turn(0)
         ht_turn(1)
-        h_add(2, 1)
+        h_add((2,), 1)
         ht_empty(0, "V")
         ht_empty(1, "S")
-        depth_widen()
-        h_passes((4,), 1, range(3))
-        h_passes((5,), 1, range(3))
-        h_add(3, 1)
-        ht_quant(0)
-        pop_widen(2)
+        nc.scalar.copy(out=depth_f[:], in_=depth_bf[:].rearrange("p g t -> p (g t)"))
+        h_passes((4,), 1, (2,))
+        h_passes((5,), 1, all_passes)
+        ht_quant(0, 1)
+        h_add((3,), 1)
+        pop_widen_vector(2)
         x_sort(6)
-        ht_quant(1)
+        ht_quant(1, 1)
         x_sort(7)
-        mag_step(0)
-        h_add(4, 0)
-        h_add(4, 1)
-        h_add(5, 0)
-        h_add(5, 1)
+
+        spectrum(0, banks=range(BINS - 1))
+        h_add((4,), 0)
+        spectrum(0, banks=(BINS - 1,))
+        h_add((4,), 1)
+        h_add((5,), 0)
+        h_add((5,), 1)
         ht_turn(2)
         ht_turn(3)
         x_turn(6)
         x_turn(7)
         ht_empty(2, "S")
         ht_empty(3, "S")
-        pop_widen(3)
+        pop_widen_vector(3)
         ht_quant(2, 2)
-        x_empties(3, "VSV")
-        mag_step(1)
+        x_empty(3, "VSV")
+        spectrum(1)
         x_quant(3, 0, 2)
         x_quant(3, 2, 3)
         ht_turn(4)
@@ -532,42 +482,40 @@ def tile_hrtf_weights_synthesis_s8_kernel(
         ht_empty(5, "S")
         pop_empty(0, 0)
         pop_empty(1, 0)
-        mag_step(2)
+        spectrum(2)
         h_group(0, 1, "S")
         pop_empty(0, 1)
         ht_quant(4, 2)
         pop_empty(1, 1)
-        for i in (6, 7):
-            h_passes((i,), 0, range(3))
-            mag_step(3, banks=(2 * (i - 6), 2 * (i - 6) + 1))
+
+        for a in range(2):
+            h_passes((6 + a,), 0, all_passes)
+            spectrum(3, banks=(2 * a, 2 * a + 1))
         h_quant(0, 0)
         pop_quant(0)
-        h_add(6, 0)
+        h_add((6,), 0)
         pop_quant(1)
-        h_add(7, 0)
+        h_add((7,), 0)
         h_quant(0, 1)
         h_group(1, 0, "V")
-        for i in (6, 7):
-            h_passes((i,), 1, range(3))
-            h_add(i, 1)
-            mag_step(4, banks=(2 * (i - 6), 2 * (i - 6) + 1))
+        for a in range(2):
+            h_passes((6 + a,), 1, all_passes)
+            h_add((6 + a,), 1)
+            spectrum(4, banks=(2 * a, 2 * a + 1))
         h_quant(1, 0)
         h_group(1, 1, "V")
-        mag_step(5)
+        spectrum(5)
+
         ht_turn(6)
         ht_turn(7)
         h_quant(1, 1)
         ht_empty(6, "V")
         ht_empty(7, "S")
         ht_quant(6, 2)
-        for a in range(4):
-            load_mm(a, 0)
-            load_empty(a, 0, "SVSV"[a])
-            load_store(a, 0, 1)
-        for a in range(4):
-            load_mm(a, 1)
-            load_empty(a, 1, "V")
-            load_store(a, 1, 2)
-            mag_step(6, banks=(a,))
-        mag_step(7, banks=(0, 1))
-        mag_step(7, banks=(2, 3), run=1)
+        for s in range(4):
+            loading(s, 0, "SV"[s % 2])
+        for s in range(4):
+            loading(s, 1, "V")
+            spectrum(6, banks=(s,))
+        spectrum(7, banks=(0, 1))
+        spectrum(7, banks=(2, 3), store_every=1)

@@ -60,7 +60,6 @@ def tile_hrtf_weights_synthesis_s8_kernel(
 
         ident = kept("ident", [P, P], F32)
         table_probe = kept("table_probe", [P, 1], F32)
-        zeros = kept("zeros", [P, BANK], BF16)
         x_raw = [shared.tile([P, 2 * K], BF16, name="x_raw%d" % j, tag="x_mag", align_bytes=64) for j in range(4)]
         w_raw = [
             shared.tile([P, 4, C], BF16, name="w_raw%d" % q, tag="w_load", bufs=K_PASSES, align_bytes=64)
@@ -87,7 +86,6 @@ def tile_hrtf_weights_synthesis_s8_kernel(
         pop_codes = [kept("pop_codes%d" % g, [P, R], U32) for g in range(2)]
         pop_scales = [kept("pop_scales%d" % g, [P, R], U8) for g in range(2)]
 
-        nc.vector.memset(zeros[:], 0.0)
         nc.vector.memset(table_probe[:], 0.0)
         nc.vector.memset(one[:], 1.0)
         nc.scalar.activation(out=table_probe[:], in_=table_probe[:], func=EXP)
@@ -147,12 +145,6 @@ def tile_hrtf_weights_synthesis_s8_kernel(
 
         def quantize(codes, scales, values):
             nc.vector.quantize_mx(out=codes.bitcast(E4M3), scales=scales, in_=values)
-
-        def warm(count, moving):
-            bank = take_bank("warm")
-            for repeat in range(count):
-                nc.tensor.matmul(bank[:], lhsT=zeros[:, 0:P], rhs=moving, start=True, stop=True)
-            give_bank("warm")
 
         def empty_turned(engine, out, bank):
             copy(
@@ -387,7 +379,6 @@ def tile_hrtf_weights_synthesis_s8_kernel(
 
         all_passes = range(K_PASSES)
 
-        warm(4, zeros[:])
         x_turn(0)
         x_turn(1)
         x_empty(0, "VSS")
@@ -396,8 +387,6 @@ def tile_hrtf_weights_synthesis_s8_kernel(
         w_group(0, 0)
         w_group(1, 0)
         w_quant(0, 0)
-        warm(2, zeros[:])
-        warm(3, w_raw[0][:, 0, 0:BANK])
 
         x_turn(2)
         x_turn(3)

@@ -457,8 +457,8 @@ def tile_hrtf_weights_synthesis_s8_kernel(
         ht_empty(2, "S")
         ht_empty(3, "S")
         pop_widen_vector(3)
+        x_empty(3, "SVS")
         ht_quant(2, 2)
-        x_empty(3, "VSV")
         spectrum(1)
         x_quant(3, 0, 2)
         x_quant(3, 2, 3)
@@ -483,9 +483,8 @@ def tile_hrtf_weights_synthesis_s8_kernel(
         h_quant(0, 0)
         pop_quant(0)
         h_add((6,), 0)
-        pop_quant(1)
         h_add((7,), 0)
-        h_quant(0, 1)
+        pop_quant(1)
         h_group(1, 0, "V")
         for a in range(2):
             h_passes((6 + a,), 1, all_passes)
@@ -493,16 +492,17 @@ def tile_hrtf_weights_synthesis_s8_kernel(
             spectrum(4, banks=(2 * a, 2 * a + 1))
         h_quant(1, 0)
         h_group(1, 1, "V")
+        h_quant(0, 1)
         spectrum(5)
 
         ht_turn(6)
         ht_turn(7)
-        h_quant(1, 1)
         ht_empty(6, "V")
         ht_empty(7, "S")
+        h_quant(1, 1)
         ht_quant(6, 2)
         for s in range(4):
-            loading(s, 0, "SV"[s % 2])
+            loading(s, 0, "S")
         for s in range(4):
             loading(s, 1, "V")
             spectrum(6, banks=(s,))

@@ -26,7 +26,7 @@ TURNED = 2 * BANK
 K_PASSES = K // PASS
 BINS = F // BANK
 
-VECTOR_COLS = (320, 192)
+VECTOR_COLS = (288, 192)
 
 
 def tile_hrtf_weights_synthesis_s8_kernel(
@@ -74,8 +74,8 @@ def tile_hrtf_weights_synthesis_s8_kernel(
         pop_sc = kept("pop_sc", [P, 2, 4], F32)
         one = kept("one", [P, 1], F32)
         pop_sorted = [kept("pop_sorted%d" % s, [P, M], BF16) for s in range(4)]
-        x_codes = [kept("x_codes%d" % j, [P, K_PASSES, 2 * P], U32) for j in range(4)]
-        x_scales = [kept("x_scales%d" % j, [P, K_PASSES, 2 * P], U8) for j in range(4)]
+        x_codes = [kept("x_codes%d" % j, [P, 2 * K_PASSES * P], U32) for j in range(4)]
+        x_scales = [kept("x_scales%d" % j, [P, 2 * K_PASSES * P], U8) for j in range(4)]
         w_codes = [[kept("w_codes%d%d" % (h, q), [P, BANK], U32) for q in range(K_PASSES)] for h in range(2)]
         w_scales = [[kept("w_scales%d%d" % (h, q), [P, BANK], U8) for q in range(K_PASSES)] for h in range(2)]
         h_bf = [[kept("h_bf%d%d" % (g, h), [P, 4 * BANK], BF16) for h in range(2)] for g in range(2)]
@@ -86,8 +86,8 @@ def tile_hrtf_weights_synthesis_s8_kernel(
         pop_codes = [kept("pop_codes%d" % g, [P, R], U32) for g in range(2)]
         pop_scales = [kept("pop_scales%d" % g, [P, R], U8) for g in range(2)]
 
-        nc.vector.memset(table_probe[:], 0.0)
         nc.vector.memset(one[:], 1.0)
+        nc.vector.memset(table_probe[:], 0.0)
         nc.scalar.activation(out=table_probe[:], in_=table_probe[:], func=EXP)
         make_identity(nc, ident[:])
         b_scales_i32 = b_scales[:].rearrange("p g n -> p (g n)").bitcast(I32)
@@ -100,9 +100,9 @@ def tile_hrtf_weights_synthesis_s8_kernel(
                 out=x_raw[i // 2][:, K * (i % 2):K * (i % 2 + tiles)], in_=src[:, K * t:K * (t + tiles)]
             )
 
-        def fetch_w(q):
+        def fetch_w(q, cols=slice(0, C)):
             src = w[q * PASS:(q + 1) * PASS, :]
-            nc.sync.dma_start(out=w_raw[q][:], in_=src.rearrange("(p t) c -> p t c", t=4))
+            nc.sync.dma_start(out=w_raw[q][:, :, cols], in_=src.rearrange("(p t) c -> p t c", t=4)[:, :, cols])
 
         def fetch_prior(j):
             g, t = divmod(2 * j, 4)
@@ -120,10 +120,15 @@ def tile_hrtf_weights_synthesis_s8_kernel(
                 in_=basis_words.bitcast(I32).rearrange("g p n -> p g n"),
             )
 
-        for q in range(K_PASSES):
-            fetch_x(2 * q, 1)
-            fetch_x(2 * q + 1, 1)
-            fetch_w(q)
+        fetch_x(0, 1)
+        fetch_x(1, 1)
+        fetch_w(0)
+        fetch_x(2, 1)
+        fetch_x(3, 1)
+        fetch_w(1)
+        fetch_x(4, 1)
+        fetch_x(5, 1)
+        fetch_w(2)
         fetch_prior(0)
         nc.sync.dma_start(out=pop_raw[:], in_=pop_bytes.rearrange("(r s) k -> r s k", s=4))
         fetch_prior(1)
@@ -133,6 +138,14 @@ def tile_hrtf_weights_synthesis_s8_kernel(
         fetch_prior(2)
         fetch_prior(3)
         nc.sync.dma_start(out=pop_sc[:], in_=pop_scale.rearrange("o (g p t) -> p (o g) t", p=P, t=4))
+
+        def warm_up(count):
+            bank = take_bank("warm")
+            for n in range(count):
+                nc.tensor.matmul(
+                    bank[:], lhsT=one[:].to_broadcast([P, P]), rhs=one[:].to_broadcast([P, BANK]), start=True, stop=True
+                )
+            give_bank("warm")
 
         def words(ap):
             return ap.bitcast(F32)
@@ -166,38 +179,43 @@ def tile_hrtf_weights_synthesis_s8_kernel(
         def x_words(i):
             return words(x_raw[i // 2][:, K * (i % 2):K * (i % 2 + 1)])
 
-        def x_sort(i):
+        def x_sort(i, engine):
             tile = stage.tile([P, K // 2], F32, name="x_sorted", align_bytes=64)
             x_sorted[i] = tile
-            nc.vector.tensor_copy(
-                out=tile[:].rearrange("m (u n) -> m u n", u=2), in_=x_words(i).rearrange("m (n u) -> m u n", u=2)
+            copy(
+                engine, tile[:].rearrange("m (u n) -> m u n", u=2), x_words(i).rearrange("m (n u) -> m u n", u=2)
             )
 
-        def x_turn(i):
-            j, a = divmod(i, 2)
-            for q in range(K_PASSES):
-                bank = take_bank(("x", j, q)) if a == 0 else bank_of["x", j, q][0]
+        def x_turn(i, tiles, only=None):
+            for n in range(K_PASSES * tiles):
+                if only is not None and n // K_PASSES != only:
+                    continue
+                a, q = divmod(n, K_PASSES)
+                bank = take_bank(("x", i, n // 2)) if n % 2 == 0 else bank_of["x", i, n // 2][0]
                 for u in range(2):
-                    if i in x_sorted:
+                    if i + a in x_sorted:
                         first = (K_PASSES * u + q) * P
-                        src = x_sorted[i][:, first:first + P]
+                        src = x_sorted[i + a][:, first:first + P]
                     else:
-                        src = x_words(i)[:, WORDS * q + u:WORDS * (q + 1):2]
-                    col = (2 * a + u) * P
+                        src = x_words(i + a)[:, WORDS * q + u:WORDS * (q + 1):2]
+                    col = (2 * (n % 2) + u) * P
                     nc.tensor.transpose(bank[:, col:col + P], src, ident[:])
 
-        def x_empty(j, engines):
-            tile = stage.tile([P, K_PASSES * TURNED], BF16, name="x_grouped", align_bytes=64)
-            x_grouped[j] = tile
-            for q in range(K_PASSES):
-                empty_turned(engines[q], tile[:, TURNED * q:TURNED * (q + 1)], give_bank(("x", j, q)))
-
-        def x_quant(j, q0, q1):
-            quantize(
-                x_codes[j][:, q0:q1, :].rearrange("p q m -> p (q m)"),
-                x_scales[j][:, q0:q1, :].rearrange("p q m -> p (q m)"),
-                x_grouped[j][:, TURNED * q0:TURNED * q1],
+        def x_empty(i, tiles, n, engine):
+            j, a = divmod(i, 2)
+            if j not in x_grouped:
+                tile = stage.tile([P, 2 * K_PASSES * PASS], BF16, name="x_grouped", align_bytes=64)
+                x_grouped[j] = tile
+            count = min(2, K_PASSES * tiles - 2 * n)
+            first = PASS * (K_PASSES * a + 2 * n)
+            copy(
+                engine,
+                words(x_grouped[j][:, first:first + PASS * count]).rearrange("p (a m u) -> p a m u", a=count, u=2),
+                give_bank(("x", i, n))[:, :WORDS * count].rearrange("p (a u m) -> p a m u", a=count, u=2),
             )
+
+        def x_quant(j, n0, n1):
+            quantize(x_codes[j][:, P * n0:P * n1], x_scales[j][:, P * n0:P * n1], x_grouped[j][:, PASS * n0:PASS * n1])
 
         w_grouped = {}
 
@@ -215,11 +233,11 @@ def tile_hrtf_weights_synthesis_s8_kernel(
             for q in passes:
                 for i in tiles:
                     bank = take_bank(("h", i, h)) if q == 0 else bank_of["h", i, h][0]
-                    cols = slice((i % 2) * P, (i % 2 + 1) * P)
+                    first = (K_PASSES * (i % 2) + q) * P
                     nc.tensor.matmul_mx(
                         out=bank[:],
-                        lhsT=x_codes[i // 2][:, q, cols].bitcast(E4M3),
-                        lhsT_scale=x_scales[i // 2][:, q, cols],
+                        lhsT=x_codes[i // 2][:, first:first + P].bitcast(E4M3),
+                        lhsT_scale=x_scales[i // 2][:, first:first + P],
                         rhs=w_codes[h][q][:].bitcast(E4M3),
                         rhs_scale=w_scales[h][q][:],
                         start=(q == 0),
@@ -293,10 +311,11 @@ def tile_hrtf_weights_synthesis_s8_kernel(
 
         h_grouped = {}
 
-        def h_group(g, h, engine):
-            tile = stage.tile([P, BANK, 4], BF16, name="grouped", bufs=4, align_bytes=64)
-            h_grouped[g, h] = tile
-            interleave(engine, tile[:], h_bf[g][h][:].rearrange("p (t c) -> p t c", t=4))
+        def h_group(g, h, engine, cols=slice(0, BANK)):
+            if (g, h) not in h_grouped:
+                tile = stage.tile([P, BANK, 4], BF16, name="grouped", bufs=4, align_bytes=64)
+                h_grouped[g, h] = tile
+            interleave(engine, h_grouped[g, h][:, cols, :], h_bf[g][h][:].rearrange("p (t c) -> p t c", t=4)[:, :, cols])
 
         def h_quant(g, h):
             cols = slice(BANK * h, BANK * (h + 1))
@@ -352,7 +371,7 @@ def tile_hrtf_weights_synthesis_s8_kernel(
         load_rows = load.rearrange("(r s) c -> s r c", s=4)
         load_tiles = {}
 
-        def loading(s, h, engine):
+        def loading(s, h, engine, store_from):
             bank = take_bank(("load", s, h))
             cols = slice(BANK * h, BANK * (h + 1))
             for g in range(2):
@@ -375,48 +394,53 @@ def tile_hrtf_weights_synthesis_s8_kernel(
                 out.rearrange("r (p u e) -> r p u e", u=2, e=2),
                 give_bank(("load", s, h))[:].rearrange("r (u p e) -> r p u e", u=2, e=2),
             )
-            nc.sync.dma_start(out=load_rows[s, :, cols], in_=out)
+            if store_from is not None:
+                cols = slice(BANK * store_from, BANK * (h + 1))
+                row = load_tiles[s // 2][:, C * (s % 2):C * (s % 2 + 1)]
+                nc.sync.dma_start(out=load_rows[s, :, cols], in_=row[:, cols])
 
         all_passes = range(K_PASSES)
-
-        x_turn(0)
-        x_turn(1)
-        x_empty(0, "VSS")
+        warm_up(1)
+        for i in (0, 1):
+            x_turn(i, 1)
+            x_empty(i, 1, 0, "V")
+            x_empty(i, 1, 1, "S")
+        warm_up(2)
         x_quant(0, 0, 2)
-        x_quant(0, 2, 3)
         w_group(0, 0)
-        w_group(1, 0)
+        x_quant(0, 2, 6)
+        x_turn(2, 2)
         w_quant(0, 0)
-
-        x_turn(2)
-        x_turn(3)
+        w_group(1, 0)
         h_passes((0, 1), 0, (0,))
-        x_empty(1, "VSS")
+        x_empty(2, 2, 0, "V")
+        x_empty(2, 2, 1, "S")
+        x_empty(2, 2, 2, "S")
         w_quant(1, 0)
-        h_passes((0,), 1, (0,))
+        h_passes((0, 1), 1, (0,))
         x_quant(1, 0, 2)
         w_group(0, 1)
-        x_quant(1, 2, 3)
+        x_quant(1, 2, 6)
+        h_passes((2,), 0, (0,))
+        x_turn(4, 2)
         w_quant(0, 1)
-        h_passes((2, 3), 0, (0,))
-
-        x_turn(4)
-        x_turn(5)
+        h_passes((0, 1, 2), 0, (1,))
         w_group(1, 1)
-        x_empty(2, "VSS")
+        x_empty(4, 2, 0, "V")
+        x_empty(4, 2, 1, "S")
+        x_empty(4, 2, 2, "S")
+        h_passes((3,), 0, (0, 1))
         w_quant(1, 1)
-        h_passes(range(4), 0, (1,))
-        h_passes((0,), 1, (1,))
+        h_passes((0, 1), 1, (1,))
         x_quant(2, 0, 2)
         w_group(0, 2)
-        x_quant(2, 2, 3)
+        x_quant(2, 2, 6)
+        h_passes((4,), 0, (0, 1))
         w_quant(0, 2)
-        h_passes((1,), 1, (0, 1))
-        h_passes((4, 5), 0, (0, 1))
+        h_passes((5,), 0, (0, 1))
         w_group(1, 2)
         h_passes(range(6), 0, (2,))
         w_quant(1, 2)
-
         h_add((0,), 0)
         for s in (0, 1):
             pop_cast_scalar(s)
@@ -440,9 +464,9 @@ def tile_hrtf_weights_synthesis_s8_kernel(
         ht_quant(0, 1)
         h_add((3,), 1)
         pop_widen_vector(2)
-        x_sort(6)
+        x_sort(6, "V")
         ht_quant(1, 1)
-        x_sort(7)
+        x_sort(7, "V")
 
         spectrum(0, banks=range(BINS - 1))
         h_add((4,), 0)
@@ -452,16 +476,16 @@ def tile_hrtf_weights_synthesis_s8_kernel(
         h_add((5,), 1)
         ht_turn(2)
         ht_turn(3)
-        x_turn(6)
-        x_turn(7)
+        x_turn(6, 2)
         ht_empty(2, "S")
         ht_empty(3, "S")
         pop_widen_vector(3)
-        x_empty(3, "SVS")
+        for n in range(3):
+            x_empty(6, 2, n, "SVS"[n])
         ht_quant(2, 2)
         spectrum(1)
         x_quant(3, 0, 2)
-        x_quant(3, 2, 3)
+        x_quant(3, 2, 6)
         ht_turn(4)
         ht_turn(5)
         for z in range(2):
@@ -502,9 +526,9 @@ def tile_hrtf_weights_synthesis_s8_kernel(
         h_quant(1, 1)
         ht_quant(6, 2)
         for s in range(4):
-            loading(s, 0, "S")
+            loading(s, 0, "S", 0)
         for s in range(4):
-            loading(s, 1, "V")
+            loading(s, 1, "V", 1)
             spectrum(6, banks=(s,))
         spectrum(7, banks=(0, 1))
         spectrum(7, banks=(2, 3), store_every=1)

@@ -130,12 +130,12 @@ def tile_hrtf_weights_synthesis_s8_kernel(
         fetch_x(5, 1)
         fetch_w(2)
         fetch_prior(0)
-        nc.sync.dma_start(out=pop_raw[:], in_=pop_bytes.rearrange("(r s) k -> r s k", s=4))
         fetch_prior(1)
         fetch_basis()
         nc.sync.dma_start(out=depth_bf[:], in_=depth.rearrange("(g p t) -> p g t", p=P, t=4))
         fetch_x(6, 2)
         fetch_prior(2)
+        nc.sync.dma_start(out=pop_raw[:], in_=pop_bytes.rearrange("(r s) k -> r s k", s=4))
         fetch_prior(3)
         nc.sync.dma_start(out=pop_sc[:], in_=pop_scale.rearrange("o (g p t) -> p (o g) t", p=P, t=4))
 
@@ -321,7 +321,6 @@ def tile_hrtf_weights_synthesis_s8_kernel(
             cols = slice(BANK * h, BANK * (h + 1))
             quantize(h_codes[g][:, cols], h_scales[g][:, cols], h_grouped[g, h][:].rearrange("p c t -> p (c t)"))
 
-        pop_wide = {}
         pop_grouped = {}
 
         def pop_widen_vector(s):
@@ -331,17 +330,6 @@ def tile_hrtf_weights_synthesis_s8_kernel(
                 scalar1=one[:],
                 scalar2=None,
                 op0=MULT,
-            )
-
-        def pop_cast_scalar(s):
-            tile = stage.tile([P, M], BF16, name="pop_wide", align_bytes=64)
-            pop_wide[s] = tile
-            nc.scalar.copy(out=tile[:], in_=pop_raw[:, s, :].bitcast(FP8))
-
-        def pop_sort_scalar(s):
-            nc.scalar.copy(
-                out=words(pop_sorted[s][:]).rearrange("r (u n) -> r u n", u=2),
-                in_=words(pop_wide[s][:]).rearrange("r (n u) -> r u n", u=2),
             )
 
         def pop_turn(g, z):
@@ -442,10 +430,6 @@ def tile_hrtf_weights_synthesis_s8_kernel(
         h_passes(range(6), 0, (2,))
         w_quant(1, 2)
         h_add((0,), 0)
-        for s in (0, 1):
-            pop_cast_scalar(s)
-        for s in (0, 1):
-            pop_sort_scalar(s)
         h_add((1, 2, 3), 0)
         h_group(0, 0, "S")
         h_passes((0, 1), 1, (2,))
@@ -463,7 +447,6 @@ def tile_hrtf_weights_synthesis_s8_kernel(
         h_passes((5,), 1, all_passes)
         ht_quant(0, 1)
         h_add((3,), 1)
-        pop_widen_vector(2)
         x_sort(6, "V")
         ht_quant(1, 1)
         x_sort(7, "V")
@@ -479,11 +462,14 @@ def tile_hrtf_weights_synthesis_s8_kernel(
         x_turn(6, 2)
         ht_empty(2, "S")
         ht_empty(3, "S")
-        pop_widen_vector(3)
+        pop_widen_vector(0)
+        pop_widen_vector(1)
         for n in range(3):
-            x_empty(6, 2, n, "SVS"[n])
+            x_empty(6, 2, n, "SSS"[n])
         ht_quant(2, 2)
         spectrum(1)
+        pop_widen_vector(2)
+        pop_widen_vector(3)
         x_quant(3, 0, 2)
         x_quant(3, 2, 6)
         ht_turn(4)

@@ -55,7 +55,7 @@ def tile_hrtf_weights_synthesis_s8_kernel(
             return bank
 
         def kept(name, shape, dt):
-            tile = keep.tile(shape, dt, name=name, align_bytes=64)
+            tile = keep.tile(shape, dt, name=name, align_bytes=256)
             return tile
 
         ident = kept("ident", [P, P], F32)

@@ -26,7 +26,7 @@ TURNED = 2 * BANK
 K_PASSES = K // PASS
 BINS = F // BANK
 
-VECTOR_COLS = (288, 192)
+VECTOR_COLS = (288, 224)
 
 
 def tile_hrtf_weights_synthesis_s8_kernel(
@@ -60,9 +60,9 @@ def tile_hrtf_weights_synthesis_s8_kernel(
 
         ident = kept("ident", [P, P], F32)
         table_probe = kept("table_probe", [P, 1], F32)
-        x_raw = [shared.tile([P, 2 * K], BF16, name="x_raw%d" % j, tag="x_mag", align_bytes=64) for j in range(4)]
+        x_raw = [shared.tile([P, 2 * K], BF16, name="x_raw%d" % j, tag="x_mag", align_bytes=256) for j in range(4)]
         w_raw = [
-            shared.tile([P, 4, C], BF16, name="w_raw%d" % q, tag="w_load", bufs=K_PASSES, align_bytes=64)
+            shared.tile([P, 4, C], BF16, name="w_raw%d" % q, tag="w_load", bufs=K_PASSES, align_bytes=256)
             for q in range(K_PASSES)
         ]
         prior_sb = [kept("prior%d" % j, [P, 2, C], BF16) for j in range(4)]
@@ -125,16 +125,16 @@ def tile_hrtf_weights_synthesis_s8_kernel(
         fetch_w(0)
         fetch_x(2, 1)
         fetch_x(3, 1)
-        fetch_w(1)
         fetch_x(4, 1)
-        fetch_x(5, 1)
+        fetch_w(1)
         fetch_w(2)
         fetch_prior(0)
+        fetch_x(5, 1)
         fetch_prior(1)
         fetch_basis()
         nc.sync.dma_start(out=depth_bf[:], in_=depth.rearrange("(g p t) -> p g t", p=P, t=4))
-        fetch_x(6, 2)
         fetch_prior(2)
+        fetch_x(6, 2)
         nc.sync.dma_start(out=pop_raw[:], in_=pop_bytes.rearrange("(r s) k -> r s k", s=4))
         fetch_prior(3)
         nc.sync.dma_start(out=pop_sc[:], in_=pop_scale.rearrange("o (g p t) -> p (o g) t", p=P, t=4))
@@ -180,7 +180,7 @@ def tile_hrtf_weights_synthesis_s8_kernel(
             return words(x_raw[i // 2][:, K * (i % 2):K * (i % 2 + 1)])
 
         def x_sort(i, engine):
-            tile = stage.tile([P, K // 2], F32, name="x_sorted", align_bytes=64)
+            tile = stage.tile([P, K // 2], F32, name="x_sorted", align_bytes=256)
             x_sorted[i] = tile
             copy(
                 engine, tile[:].rearrange("m (u n) -> m u n", u=2), x_words(i).rearrange("m (n u) -> m u n", u=2)
@@ -204,7 +204,7 @@ def tile_hrtf_weights_synthesis_s8_kernel(
         def x_empty(i, tiles, n, engine):
             j, a = divmod(i, 2)
             if j not in x_grouped:
-                tile = stage.tile([P, 2 * K_PASSES * PASS], BF16, name="x_grouped", align_bytes=64)
+                tile = stage.tile([P, 2 * K_PASSES * PASS], BF16, name="x_grouped", align_bytes=256)
                 x_grouped[j] = tile
             count = min(2, K_PASSES * tiles - 2 * n)
             first = PASS * (K_PASSES * a + 2 * n)
@@ -219,29 +219,31 @@ def tile_hrtf_weights_synthesis_s8_kernel(
 
         w_grouped = {}
 
-        def w_group(h, q):
-            tile = stage.tile([P, BANK, 4], BF16, name="w_grouped", bufs=3, align_bytes=64)
+        def w_group(h, q, share=None):
+            tile = stage.tile([P, BANK, 4], BF16, name="w_grouped", bufs=3, align_bytes=256)
             w_grouped[h, q] = tile
             half = w_raw[q][:, :, h * BANK:(h + 1) * BANK]
-            for engine, cols in (("V", slice(0, VECTOR_COLS[h])), ("S", slice(VECTOR_COLS[h], BANK))):
+            share = share or VECTOR_COLS[h]
+            for engine, cols in (("V", slice(0, share)), ("S", slice(share, BANK))):
                 interleave(engine, tile[:, cols, :], half[:, :, cols])
 
-        def w_quant(h, q):
-            quantize(w_codes[h][q][:], w_scales[h][q][:], w_grouped[h, q][:].rearrange("p c t -> p (c t)"))
+        def w_quant(h, q, cols=slice(0, BANK)):
+            values = w_grouped[h, q][:, cols, :].rearrange("p c t -> p (c t)")
+            quantize(w_codes[h][q][:, cols], w_scales[h][q][:, cols], values)
 
-        def h_passes(tiles, h, passes):
+        def h_passes(tiles, h, passes, cols=slice(0, BANK)):
             for q in passes:
                 for i in tiles:
                     bank = take_bank(("h", i, h)) if q == 0 else bank_of["h", i, h][0]
                     first = (K_PASSES * (i % 2) + q) * P
                     nc.tensor.matmul_mx(
-                        out=bank[:],
+                        out=bank[:, cols],
                         lhsT=x_codes[i // 2][:, first:first + P].bitcast(E4M3),
                         lhsT_scale=x_scales[i // 2][:, first:first + P],
-                        rhs=w_codes[h][q][:].bitcast(E4M3),
-                        rhs_scale=w_scales[h][q][:],
+                        rhs=w_codes[h][q][:, cols].bitcast(E4M3),
+                        rhs_scale=w_scales[h][q][:, cols],
                         start=(q == 0),
-                        stop=(q == K_PASSES - 1),
+                        stop=(q == K_PASSES - 1 and cols.stop == BANK),
                     )
 
         def h_row(i, h):
@@ -270,7 +272,7 @@ def tile_hrtf_weights_synthesis_s8_kernel(
         def ht_empty(i, engine):
             j, a = divmod(i, 2)
             if a == 0:
-                tile = stage.tile([P, 2 * TURNED], BF16, name="ht_grouped", align_bytes=64)
+                tile = stage.tile([P, 2 * TURNED], BF16, name="ht_grouped", align_bytes=256)
                 ht_grouped[j] = tile
             empty_turned(engine, ht_grouped[j][:, TURNED * a:TURNED * (a + 1)], give_bank(("ht", i)))
 
@@ -297,7 +299,7 @@ def tile_hrtf_weights_synthesis_s8_kernel(
                         stop=(h == 1),
                     )
                 if f == 0:
-                    tile = shared.tile([P, F], F32, name="mag_out", tag="x_mag", align_bytes=64)
+                    tile = shared.tile([P, F], F32, name="mag_out", tag="x_mag", align_bytes=256)
                     mag_tiles[i] = tile
                 nc.scalar.activation(
                     out=mag_tiles[i][:, BANK * f:BANK * (f + 1)],
@@ -313,7 +315,7 @@ def tile_hrtf_weights_synthesis_s8_kernel(
 
         def h_group(g, h, engine, cols=slice(0, BANK)):
             if (g, h) not in h_grouped:
-                tile = stage.tile([P, BANK, 4], BF16, name="grouped", bufs=4, align_bytes=64)
+                tile = stage.tile([P, BANK, 4], BF16, name="grouped", bufs=4, align_bytes=256)
                 h_grouped[g, h] = tile
             interleave(engine, h_grouped[g, h][:, cols, :], h_bf[g][h][:].rearrange("p (t c) -> p t c", t=4)[:, :, cols])
 
@@ -344,7 +346,7 @@ def tile_hrtf_weights_synthesis_s8_kernel(
 
         def pop_empty(g, z):
             if z == 0:
-                tile = stage.tile([P, 2 * TURNED], BF16, name="grouped", bufs=4, align_bytes=64)
+                tile = stage.tile([P, 2 * TURNED], BF16, name="grouped", bufs=4, align_bytes=256)
                 pop_grouped[g] = tile
             nc.vector.tensor_tensor(
                 out=pop_grouped[g][:, TURNED * z:TURNED * (z + 1)].rearrange("p (r u e) -> p r u e", u=2, e=2),
@@ -373,7 +375,7 @@ def tile_hrtf_weights_synthesis_s8_kernel(
                     stop=(g == 1),
                 )
             if s // 2 not in load_tiles:
-                tile = shared.tile([P, 2 * C], F32, name="load_out", tag="w_load", bufs=K_PASSES, align_bytes=64)
+                tile = shared.tile([P, 2 * C], F32, name="load_out", tag="w_load", bufs=K_PASSES, align_bytes=256)
                 load_tiles[s // 2] = tile
             first = C * (s % 2) + BANK * h
             out = load_tiles[s // 2][:, first:first + BANK]
@@ -388,6 +390,7 @@ def tile_hrtf_weights_synthesis_s8_kernel(
                 nc.sync.dma_start(out=load_rows[s, :, cols], in_=row[:, cols])
 
         all_passes = range(K_PASSES)
+        low, high = slice(0, WORDS), slice(WORDS, BANK)
         warm_up(1)
         for i in (0, 1):
             x_turn(i, 1)
@@ -395,126 +398,129 @@ def tile_hrtf_weights_synthesis_s8_kernel(
             x_empty(i, 1, 1, "S")
         warm_up(2)
         x_quant(0, 0, 2)
-        w_group(0, 0)
         x_quant(0, 2, 6)
+        w_group(0, 0)
         x_turn(2, 2)
-        w_quant(0, 0)
         w_group(1, 0)
-        h_passes((0, 1), 0, (0,))
+        w_quant(0, 0)
         x_empty(2, 2, 0, "V")
+        x_turn(4, 1)
+        h_passes((0, 1), 0, (0,))
         x_empty(2, 2, 1, "S")
         x_empty(2, 2, 2, "S")
         w_quant(1, 0)
-        h_passes((0, 1), 1, (0,))
         x_quant(1, 0, 2)
-        w_group(0, 1)
-        x_quant(1, 2, 6)
+        h_passes((0, 1), 1, (0,))
+        x_empty(4, 1, 0, "S")
+        x_empty(4, 1, 1, "S")
         h_passes((2,), 0, (0,))
-        x_turn(4, 2)
-        w_quant(0, 1)
-        h_passes((0, 1, 2), 0, (1,))
-        w_group(1, 1)
-        x_empty(4, 2, 0, "V")
-        x_empty(4, 2, 1, "S")
-        x_empty(4, 2, 2, "S")
-        h_passes((3,), 0, (0, 1))
-        w_quant(1, 1)
-        h_passes((0, 1), 1, (1,))
+        x_quant(1, 2, 6)
+        h_passes((2,), 1, (0,))
+        h_passes((3,), 0, (0,))
         x_quant(2, 0, 2)
+        w_group(0, 1)
+        h_passes((4,), 0, (0,))
+        w_group(1, 1)
+        w_quant(0, 1)
+        h_passes(range(5), 0, (1,))
         w_group(0, 2)
-        x_quant(2, 2, 6)
-        h_passes((4,), 0, (0, 1))
+        w_quant(1, 1)
+        h_passes(range(3), 1, (1,))
+        x_quant(2, 2, 3)
         w_quant(0, 2)
-        h_passes((5,), 0, (0, 1))
+        h_passes(range(5), 0, (2,))
         w_group(1, 2)
-        h_passes(range(6), 0, (2,))
-        w_quant(1, 2)
+        x_sort(5, "S")
         h_add((0,), 0)
-        h_add((1, 2, 3), 0)
-        h_group(0, 0, "S")
-        h_passes((0, 1), 1, (2,))
-        h_passes((2,), 1, all_passes)
-        h_passes((3,), 1, all_passes)
+        w_quant(1, 2)
+        h_passes((3,), 1, (0, 1))
+        h_passes(range(4), 1, (2,))
+        h_add((1, 2), 0)
+        x_turn(5, 1)
         h_add((0, 1), 1)
-        h_passes((4,), 1, (0, 1))
         ht_turn(0)
         ht_turn(1)
-        h_add((2,), 1)
-        ht_empty(0, "V")
+        x_empty(5, 1, 0, "S")
+        ht_empty(0, "S")
+        x_empty(5, 1, 1, "S")
         ht_empty(1, "S")
         nc.scalar.copy(out=depth_f[:], in_=depth_bf[:].rearrange("p g t -> p (g t)"))
-        h_passes((4,), 1, (2,))
-        h_passes((5,), 1, all_passes)
+        h_add((3,), 0)
+        h_passes((4,), 1, all_passes)
+        x_quant(2, 3, 5)
         ht_quant(0, 1)
-        h_add((3,), 1)
-        x_sort(6, "V")
+        x_quant(2, 5, 6)
+        h_passes((5,), 0, all_passes)
+        h_add((2,), 1)
         ht_quant(1, 1)
-        x_sort(7, "V")
-
-        spectrum(0, banks=range(BINS - 1))
+        h_add((3,), 1)
+        spectrum(0)
         h_add((4,), 0)
-        spectrum(0, banks=(BINS - 1,))
         h_add((4,), 1)
+        h_passes((5,), 1, all_passes)
+        x_sort(6, "V")
+        x_sort(7, "V")
+        h_group(0, 0, "S", low)
         h_add((5,), 0)
-        h_add((5,), 1)
+        x_turn(6, 2)
+        x_empty(6, 2, 0, "S")
+        x_empty(6, 2, 1, "S")
         ht_turn(2)
         ht_turn(3)
-        x_turn(6, 2)
-        ht_empty(2, "S")
-        ht_empty(3, "S")
-        pop_widen_vector(0)
-        pop_widen_vector(1)
-        for n in range(3):
-            x_empty(6, 2, n, "SSS"[n])
-        ht_quant(2, 2)
-        spectrum(1)
-        pop_widen_vector(2)
-        pop_widen_vector(3)
+        x_empty(6, 2, 2, "V")
         x_quant(3, 0, 2)
         x_quant(3, 2, 6)
-        ht_turn(4)
-        ht_turn(5)
+        ht_empty(2, "S")
+        ht_empty(3, "S")
+        h_add((5,), 1)
+        spectrum(1)
+        ht_quant(2, 2)
+        pop_widen_vector(0)
+        pop_widen_vector(1)
+        h_passes((6,), 0, all_passes)
+        h_passes((6,), 1, all_passes)
+        h_group(0, 1, "S", slice(0, WORDS))
+        pop_widen_vector(2)
+        pop_widen_vector(3)
+        h_add((6,), 0)
+        h_add((6,), 1)
+        spectrum(2)
+        h_group(0, 0, "V", high)
+        for i in (4, 5, 6):
+            ht_turn(i)
+            ht_empty(i, "S")
         for z in range(2):
             for g in range(2):
                 pop_turn(g, z)
-        ht_empty(4, "S")
-        ht_empty(5, "S")
-        pop_empty(0, 0)
-        pop_empty(1, 0)
-        spectrum(2)
-        h_group(0, 1, "S")
-        pop_empty(0, 1)
-        ht_quant(4, 2)
-        pop_empty(1, 1)
-
-        for a in range(2):
-            h_passes((6 + a,), 0, all_passes)
-            spectrum(3, banks=(2 * a, 2 * a + 1))
+        h_group(0, 1, "V", slice(WORDS, BANK))
         h_quant(0, 0)
-        pop_quant(0)
-        h_add((6,), 0)
-        h_add((7,), 0)
-        pop_quant(1)
-        h_group(1, 0, "V")
-        for a in range(2):
-            h_passes((6 + a,), 1, all_passes)
-            h_add((6 + a,), 1)
-            spectrum(4, banks=(2 * a, 2 * a + 1))
-        h_quant(1, 0)
-        h_group(1, 1, "V")
+        pop_empty(0, 0)
+        ht_quant(4, 2)
+        spectrum(3, banks=(0, 1))
+        pop_empty(1, 0)
+        spectrum(3, banks=(2, 3))
+        pop_empty(0, 1)
+        spectrum(4)
+        h_passes((7,), 0, all_passes)
+        pop_empty(1, 1)
         h_quant(0, 1)
+        h_add((7,), 0)
+        ht_quant(6, 1)
         spectrum(5)
-
-        ht_turn(6)
+        h_group(1, 0, "V")
+        pop_quant(0)
+        h_passes((7,), 1, all_passes)
+        h_quant(1, 0)
+        h_add((7,), 1)
+        spectrum(6)
+        pop_quant(1)
+        h_group(1, 1, "V")
         ht_turn(7)
-        ht_empty(6, "V")
-        ht_empty(7, "S")
+        ht_empty(7, "V")
+        ht_quant(7, 1)
         h_quant(1, 1)
-        ht_quant(6, 2)
         for s in range(4):
             loading(s, 0, "S", 0)
         for s in range(4):
+            spectrum(7, banks=(s,), store_every=1)
             loading(s, 1, "V", 1)
-            spectrum(6, banks=(s,))
-        spectrum(7, banks=(0, 1))
-        spectrum(7, banks=(2, 3), store_every=1)

@@ -139,14 +139,6 @@ def tile_hrtf_weights_synthesis_s8_kernel(
         fetch_prior(3)
         nc.sync.dma_start(out=pop_sc[:], in_=pop_scale.rearrange("o (g p t) -> p (o g) t", p=P, t=4))
 
-        def warm_up(count):
-            bank = take_bank("warm")
-            for n in range(count):
-                nc.tensor.matmul(
-                    bank[:], lhsT=one[:].to_broadcast([P, P]), rhs=one[:].to_broadcast([P, BANK]), start=True, stop=True
-                )
-            give_bank("warm")
-
         def words(ap):
             return ap.bitcast(F32)
 
@@ -391,12 +383,10 @@ def tile_hrtf_weights_synthesis_s8_kernel(
 
         all_passes = range(K_PASSES)
         low, high = slice(0, WORDS), slice(WORDS, BANK)
-        warm_up(1)
         for i in (0, 1):
             x_turn(i, 1)
             x_empty(i, 1, 0, "V")
             x_empty(i, 1, 1, "S")
-        warm_up(2)
         x_quant(0, 0, 2)
         x_quant(0, 2, 6)
         w_group(0, 0)

@@ -87,8 +87,7 @@ def tile_hrtf_weights_synthesis_s8_kernel(
         pop_scales = [kept("pop_scales%d" % g, [P, R], U8) for g in range(2)]
 
         nc.vector.memset(one[:], 1.0)
-        nc.vector.memset(table_probe[:], 0.0)
-        nc.scalar.activation(out=table_probe[:], in_=table_probe[:], func=EXP)
+        nc.scalar.activation(out=table_probe[:], in_=one[:], func=EXP)
         make_identity(nc, ident[:])
         b_scales_i32 = b_scales[:].rearrange("p g n -> p (g n)").bitcast(I32)
         nc.gpsimd.memset(b_scales_i32, 0)
@@ -211,13 +210,12 @@ def tile_hrtf_weights_synthesis_s8_kernel(
 
         w_grouped = {}
 
-        def w_group(h, q, share=None):
-            tile = stage.tile([P, BANK, 4], BF16, name="w_grouped", bufs=3, align_bytes=256)
-            w_grouped[h, q] = tile
-            half = w_raw[q][:, :, h * BANK:(h + 1) * BANK]
-            share = share or VECTOR_COLS[h]
-            for engine, cols in (("V", slice(0, share)), ("S", slice(share, BANK))):
-                interleave(engine, tile[:, cols, :], half[:, :, cols])
+        def w_group(h, q, engine, first, last):
+            if (h, q) not in w_grouped:
+                tile = stage.tile([P, BANK, 4], BF16, name="w_grouped", bufs=3, align_bytes=256)
+                w_grouped[h, q] = tile
+            cols = slice(first, last)
+            interleave(engine, w_grouped[h, q][:, cols, :], w_raw[q][:, :, h * BANK:(h + 1) * BANK][:, :, cols])
 
         def w_quant(h, q, cols=slice(0, BANK)):
             values = w_grouped[h, q][:, cols, :].rearrange("p c t -> p (c t)")
@@ -389,9 +387,11 @@ def tile_hrtf_weights_synthesis_s8_kernel(
             x_empty(i, 1, 1, "S")
         x_quant(0, 0, 2)
         x_quant(0, 2, 6)
-        w_group(0, 0)
+        w_group(0, 0, "V", 0, 288)
+        w_group(0, 0, "S", 288, 512)
         x_turn(2, 2)
-        w_group(1, 0)
+        w_group(1, 0, "V", 0, 224)
+        w_group(1, 0, "S", 224, 512)
         w_quant(0, 0)
         x_empty(2, 2, 0, "V")
         x_turn(4, 1)
@@ -408,18 +408,22 @@ def tile_hrtf_weights_synthesis_s8_kernel(
         h_passes((2,), 1, (0,))
         h_passes((3,), 0, (0,))
         x_quant(2, 0, 2)
-        w_group(0, 1)
+        w_group(0, 1, "V", 0, 288)
+        w_group(0, 1, "S", 288, 512)
         h_passes((4,), 0, (0,))
-        w_group(1, 1)
+        w_group(1, 1, "V", 0, 224)
+        w_group(1, 1, "S", 224, 512)
         w_quant(0, 1)
         h_passes(range(5), 0, (1,))
-        w_group(0, 2)
+        w_group(0, 2, "V", 0, 288)
+        w_group(0, 2, "S", 288, 512)
         w_quant(1, 1)
         h_passes(range(3), 1, (1,))
         x_quant(2, 2, 3)
         w_quant(0, 2)
         h_passes(range(5), 0, (2,))
-        w_group(1, 2)
+        w_group(1, 2, "V", 0, 224)
+        w_group(1, 2, "S", 224, 512)
         x_sort(5, "S")
         h_add((0,), 0)
         w_quant(1, 2)
@@ -441,6 +445,7 @@ def tile_hrtf_weights_synthesis_s8_kernel(
         ht_quant(0, 1)
         x_quant(2, 5, 6)
         h_passes((5,), 0, all_passes)
+        h_group(0, 0, "S", low)
         h_add((2,), 1)
         ht_quant(1, 1)
         h_add((3,), 1)
@@ -450,41 +455,43 @@ def tile_hrtf_weights_synthesis_s8_kernel(
         h_passes((5,), 1, all_passes)
         x_sort(6, "V")
         x_sort(7, "V")
-        h_group(0, 0, "S", low)
         h_add((5,), 0)
+        pop_widen_vector(0)
         x_turn(6, 2)
         x_empty(6, 2, 0, "S")
         x_empty(6, 2, 1, "S")
         ht_turn(2)
-        ht_turn(3)
         x_empty(6, 2, 2, "V")
         x_quant(3, 0, 2)
-        x_quant(3, 2, 6)
-        ht_empty(2, "S")
-        ht_empty(3, "S")
         h_add((5,), 1)
-        spectrum(1)
-        ht_quant(2, 2)
-        pop_widen_vector(0)
+        x_quant(3, 2, 6)
         pop_widen_vector(1)
-        h_passes((6,), 0, all_passes)
-        h_passes((6,), 1, all_passes)
-        h_group(0, 1, "S", slice(0, WORDS))
+        ht_empty(2, "S")
+        spectrum(1)
+        ht_quant(2, 1)
         pop_widen_vector(2)
         pop_widen_vector(3)
-        h_add((6,), 0)
-        h_add((6,), 1)
-        spectrum(2)
-        h_group(0, 0, "V", high)
-        for i in (4, 5, 6):
+        h_passes((6,), 0, all_passes)
+        h_group(0, 1, "S", slice(0, P))
+        for i in (3, 4, 5):
             ht_turn(i)
             ht_empty(i, "S")
-        for z in range(2):
-            for g in range(2):
-                pop_turn(g, z)
-        h_group(0, 1, "V", slice(WORDS, BANK))
-        h_quant(0, 0)
+        pop_turn(0, 0)
+        h_passes((6,), 1, all_passes)
+        h_group(0, 1, "S", slice(P, WORDS))
+        h_add((6,), 0)
+        h_group(0, 0, "V", high)
         pop_empty(0, 0)
+        h_add((6,), 1)
+        spectrum(2)
+        ht_quant(3, 1)
+        ht_turn(6)
+        pop_turn(1, 0)
+        pop_turn(0, 1)
+        pop_turn(1, 1)
+        h_quant(0, 0)
+        ht_empty(6, "S")
+        h_group(0, 1, "V", high)
         ht_quant(4, 2)
         spectrum(3, banks=(0, 1))
         pop_empty(1, 0)
@@ -494,11 +501,11 @@ def tile_hrtf_weights_synthesis_s8_kernel(
         h_passes((7,), 0, all_passes)
         pop_empty(1, 1)
         h_quant(0, 1)
+        pop_quant(0)
         h_add((7,), 0)
         ht_quant(6, 1)
         spectrum(5)
         h_group(1, 0, "V")
-        pop_quant(0)
         h_passes((7,), 1, all_passes)
         h_quant(1, 0)
         h_add((7,), 1)

@@ -74,8 +74,8 @@ def tile_hrtf_weights_synthesis_s8_kernel(
         pop_sc = kept("pop_sc", [P, 2, 4], F32)
         one = kept("one", [P, 1], F32)
         pop_sorted = [kept("pop_sorted%d" % s, [P, M], BF16) for s in range(4)]
-        x_codes = [kept("x_codes%d" % j, [P, 2 * K_PASSES * P], U32) for j in range(4)]
-        x_scales = [kept("x_scales%d" % j, [P, 2 * K_PASSES * P], U8) for j in range(4)]
+        x_codes = kept("x_codes", [P, 8 * K_PASSES * P], U32)
+        x_scales = kept("x_scales", [P, 8 * K_PASSES * P], U8)
         w_codes = [[kept("w_codes%d%d" % (h, q), [P, BANK], U32) for q in range(K_PASSES)] for h in range(2)]
         w_scales = [[kept("w_scales%d%d" % (h, q), [P, BANK], U8) for q in range(K_PASSES)] for h in range(2)]
         h_bf = [[kept("h_bf%d%d" % (g, h), [P, 4 * BANK], BF16) for h in range(2)] for g in range(2)]
@@ -120,12 +120,12 @@ def tile_hrtf_weights_synthesis_s8_kernel(
             )
 
         fetch_x(0, 1)
-        fetch_x(1, 1)
         fetch_w(0)
+        fetch_x(1, 1)
         fetch_x(2, 1)
+        fetch_w(1)
         fetch_x(3, 1)
         fetch_x(4, 1)
-        fetch_w(1)
         fetch_w(2)
         fetch_prior(0)
         fetch_x(5, 1)
@@ -193,20 +193,28 @@ def tile_hrtf_weights_synthesis_s8_kernel(
                     nc.tensor.transpose(bank[:, col:col + P], src, ident[:])
 
         def x_empty(i, tiles, n, engine):
-            j, a = divmod(i, 2)
-            if j not in x_grouped:
-                tile = stage.tile([P, 2 * K_PASSES * PASS], BF16, name="x_grouped", align_bytes=256)
-                x_grouped[j] = tile
+            if i not in x_grouped:
+                tile = stage.tile([P, K_PASSES * PASS * tiles], BF16, name="x_grouped", align_bytes=256)
+                x_grouped[i] = tile
             count = min(2, K_PASSES * tiles - 2 * n)
-            first = PASS * (K_PASSES * a + 2 * n)
+            first = 2 * PASS * n
             copy(
                 engine,
-                words(x_grouped[j][:, first:first + PASS * count]).rearrange("p (a m u) -> p a m u", a=count, u=2),
+                words(x_grouped[i][:, first:first + PASS * count]).rearrange("p (a m u) -> p a m u", a=count, u=2),
                 give_bank(("x", i, n))[:, :WORDS * count].rearrange("p (a u m) -> p a m u", a=count, u=2),
             )
 
-        def x_quant(j, n0, n1):
-            quantize(x_codes[j][:, P * n0:P * n1], x_scales[j][:, P * n0:P * n1], x_grouped[j][:, PASS * n0:PASS * n1])
+        def x_quant(i, n0, n1):
+            cols = slice(P * (K_PASSES * i + n0), P * (K_PASSES * i + n1))
+            quantize(x_codes[:, cols], x_scales[:, cols], x_grouped[i][:, PASS * n0:PASS * n1])
+
+        def warm_up(count):
+            bank = take_bank("warm")
+            for n in range(count):
+                nc.tensor.matmul(
+                    out=bank[:], lhsT=x_raw[0][:, :P], rhs=x_raw[0][:, :BANK], start=True, stop=True
+                )
+            give_bank("warm")
 
         w_grouped = {}
 
@@ -225,11 +233,11 @@ def tile_hrtf_weights_synthesis_s8_kernel(
             for q in passes:
                 for i in tiles:
                     bank = take_bank(("h", i, h)) if q == 0 else bank_of["h", i, h][0]
-                    first = (K_PASSES * (i % 2) + q) * P
+                    first = (K_PASSES * i + q) * P
                     nc.tensor.matmul_mx(
                         out=bank[:, cols],
-                        lhsT=x_codes[i // 2][:, first:first + P].bitcast(E4M3),
-                        lhsT_scale=x_scales[i // 2][:, first:first + P],
+                        lhsT=x_codes[:, first:first + P].bitcast(E4M3),
+                        lhsT_scale=x_scales[:, first:first + P],
                         rhs=w_codes[h][q][:, cols].bitcast(E4M3),
                         rhs_scale=w_scales[h][q][:, cols],
                         start=(q == 0),
@@ -381,45 +389,51 @@ def tile_hrtf_weights_synthesis_s8_kernel(
 
         all_passes = range(K_PASSES)
         low, high = slice(0, WORDS), slice(WORDS, BANK)
-        for i in (0, 1):
-            x_turn(i, 1)
-            x_empty(i, 1, 0, "V")
-            x_empty(i, 1, 1, "S")
-        x_quant(0, 0, 2)
-        x_quant(0, 2, 6)
-        w_group(0, 0, "V", 0, 288)
-        w_group(0, 0, "S", 288, 512)
-        x_turn(2, 2)
-        w_group(1, 0, "V", 0, 224)
-        w_group(1, 0, "S", 224, 512)
+        x_turn(0, 1)
+        x_empty(0, 1, 0, "V")
+        x_empty(0, 1, 1, "S")
+        w_group(0, 0, "V", 0, 320)
+        w_group(0, 0, "S", 320, 512)
+        warm_up(4)
+        x_turn(1, 2, 0)
+        warm_up(1)
+        x_turn(1, 2, 1)
+        x_quant(0, 0, 3)
+        w_group(1, 0, "S", 384, 512)
         w_quant(0, 0)
-        x_empty(2, 2, 0, "V")
-        x_turn(4, 1)
-        h_passes((0, 1), 0, (0,))
-        x_empty(2, 2, 1, "S")
-        x_empty(2, 2, 2, "S")
-        w_quant(1, 0)
+        h_passes((0,), 0, (0,))
+        w_group(1, 0, "V", 0, 384)
+        x_empty(1, 2, 0, "S")
         x_quant(1, 0, 2)
+        h_passes((1,), 0, (0,))
+        w_quant(1, 0)
         h_passes((0, 1), 1, (0,))
-        x_empty(4, 1, 0, "S")
-        x_empty(4, 1, 1, "S")
+        x_empty(1, 2, 1, "S")
+        x_empty(1, 2, 2, "S")
+        x_quant(1, 2, 4)
         h_passes((2,), 0, (0,))
-        x_quant(1, 2, 6)
-        h_passes((2,), 1, (0,))
-        h_passes((3,), 0, (0,))
-        x_quant(2, 0, 2)
-        w_group(0, 1, "V", 0, 288)
-        w_group(0, 1, "S", 288, 512)
-        h_passes((4,), 0, (0,))
-        w_group(1, 1, "V", 0, 224)
-        w_group(1, 1, "S", 224, 512)
+        x_turn(3, 2, 0)
+        x_turn(3, 2, 1)
+        w_group(0, 1, "V", 0, 320)
+        w_group(0, 1, "S", 320, 512)
+        x_quant(1, 4, 6)
+        w_group(1, 1, "S", 320, 512)
         w_quant(0, 1)
-        h_passes(range(5), 0, (1,))
-        w_group(0, 2, "V", 0, 288)
-        w_group(0, 2, "S", 288, 512)
+        x_empty(3, 2, 0, "S")
+        w_group(1, 1, "V", 0, 320)
+        h_passes((0, 1, 2), 0, (1,))
+        h_passes((2,), 1, (0,))
+        x_empty(3, 2, 1, "S")
+        x_quant(3, 0, 2)
         w_quant(1, 1)
-        h_passes(range(3), 1, (1,))
-        x_quant(2, 2, 3)
+        h_passes((0, 1, 2), 1, (1,))
+        h_passes((3,), 0, (0, 1))
+        x_empty(3, 2, 2, "S")
+        x_quant(3, 2, 4)
+        w_group(0, 2, "V", 0, 320)
+        w_group(0, 2, "S", 320, 512)
+        x_quant(3, 4, 6)
+        h_passes((4,), 0, (0, 1))
         w_quant(0, 2)
         h_passes(range(5), 0, (2,))
         w_group(1, 2, "V", 0, 224)
@@ -441,9 +455,9 @@ def tile_hrtf_weights_synthesis_s8_kernel(
         nc.scalar.copy(out=depth_f[:], in_=depth_bf[:].rearrange("p g t -> p (g t)"))
         h_add((3,), 0)
         h_passes((4,), 1, all_passes)
-        x_quant(2, 3, 5)
+        x_quant(5, 0, 2)
         ht_quant(0, 1)
-        x_quant(2, 5, 6)
+        x_quant(5, 2, 3)
         h_passes((5,), 0, all_passes)
         h_group(0, 0, "S", low)
         h_add((2,), 1)
@@ -457,41 +471,38 @@ def tile_hrtf_weights_synthesis_s8_kernel(
         x_sort(7, "V")
         h_add((5,), 0)
         pop_widen_vector(0)
+        pop_widen_vector(1)
         x_turn(6, 2)
         x_empty(6, 2, 0, "S")
         x_empty(6, 2, 1, "S")
         ht_turn(2)
+        ht_turn(3)
         x_empty(6, 2, 2, "V")
-        x_quant(3, 0, 2)
-        h_add((5,), 1)
-        x_quant(3, 2, 6)
-        pop_widen_vector(1)
+        x_quant(6, 0, 2)
+        x_quant(6, 2, 6)
         ht_empty(2, "S")
+        ht_empty(3, "S")
+        h_add((5,), 1)
         spectrum(1)
-        ht_quant(2, 1)
+        ht_quant(2, 2)
+        h_passes((6,), 0, all_passes)
+        h_passes((6,), 1, all_passes)
+        h_group(0, 1, "S", slice(0, WORDS))
         pop_widen_vector(2)
         pop_widen_vector(3)
-        h_passes((6,), 0, all_passes)
-        h_group(0, 1, "S", slice(0, P))
-        for i in (3, 4, 5):
-            ht_turn(i)
-            ht_empty(i, "S")
-        pop_turn(0, 0)
-        h_passes((6,), 1, all_passes)
-        h_group(0, 1, "S", slice(P, WORDS))
         h_add((6,), 0)
-        h_group(0, 0, "V", high)
-        pop_empty(0, 0)
         h_add((6,), 1)
         spectrum(2)
-        ht_quant(3, 1)
-        ht_turn(6)
-        pop_turn(1, 0)
-        pop_turn(0, 1)
-        pop_turn(1, 1)
+        h_group(0, 0, "V", high)
+        for i in (4, 5, 6):
+            ht_turn(i)
+            ht_empty(i, "S")
+        for z in range(2):
+            for g in range(2):
+                pop_turn(g, z)
+        h_group(0, 1, "V", slice(WORDS, BANK))
         h_quant(0, 0)
-        ht_empty(6, "S")
-        h_group(0, 1, "V", high)
+        pop_empty(0, 0)
         ht_quant(4, 2)
         spectrum(3, banks=(0, 1))
         pop_empty(1, 0)
@@ -501,11 +512,11 @@ def tile_hrtf_weights_synthesis_s8_kernel(
         h_passes((7,), 0, all_passes)
         pop_empty(1, 1)
         h_quant(0, 1)
-        pop_quant(0)
         h_add((7,), 0)
         ht_quant(6, 1)
         spectrum(5)
         h_group(1, 0, "V")
+        pop_quant(0)
         h_passes((7,), 1, all_passes)
         h_quant(1, 0)
         h_add((7,), 1)

@@ -54,6 +54,11 @@ def tile_hrtf_weights_synthesis_s8_kernel(
             free_banks.append(number)
             return bank
 
+        def hold_back(key):
+            number = bank_of[key][1]
+            free_banks.remove(number)
+            free_banks.append(number)
+
         def kept(name, shape, dt):
             tile = keep.tile(shape, dt, name=name, align_bytes=256)
             return tile
@@ -132,8 +137,8 @@ def tile_hrtf_weights_synthesis_s8_kernel(
         fetch_prior(1)
         fetch_basis()
         nc.sync.dma_start(out=depth_bf[:], in_=depth.rearrange("(g p t) -> p g t", p=P, t=4))
-        fetch_prior(2)
         fetch_x(6, 2)
+        fetch_prior(2)
         nc.sync.dma_start(out=pop_raw[:], in_=pop_bytes.rearrange("(r s) k -> r s k", s=4))
         fetch_prior(3)
         nc.sync.dma_start(out=pop_sc[:], in_=pop_scale.rearrange("o (g p t) -> p (o g) t", p=P, t=4))
@@ -247,14 +252,27 @@ def tile_hrtf_weights_synthesis_s8_kernel(
         def h_row(i, h):
             return h_bf[i // 4][h][:, (i % 4) * BANK:(i % 4 + 1) * BANK]
 
-        def h_add(tiles, h):
+        parked = {}
+
+        def h_park(i, h):
+            tile = stage.tile([P, BANK], F32, name="parked", tag="grouped", bufs=4, align_bytes=256)
+            parked[i, h] = tile[:].rearrange("m (u p e) -> m u p e", u=2, e=2)
+            nc.scalar.copy(
+                out=parked[i, h], in_=give_bank(("h", i, h))[:].rearrange("m (p u e) -> m u p e", u=2, e=2)
+            )
+
+        def h_add(tiles, h, part=slice(0, 2)):
             for i in tiles:
+                if (i, h) in parked:
+                    total = parked[i, h]
+                else:
+                    total = give_bank(("h", i, h))[:].rearrange("m (p u e) -> m u p e", u=2, e=2)
                 nc.vector.tensor_tensor(
-                    out=h_row(i, h).rearrange("m (u p e) -> m u p e", u=2, e=2),
-                    in0=give_bank(("h", i, h))[:].rearrange("m (p u e) -> m u p e", u=2, e=2),
+                    out=h_row(i, h).rearrange("m (u p e) -> m u p e", u=2, e=2)[:, part],
+                    in0=total[:, part],
                     in1=prior_sb[i // 2][:, i % 2, h * BANK:(h + 1) * BANK].rearrange(
                         "m (p u e) -> m u p e", u=2, e=2
-                    ),
+                    )[:, part],
                     op=ADD,
                 )
 
@@ -399,10 +417,10 @@ def tile_hrtf_weights_synthesis_s8_kernel(
         warm_up(1)
         x_turn(1, 2, 1)
         x_quant(0, 0, 3)
-        w_group(1, 0, "S", 384, 512)
+        w_group(1, 0, "S", 320, 512)
         w_quant(0, 0)
         h_passes((0,), 0, (0,))
-        w_group(1, 0, "V", 0, 384)
+        w_group(1, 0, "V", 0, 320)
         x_empty(1, 2, 0, "S")
         x_quant(1, 0, 2)
         h_passes((1,), 0, (0,))
@@ -426,50 +444,64 @@ def tile_hrtf_weights_synthesis_s8_kernel(
         x_empty(3, 2, 1, "S")
         x_quant(3, 0, 2)
         w_quant(1, 1)
-        h_passes((0, 1, 2), 1, (1,))
         h_passes((3,), 0, (0, 1))
+        h_passes((0, 1, 2), 1, (1,))
         x_empty(3, 2, 2, "S")
         x_quant(3, 2, 4)
-        w_group(0, 2, "V", 0, 320)
-        w_group(0, 2, "S", 320, 512)
+        w_group(0, 2, "V", 0, 160)
+        w_group(0, 2, "S", 160, 256)
         x_quant(3, 4, 6)
         h_passes((4,), 0, (0, 1))
-        w_quant(0, 2)
-        h_passes(range(5), 0, (2,))
-        w_group(1, 2, "V", 0, 224)
-        w_group(1, 2, "S", 224, 512)
-        x_sort(5, "S")
+        w_group(0, 2, "S", 416, 512)
+        w_quant(0, 2, low)
+        h_passes(range(5), 0, (2,), low)
+        w_group(0, 2, "V", 256, 416)
+        w_group(1, 2, "V", 0, 96)
+        w_group(1, 2, "S", 96, 256)
+        w_quant(0, 2, high)
+        h_passes(range(5), 0, (2,), high)
+        w_group(1, 2, "V", 256, 352)
+        w_group(1, 2, "S", 352, 512)
+        w_quant(1, 2, low)
+        h_passes(range(3), 1, (2,), low)
+        w_quant(1, 2, high)
+        h_passes(range(3), 1, (2,), high)
         h_add((0,), 0)
-        w_quant(1, 2)
-        h_passes((3,), 1, (0, 1))
-        h_passes(range(4), 1, (2,))
-        h_add((1, 2), 0)
+        h_passes((3,), 1, all_passes)
+        x_sort(5, "S")
+        h_park(2, 0)
+        h_add((1,), 0)
+        h_park(4, 0)
         x_turn(5, 1)
         h_add((0, 1), 1)
         ht_turn(0)
         ht_turn(1)
+        h_add((3,), 0)
+        h_add((2,), 0, slice(0, 1))
         x_empty(5, 1, 0, "S")
-        ht_empty(0, "S")
         x_empty(5, 1, 1, "S")
+        ht_empty(0, "S")
         ht_empty(1, "S")
         nc.scalar.copy(out=depth_f[:], in_=depth_bf[:].rearrange("p g t -> p (g t)"))
-        h_add((3,), 0)
         h_passes((4,), 1, all_passes)
         x_quant(5, 0, 2)
-        ht_quant(0, 1)
         x_quant(5, 2, 3)
+        h_add((2,), 0, slice(1, 2))
+        ht_quant(0, 1)
         h_passes((5,), 0, all_passes)
         h_group(0, 0, "S", low)
         h_add((2,), 1)
         ht_quant(1, 1)
         h_add((3,), 1)
-        spectrum(0)
-        h_add((4,), 0)
-        h_add((4,), 1)
         h_passes((5,), 1, all_passes)
+        spectrum(0)
         x_sort(6, "V")
         x_sort(7, "V")
+        h_add((4,), 1)
         h_add((5,), 0)
+        hold_back(("mag", 0, 2))
+        hold_back(("mag", 0, 3))
+        h_add((4,), 0)
         pop_widen_vector(0)
         pop_widen_vector(1)
         x_turn(6, 2)

@@ -494,73 +494,70 @@ def tile_hrtf_weights_synthesis_s8_kernel(
         ht_quant(1, 1)
         h_add((3,), 1)
         h_passes((5,), 1, all_passes)
-        spectrum(0)
+        spectrum(0, store_every=BINS)
         x_sort(6, "V")
         x_sort(7, "V")
         h_add((4,), 1)
         h_add((5,), 0)
-        hold_back(("mag", 0, 2))
-        hold_back(("mag", 0, 3))
         h_add((4,), 0)
-        pop_widen_vector(0)
-        pop_widen_vector(1)
-        x_turn(6, 2)
-        x_empty(6, 2, 0, "S")
-        x_empty(6, 2, 1, "S")
-        ht_turn(2)
-        ht_turn(3)
-        x_empty(6, 2, 2, "V")
-        x_quant(6, 0, 2)
-        x_quant(6, 2, 6)
-        ht_empty(2, "S")
-        ht_empty(3, "S")
         h_add((5,), 1)
-        spectrum(1)
-        ht_quant(2, 2)
-        h_passes((6,), 0, all_passes)
-        h_passes((6,), 1, all_passes)
-        h_group(0, 1, "S", slice(0, WORDS))
-        pop_widen_vector(2)
-        pop_widen_vector(3)
-        h_add((6,), 0)
-        h_add((6,), 1)
-        spectrum(2)
+        spectrum(1, store_every=BINS)
+        for s in range(4):
+            pop_widen_vector(s)
+        for i in (2, 3):
+            ht_turn(i)
+            ht_empty(i, "S")
+        x_turn(6, 2)
         h_group(0, 0, "V", high)
-        for i in (4, 5, 6):
+        x_empty(6, 2, 0, "V")
+        x_empty(6, 2, 1, "S")
+        x_empty(6, 2, 2, "S")
+        for i in (4, 5):
             ht_turn(i)
             ht_empty(i, "S")
         for z in range(2):
             for g in range(2):
                 pop_turn(g, z)
-        h_group(0, 1, "V", slice(WORDS, BANK))
-        h_quant(0, 0)
+        ht_quant(2, 2)
         pop_empty(0, 0)
-        ht_quant(4, 2)
-        spectrum(3, banks=(0, 1))
+        x_quant(6, 0, 2)
+        x_quant(6, 2, 6)
+        spectrum(2)
         pop_empty(1, 0)
-        spectrum(3, banks=(2, 3))
+        h_passes((6,), 0, all_passes)
+        ht_quant(4, 2)
         pop_empty(0, 1)
-        spectrum(4)
-        h_passes((7,), 0, all_passes)
+        h_add((6,), 0)
+        spectrum(3)
+        h_group(0, 1, "S", low)
         pop_empty(1, 1)
-        h_quant(0, 1)
+        h_passes((6,), 1, all_passes)
+        h_quant(0, 0)
+        h_add((6,), 1)
+        h_passes((7,), 0, all_passes)
+        h_group(0, 1, "V", high)
         h_add((7,), 0)
-        ht_quant(6, 1)
-        spectrum(5)
-        h_group(1, 0, "V")
+        spectrum(4)
         pop_quant(0)
-        h_passes((7,), 1, all_passes)
-        h_quant(1, 0)
-        h_add((7,), 1)
-        spectrum(6)
+        h_group(1, 0, "V")
         pop_quant(1)
-        h_group(1, 1, "V")
+        spectrum(5, banks=(0, 1))
+        h_passes((7,), 1, all_passes)
+        h_add((7,), 1)
+        spectrum(5, banks=(2, 3))
+        h_quant(1, 0)
+        ht_turn(6)
         ht_turn(7)
-        ht_empty(7, "V")
-        ht_quant(7, 1)
-        h_quant(1, 1)
+        ht_empty(6, "V")
+        ht_empty(7, "S")
         for s in range(4):
             loading(s, 0, "S", 0)
+            if s == 0:
+                ht_quant(6, 2)
+        h_group(1, 1, "V")
+        h_quant(0, 1)
+        spectrum(6, store_every=1)
+        h_quant(1, 1)
         for s in range(4):
             spectrum(7, banks=(s,), store_every=1)
             loading(s, 1, "V", 1)

@@ -371,8 +371,9 @@ def tile_hrtf_weights_synthesis_s8_kernel(
                 op=MULT,
             )
 
-        def pop_quant(g):
-            quantize(pop_codes[g][:], pop_scales[g][:], pop_grouped[g][:])
+        def pop_quant(g, z):
+            cols = slice(2 * P * z, 2 * P * (z + 1))
+            quantize(pop_codes[g][:, cols], pop_scales[g][:, cols], pop_grouped[g][:, TURNED * z:TURNED * (z + 1)])
 
         load_rows = load.rearrange("(r s) c -> s r c", s=4)
         load_tiles = {}
@@ -501,63 +502,72 @@ def tile_hrtf_weights_synthesis_s8_kernel(
         h_add((5,), 0)
         h_add((4,), 0)
         h_add((5,), 1)
-        spectrum(1, store_every=BINS)
-        for s in range(4):
-            pop_widen_vector(s)
+        spectrum(1, banks=(0, 1))
+        h_group(0, 0, "V", high)
         for i in (2, 3):
             ht_turn(i)
-            ht_empty(i, "S")
+            ht_empty(i, "V")
         x_turn(6, 2)
-        h_group(0, 0, "V", high)
-        x_empty(6, 2, 0, "V")
-        x_empty(6, 2, 1, "S")
+        ht_quant(2, 1)
+        x_empty(6, 2, 0, "S")
+        x_empty(6, 2, 1, "V")
+        ht_quant(3, 1)
+        h_quant(0, 0)
         x_empty(6, 2, 2, "S")
         for i in (4, 5):
             ht_turn(i)
             ht_empty(i, "S")
+        spectrum(1, banks=(2, 3))
+        spectrum(2, store_every=BINS)
+        h_group(0, 1, "V", high)
+        x_quant(6, 0, 2)
+        x_quant(6, 2, 6)
+        h_passes((6,), 0, all_passes)
+        ht_quant(4, 2)
+        h_group(0, 1, "V", low)
+        h_add((6,), 0)
+        spectrum(3, store_every=BINS)
+        h_quant(0, 1)
+        h_passes((6,), 1, all_passes)
+        pop_widen_vector(0)
+        pop_widen_vector(1)
+        h_add((6,), 1)
+        h_passes((7,), 0, all_passes)
+        pop_widen_vector(2)
+        h_add((7,), 0)
+        spectrum(4)
+        pop_widen_vector(3)
+        h_group(1, 0, "V")
+        spectrum(5, banks=(0, 1))
+        h_passes((7,), 1, all_passes)
+        ht_turn(6)
+        ht_empty(6, "S")
+        h_quant(1, 0)
+        h_add((7,), 1)
         for z in range(2):
             for g in range(2):
                 pop_turn(g, z)
-        ht_quant(2, 2)
-        pop_empty(0, 0)
-        x_quant(6, 0, 2)
-        x_quant(6, 2, 6)
-        spectrum(2)
-        pop_empty(1, 0)
-        h_passes((6,), 0, all_passes)
-        ht_quant(4, 2)
-        pop_empty(0, 1)
-        h_add((6,), 0)
-        spectrum(3)
-        h_group(0, 1, "S", low)
-        pop_empty(1, 1)
-        h_passes((6,), 1, all_passes)
-        h_quant(0, 0)
-        h_add((6,), 1)
-        h_passes((7,), 0, all_passes)
-        h_group(0, 1, "V", high)
-        h_add((7,), 0)
-        spectrum(4)
-        pop_quant(0)
-        h_group(1, 0, "V")
-        pop_quant(1)
-        spectrum(5, banks=(0, 1))
-        h_passes((7,), 1, all_passes)
-        h_add((7,), 1)
-        spectrum(5, banks=(2, 3))
-        h_quant(1, 0)
-        ht_turn(6)
         ht_turn(7)
-        ht_empty(6, "V")
+        h_group(1, 1, "S", slice(0, 192))
         ht_empty(7, "S")
-        for s in range(4):
-            loading(s, 0, "S", 0)
-            if s == 0:
-                ht_quant(6, 2)
-        h_group(1, 1, "V")
-        h_quant(0, 1)
+        pop_empty(0, 0)
+        ht_quant(6, 1)
+        spectrum(5, banks=(2, 3), store_every=1)
+        pop_empty(1, 0)
+        ht_quant(7, 1)
         spectrum(6, store_every=1)
+        pop_empty(0, 1)
+        pop_quant(0, 0)
+        pop_empty(1, 1)
+        pop_quant(1, 0)
+        pop_quant(0, 1)
+        spectrum(7, store_every=1)
+        h_group(1, 1, "V", slice(192, BANK))
+        pop_quant(1, 1)
+        loading(0, 0, "S", 0)
+        loading(1, 0, "S", 0)
         h_quant(1, 1)
+        loading(2, 0, "S", 0)
+        loading(3, 0, "V", 0)
         for s in range(4):
-            spectrum(7, banks=(s,), store_every=1)
-            loading(s, 1, "V", 1)
+            loading(s, 1, "V" if s % 2 else "S", 1)

@@ -431,6 +431,7 @@ def tile_hrtf_weights_synthesis_s8_kernel(
         x_empty(1, 2, 2, "S")
         x_quant(1, 2, 4)
         h_passes((2,), 0, (0,))
+        warm_up(1)
         x_turn(3, 2, 0)
         x_turn(3, 2, 1)
         w_group(0, 1, "V", 0, 320)

@@ -413,9 +413,9 @@ def tile_hrtf_weights_synthesis_s8_kernel(
         x_empty(0, 1, 1, "S")
         w_group(0, 0, "V", 0, 320)
         w_group(0, 0, "S", 320, 512)
-        warm_up(4)
+        warm_up(3)
         x_turn(1, 2, 0)
-        warm_up(1)
+        warm_up(2)
         x_turn(1, 2, 1)
         x_quant(0, 0, 3)
         w_group(1, 0, "S", 320, 512)

@@ -183,9 +183,7 @@ def tile_hrtf_weights_synthesis_s8_kernel(
             )
 
         def x_turn(i, tiles, only=None):
-            for n in range(K_PASSES * tiles):
-                if only is not None and n // K_PASSES != only:
-                    continue
+            for n in range(K_PASSES * tiles) if only is None else only:
                 a, q = divmod(n, K_PASSES)
                 bank = take_bank(("x", i, n // 2)) if n % 2 == 0 else bank_of["x", i, n // 2][0]
                 for u in range(2):
@@ -414,9 +412,11 @@ def tile_hrtf_weights_synthesis_s8_kernel(
         w_group(0, 0, "V", 0, 320)
         w_group(0, 0, "S", 320, 512)
         warm_up(3)
-        x_turn(1, 2, 0)
-        warm_up(2)
-        x_turn(1, 2, 1)
+        x_turn(1, 2, range(0, 2))
+        warm_up(1)
+        x_turn(1, 2, range(2, 4))
+        warm_up(1)
+        x_turn(1, 2, range(4, 6))
         x_quant(0, 0, 3)
         w_group(1, 0, "S", 320, 512)
         w_quant(0, 0)
@@ -432,8 +432,7 @@ def tile_hrtf_weights_synthesis_s8_kernel(
         x_quant(1, 2, 4)
         h_passes((2,), 0, (0,))
         warm_up(1)
-        x_turn(3, 2, 0)
-        x_turn(3, 2, 1)
+        x_turn(3, 2)
         w_group(0, 1, "V", 0, 320)
         w_group(0, 1, "S", 320, 512)
         x_quant(1, 4, 6)

@@ -124,14 +124,14 @@ def tile_hrtf_weights_synthesis_s8_kernel(
                 in_=basis_words.bitcast(I32).rearrange("g p n -> p g n"),
             )
 
-        fetch_x(0, 1)
         fetch_w(0)
+        fetch_x(0, 1)
         fetch_x(1, 1)
         fetch_x(2, 1)
         fetch_w(1)
         fetch_x(3, 1)
-        fetch_x(4, 1)
         fetch_w(2)
+        fetch_x(4, 1)
         fetch_prior(0)
         fetch_x(5, 1)
         fetch_prior(1)
@@ -182,41 +182,36 @@ def tile_hrtf_weights_synthesis_s8_kernel(
                 engine, tile[:].rearrange("m (u n) -> m u n", u=2), x_words(i).rearrange("m (n u) -> m u n", u=2)
             )
 
-        def x_turn(i, tiles, only=None):
-            for n in range(K_PASSES * tiles) if only is None else only:
-                a, q = divmod(n, K_PASSES)
-                bank = take_bank(("x", i, n // 2)) if n % 2 == 0 else bank_of["x", i, n // 2][0]
+        def x_turn(first, count, only=None):
+            bank = bank_of["x", first][0] if ("x", first) in bank_of else take_bank(("x", first))
+            for n in only or range(count):
+                i, q = divmod(first + n, K_PASSES)
                 for u in range(2):
-                    if i + a in x_sorted:
-                        first = (K_PASSES * u + q) * P
-                        src = x_sorted[i + a][:, first:first + P]
+                    if i in x_sorted:
+                        start = (K_PASSES * u + q) * P
+                        src = x_sorted[i][:, start:start + P]
                     else:
-                        src = x_words(i + a)[:, WORDS * q + u:WORDS * (q + 1):2]
-                    col = (2 * (n % 2) + u) * P
+                        src = x_words(i)[:, WORDS * q + u:WORDS * (q + 1):2]
+                    col = (2 * n + u) * P
                     nc.tensor.transpose(bank[:, col:col + P], src, ident[:])
 
-        def x_empty(i, tiles, n, engine):
-            if i not in x_grouped:
-                tile = stage.tile([P, K_PASSES * PASS * tiles], BF16, name="x_grouped", align_bytes=256)
-                x_grouped[i] = tile
-            count = min(2, K_PASSES * tiles - 2 * n)
-            first = 2 * PASS * n
+        def x_empty(first, count, engine):
+            tile = stage.tile([P, 2 * PASS], BF16, name="x_grouped", bufs=6, align_bytes=256)
+            x_grouped[first] = tile
             copy(
                 engine,
-                words(x_grouped[i][:, first:first + PASS * count]).rearrange("p (a m u) -> p a m u", a=count, u=2),
-                give_bank(("x", i, n))[:, :WORDS * count].rearrange("p (a u m) -> p a m u", a=count, u=2),
+                words(tile[:, :PASS * count]).rearrange("p (a m u) -> p a m u", a=count, u=2),
+                give_bank(("x", first))[:, :WORDS * count].rearrange("p (a u m) -> p a m u", a=count, u=2),
             )
 
-        def x_quant(i, n0, n1):
-            cols = slice(P * (K_PASSES * i + n0), P * (K_PASSES * i + n1))
-            quantize(x_codes[:, cols], x_scales[:, cols], x_grouped[i][:, PASS * n0:PASS * n1])
+        def x_quant(first, count):
+            cols = slice(P * first, P * (first + count))
+            quantize(x_codes[:, cols], x_scales[:, cols], x_grouped[first][:, :PASS * count])
 
-        def warm_up(count):
+        def warm_up(count, lhsT, rhs):
             bank = take_bank("warm")
             for n in range(count):
-                nc.tensor.matmul(
-                    out=bank[:], lhsT=x_raw[0][:, :P], rhs=x_raw[0][:, :BANK], start=True, stop=True
-                )
+                nc.tensor.matmul(out=bank[:, :rhs.shape[1]], lhsT=lhsT, rhs=rhs, start=True, stop=True)
             give_bank("warm")
 
         w_grouped = {}
@@ -406,95 +401,107 @@ def tile_hrtf_weights_synthesis_s8_kernel(
 
         all_passes = range(K_PASSES)
         low, high = slice(0, WORDS), slice(WORDS, BANK)
-        x_turn(0, 1)
-        x_empty(0, 1, 0, "V")
-        x_empty(0, 1, 1, "S")
-        w_group(0, 0, "V", 0, 320)
-        w_group(0, 0, "S", 320, 512)
-        warm_up(3)
-        x_turn(1, 2, range(0, 2))
-        warm_up(1)
-        x_turn(1, 2, range(2, 4))
-        warm_up(1)
-        x_turn(1, 2, range(4, 6))
-        x_quant(0, 0, 3)
-        w_group(1, 0, "S", 320, 512)
+        warm_up(3, ident[:], ident[:])
+        warm_up(2, w_raw[0][:, 0, :P], w_raw[0][:, 0, :BANK])
+        w_group(0, 0, "V", 0, 336)
+        w_group(0, 0, "S", 336, 512)
+        x_turn(0, 2)
+        x_turn(2, 2)
+        x_turn(4, 2)
+        w_group(1, 0, "V", 0, 336)
+        w_group(1, 0, "S", 336, 512)
         w_quant(0, 0)
-        h_passes((0,), 0, (0,))
-        w_group(1, 0, "V", 0, 320)
-        x_empty(1, 2, 0, "S")
-        x_quant(1, 0, 2)
-        h_passes((1,), 0, (0,))
+        x_empty(0, 2, "S")
+        warm_up(1, w_raw[0][:, 0, :P], w_raw[0][:, 0, :BANK])
+        x_turn(6, 1)
+        x_turn(7, 2)
         w_quant(1, 0)
-        h_passes((0, 1), 1, (0,))
-        x_empty(1, 2, 1, "S")
-        x_empty(1, 2, 2, "S")
-        x_quant(1, 2, 4)
+        x_empty(2, 2, "S")
+        x_quant(0, 2)
+        x_empty(4, 2, "S")
+        h_passes((0,), 0, (0,))
+        h_passes((0,), 1, (0,))
+        x_quant(2, 2)
+        x_empty(6, 1, "S")
+        h_passes((1,), 0, (0,))
+        h_passes((1,), 1, (0,))
+        x_empty(7, 2, "S")
+        x_quant(4, 2)
+        x_quant(6, 1)
         h_passes((2,), 0, (0,))
-        warm_up(1)
-        x_turn(3, 2)
-        w_group(0, 1, "V", 0, 320)
-        w_group(0, 1, "S", 320, 512)
-        x_quant(1, 4, 6)
-        w_group(1, 1, "S", 320, 512)
-        w_quant(0, 1)
-        x_empty(3, 2, 0, "S")
-        w_group(1, 1, "V", 0, 320)
-        h_passes((0, 1, 2), 0, (1,))
         h_passes((2,), 1, (0,))
-        x_empty(3, 2, 1, "S")
-        x_quant(3, 0, 2)
-        w_quant(1, 1)
+        x_turn(9, 2)
+        x_turn(11, 1)
+        w_group(0, 1, "V", 0, 160)
+        w_group(0, 1, "S", 160, 256)
+        w_group(0, 1, "V", 256, 416)
+        w_group(0, 1, "S", 416, 512)
+        w_quant(0, 1, low)
+        x_quant(7, 2)
+        h_passes((0, 1, 2), 0, (1,), low)
+        w_quant(0, 1, high)
+        h_passes((0, 1, 2), 0, (1,), high)
+        w_group(1, 1, "S", 0, 224)
+        w_group(1, 1, "V", 224, 256)
+        w_group(1, 1, "V", 256, 512)
+        x_empty(9, 2, "S")
+        x_empty(11, 1, "S")
+        w_quant(1, 1, low)
+        h_passes((0, 1, 2), 1, (1,), low)
+        w_quant(1, 1, high)
+        h_passes((0, 1, 2), 1, (1,), high)
+        x_quant(9, 2)
         h_passes((3,), 0, (0, 1))
-        h_passes((0, 1, 2), 1, (1,))
-        x_empty(3, 2, 2, "S")
-        x_quant(3, 2, 4)
-        w_group(0, 2, "V", 0, 160)
-        w_group(0, 2, "S", 160, 256)
-        x_quant(3, 4, 6)
-        h_passes((4,), 0, (0, 1))
-        w_group(0, 2, "S", 416, 512)
+        h_passes((3,), 1, (0, 1))
+        w_group(0, 2, "S", 0, 192)
+        w_group(0, 2, "V", 192, 256)
+        x_quant(11, 1)
+        w_group(0, 2, "V", 256, 512)
+        w_group(1, 2, "S", 0, 256)
         w_quant(0, 2, low)
-        h_passes(range(5), 0, (2,), low)
-        w_group(0, 2, "V", 256, 416)
-        w_group(1, 2, "V", 0, 96)
-        w_group(1, 2, "S", 96, 256)
+        h_passes(range(4), 0, (2,), low)
         w_quant(0, 2, high)
-        h_passes(range(5), 0, (2,), high)
-        w_group(1, 2, "V", 256, 352)
-        w_group(1, 2, "S", 352, 512)
+        h_passes(range(4), 0, (2,), high)
+        w_group(1, 2, "V", 256, 512)
         w_quant(1, 2, low)
-        h_passes(range(3), 1, (2,), low)
+        h_passes(range(4), 1, (2,), low)
         w_quant(1, 2, high)
-        h_passes(range(3), 1, (2,), high)
-        h_add((0,), 0)
-        h_passes((3,), 1, all_passes)
+        h_passes(range(4), 1, (2,), high)
+        x_sort(4, "S")
         x_sort(5, "S")
+        h_add((0, 1), 0)
         h_park(2, 0)
-        h_add((1,), 0)
-        h_park(4, 0)
-        x_turn(5, 1)
+        h_park(3, 0)
+        x_turn(12, 1)
+        x_turn(13, 2)
         h_add((0, 1), 1)
+        x_turn(15, 2)
+        x_turn(17, 1)
+        x_empty(12, 1, "S")
         ht_turn(0)
         ht_turn(1)
-        h_add((3,), 0)
-        h_add((2,), 0, slice(0, 1))
-        x_empty(5, 1, 0, "S")
-        x_empty(5, 1, 1, "S")
+        x_empty(13, 2, "S")
+        x_quant(12, 1)
+        h_add((2,), 1)
+        x_empty(15, 2, "S")
+        x_quant(13, 2)
+        x_empty(17, 1, "S")
+        for q in all_passes:
+            for h in range(2):
+                h_passes((4,), h, (q,))
+        h_add((3,), 1)
+        x_quant(15, 2)
         ht_empty(0, "S")
         ht_empty(1, "S")
         nc.scalar.copy(out=depth_f[:], in_=depth_bf[:].rearrange("p g t -> p (g t)"))
-        h_passes((4,), 1, all_passes)
-        x_quant(5, 0, 2)
-        x_quant(5, 2, 3)
-        h_add((2,), 0, slice(1, 2))
-        ht_quant(0, 1)
+        x_quant(17, 1)
+        h_add((2,), 0)
         h_passes((5,), 0, all_passes)
-        h_group(0, 0, "S", low)
-        h_add((2,), 1)
-        ht_quant(1, 1)
-        h_add((3,), 1)
+        ht_quant(0, 1)
+        h_add((3,), 0)
         h_passes((5,), 1, all_passes)
+        ht_quant(1, 1)
+        h_group(0, 0, "S", low)
         spectrum(0, store_every=BINS)
         x_sort(6, "V")
         x_sort(7, "V")
@@ -507,21 +514,23 @@ def tile_hrtf_weights_synthesis_s8_kernel(
         for i in (2, 3):
             ht_turn(i)
             ht_empty(i, "V")
-        x_turn(6, 2)
+        for n in (18, 20, 22):
+            x_turn(n, 2)
         ht_quant(2, 1)
-        x_empty(6, 2, 0, "S")
-        x_empty(6, 2, 1, "V")
+        x_empty(18, 2, "S")
+        x_empty(20, 2, "V")
         ht_quant(3, 1)
         h_quant(0, 0)
-        x_empty(6, 2, 2, "S")
+        x_empty(22, 2, "S")
         for i in (4, 5):
             ht_turn(i)
             ht_empty(i, "S")
         spectrum(1, banks=(2, 3))
         spectrum(2, store_every=BINS)
         h_group(0, 1, "V", high)
-        x_quant(6, 0, 2)
-        x_quant(6, 2, 6)
+        x_quant(18, 2)
+        x_quant(20, 2)
+        x_quant(22, 2)
         h_passes((6,), 0, all_passes)
         ht_quant(4, 2)
         h_group(0, 1, "V", low)

@@ -137,8 +137,8 @@ def tile_hrtf_weights_synthesis_s8_kernel(
         fetch_prior(1)
         fetch_basis()
         nc.sync.dma_start(out=depth_bf[:], in_=depth.rearrange("(g p t) -> p g t", p=P, t=4))
-        fetch_x(6, 2)
         fetch_prior(2)
+        fetch_x(6, 2)
         nc.sync.dma_start(out=pop_raw[:], in_=pop_bytes.rearrange("(r s) k -> r s k", s=4))
         fetch_prior(3)
         nc.sync.dma_start(out=pop_sc[:], in_=pop_scale.rearrange("o (g p t) -> p (o g) t", p=P, t=4))
@@ -493,7 +493,6 @@ def tile_hrtf_weights_synthesis_s8_kernel(
         x_quant(15, 2)
         ht_empty(0, "S")
         ht_empty(1, "S")
-        nc.scalar.copy(out=depth_f[:], in_=depth_bf[:].rearrange("p g t -> p (g t)"))
         x_quant(17, 1)
         h_add((2,), 0)
         h_passes((5,), 0, all_passes)
@@ -502,38 +501,39 @@ def tile_hrtf_weights_synthesis_s8_kernel(
         h_passes((5,), 1, all_passes)
         ht_quant(1, 1)
         h_group(0, 0, "S", low)
+        nc.vector.tensor_copy(out=depth_f[:], in_=depth_bf[:].rearrange("p g t -> p (g t)"))
         spectrum(0, store_every=BINS)
-        x_sort(6, "V")
-        x_sort(7, "V")
+        h_add((4,), 0)
         h_add((4,), 1)
         h_add((5,), 0)
-        h_add((4,), 0)
         h_add((5,), 1)
         spectrum(1, banks=(0, 1))
-        h_group(0, 0, "V", high)
+        x_sort(6, "V")
+        x_sort(7, "V")
         for i in (2, 3):
             ht_turn(i)
             ht_empty(i, "V")
+        ht_turn(4)
+        ht_empty(4, "S")
+        ht_turn(5)
+        ht_empty(5, "S")
         for n in (18, 20, 22):
             x_turn(n, 2)
         ht_quant(2, 1)
-        x_empty(18, 2, "S")
-        x_empty(20, 2, "V")
+        x_empty(18, 2, "V")
+        x_empty(20, 2, "S")
         ht_quant(3, 1)
-        h_quant(0, 0)
-        x_empty(22, 2, "S")
-        for i in (4, 5):
-            ht_turn(i)
-            ht_empty(i, "S")
+        x_empty(22, 2, "V")
         spectrum(1, banks=(2, 3))
         spectrum(2, store_every=BINS)
-        h_group(0, 1, "V", high)
         x_quant(18, 2)
         x_quant(20, 2)
+        h_group(0, 0, "V", high)
         x_quant(22, 2)
         h_passes((6,), 0, all_passes)
         ht_quant(4, 2)
-        h_group(0, 1, "V", low)
+        h_quant(0, 0)
+        h_group(0, 1, "V")
         h_add((6,), 0)
         spectrum(3, store_every=BINS)
         h_quant(0, 1)

@@ -501,6 +501,7 @@ def tile_hrtf_weights_synthesis_s8_kernel(
         h_passes((5,), 1, all_passes)
         ht_quant(1, 1)
         h_group(0, 0, "S", low)
+        h_group(0, 0, "V", high)
         nc.vector.tensor_copy(out=depth_f[:], in_=depth_bf[:].rearrange("p g t -> p (g t)"))
         spectrum(0, store_every=BINS)
         h_add((4,), 0)
@@ -528,30 +529,30 @@ def tile_hrtf_weights_synthesis_s8_kernel(
         spectrum(2, store_every=BINS)
         x_quant(18, 2)
         x_quant(20, 2)
-        h_group(0, 0, "V", high)
         x_quant(22, 2)
         h_passes((6,), 0, all_passes)
         ht_quant(4, 2)
         h_quant(0, 0)
-        h_group(0, 1, "V")
+        pop_widen_vector(0)
+        h_group(0, 1, "V", high)
         h_add((6,), 0)
         spectrum(3, store_every=BINS)
-        h_quant(0, 1)
         h_passes((6,), 1, all_passes)
-        pop_widen_vector(0)
         pop_widen_vector(1)
+        pop_widen_vector(2)
         h_add((6,), 1)
         h_passes((7,), 0, all_passes)
-        pop_widen_vector(2)
+        h_group(0, 1, "S", low)
         h_add((7,), 0)
-        spectrum(4)
         pop_widen_vector(3)
+        spectrum(4)
         h_group(1, 0, "V")
+        h_quant(0, 1)
+        h_quant(1, 0)
         spectrum(5, banks=(0, 1))
         h_passes((7,), 1, all_passes)
         ht_turn(6)
         ht_empty(6, "S")
-        h_quant(1, 0)
         h_add((7,), 1)
         for z in range(2):
             for g in range(2):
@@ -565,14 +566,14 @@ def tile_hrtf_weights_synthesis_s8_kernel(
         pop_empty(1, 0)
         ht_quant(7, 1)
         spectrum(6, store_every=1)
-        pop_empty(0, 1)
         pop_quant(0, 0)
-        pop_empty(1, 1)
         pop_quant(1, 0)
-        pop_quant(0, 1)
+        pop_empty(0, 1)
+        pop_empty(1, 1)
         spectrum(7, store_every=1)
-        h_group(1, 1, "V", slice(192, BANK))
+        pop_quant(0, 1)
         pop_quant(1, 1)
+        h_group(1, 1, "V", slice(192, BANK))
         loading(0, 0, "S", 0)
         loading(1, 0, "S", 0)
         h_quant(1, 1)

@@ -401,7 +401,7 @@ def tile_hrtf_weights_synthesis_s8_kernel(
 
         all_passes = range(K_PASSES)
         low, high = slice(0, WORDS), slice(WORDS, BANK)
-        warm_up(3, ident[:], ident[:])
+        warm_up(1, ident[:], ident[:, :1].to_broadcast([P, BANK]))
         warm_up(2, w_raw[0][:, 0, :P], w_raw[0][:, 0, :BANK])
         w_group(0, 0, "V", 0, 336)
         w_group(0, 0, "S", 336, 512)

from contextlib import ExitStack

import concourse.mybir as mybir
from concourse.masks import make_identity

M, K, C, F, R = 1024, 1536, 1024, 2048, 512
FLOPS = 2 * (M * K * C + M * C * F + R * M * C)

F32 = mybir.dt.float32
BF16 = mybir.dt.bfloat16
U32 = mybir.dt.uint32
I32 = mybir.dt.int32
U8 = mybir.dt.uint8
E4M3 = mybir.dt.float8_e4m3fn_x4
E2M1 = mybir.dt.float4_e2m1fn_x4
FP8 = mybir.dt.float8_e4m3fn
ADD = mybir.AluOpType.add
MULT = mybir.AluOpType.mult
EXP = mybir.ActivationFunctionType.Exp

P = 128
PASS = 512
BANK = 512
WORDS = PASS // 2
TURNED = 2 * BANK
K_PASSES = K // PASS
BINS = F // BANK

VECTOR_COLS = (288, 224)


def tile_hrtf_weights_synthesis_s8_kernel(
    tc, x, w, prior, basis_words, basis_scales, depth, pop_bytes, pop_scale, mag, load
):
    nc = tc.nc
    with ExitStack() as ctx:
        keep = ctx.enter_context(tc.tile_pool(name="keep", bufs=1))
        stage = ctx.enter_context(tc.tile_pool(name="stage", bufs=2))
        shared = ctx.enter_context(tc.tile_pool(name="shared", bufs=4))
        psum = ctx.enter_context(tc.psum_pool(name="psum", bufs=1))
        ctx.enter_context(tc.manual_schedule())

        free_banks = list(range(8))
        bank_of = {}

        def take_bank(key):
            number = free_banks.pop(0)
            bank = psum.tile([P, BANK], F32, name="bank%d" % number)
            bank_of[key] = (bank, number)
            return bank

        def give_bank(key):
            bank, number = bank_of[key]
            free_banks.append(number)
            return bank

        def hold_back(key):
            number = bank_of[key][1]
            free_banks.remove(number)
            free_banks.append(number)

        def kept(name, shape, dt):
            tile = keep.tile(shape, dt, name=name, align_bytes=256)
            return tile

        ident = kept("ident", [P, P], F32)
        table_probe = kept("table_probe", [P, 1], F32)
        x_raw = [shared.tile([P, 2 * K], BF16, name="x_raw%d" % j, tag="x_mag", align_bytes=256) for j in range(4)]
        w_raw = [
            shared.tile([P, 4, C], BF16, name="w_raw%d" % q, tag="w_load", bufs=K_PASSES, align_bytes=256)
            for q in range(K_PASSES)
        ]
        prior_sb = [kept("prior%d" % j, [P, 2, C], BF16) for j in range(4)]
        b_words = kept("b_words", [P, 2, 2 * F], U8)
        b_scales = kept("b_scales", [P, 2, F], U8)
        depth_bf = kept("depth_bf", [P, 2, 4], BF16)
        depth_f = kept("depth_f", [P, 8], F32)
        pop_raw = kept("pop_raw", [P, 4, M], U8)
        pop_sc = kept("pop_sc", [P, 2, 4], F32)
        one = kept("one", [P, 1], F32)
        pop_sorted = [kept("pop_sorted%d" % s, [P, M], BF16) for s in range(4)]
        x_codes = kept("x_codes", [P, 8 * K_PASSES * P], U32)
        x_scales = kept("x_scales", [P, 8 * K_PASSES * P], U8)
        w_codes = [[kept("w_codes%d%d" % (h, q), [P, BANK], U32) for q in range(K_PASSES)] for h in range(2)]
        w_scales = [[kept("w_scales%d%d" % (h, q), [P, BANK], U8) for q in range(K_PASSES)] for h in range(2)]
        h_bf = [[kept("h_bf%d%d" % (g, h), [P, 4 * BANK], BF16) for h in range(2)] for g in range(2)]
        ht_codes = [kept("ht_codes%d" % j, [P, 4 * P], U32) for j in range(4)]
        ht_scales = [kept("ht_scales%d" % j, [P, 4 * P], U8) for j in range(4)]
        h_codes = [kept("h_codes%d" % g, [P, C], U32) for g in range(2)]
        h_scales = [kept("h_scales%d" % g, [P, C], U8) for g in range(2)]
        pop_codes = [kept("pop_codes%d" % g, [P, R], U32) for g in range(2)]
        pop_scales = [kept("pop_scales%d" % g, [P, R], U8) for g in range(2)]

        nc.vector.memset(one[:], 1.0)
        nc.scalar.activation(out=table_probe[:], in_=one[:], func=EXP)
        make_identity(nc, ident[:])
        b_scales_i32 = b_scales[:].rearrange("p g n -> p (g n)").bitcast(I32)
        nc.gpsimd.memset(b_scales_i32, 0)

        def fetch_x(i, tiles):
            g, t = divmod(i, 4)
            src = x[g * PASS:(g + 1) * PASS, :].rearrange("(p t) k -> p (t k)", t=4)
            nc.sync.dma_start(
                out=x_raw[i // 2][:, K * (i % 2):K * (i % 2 + tiles)], in_=src[:, K * t:K * (t + tiles)]
            )

        def fetch_w(q, cols=slice(0, C)):
            src = w[q * PASS:(q + 1) * PASS, :]
            nc.sync.dma_start(out=w_raw[q][:, :, cols], in_=src.rearrange("(p t) c -> p t c", t=4)[:, :, cols])

        def fetch_prior(j):
            g, t = divmod(2 * j, 4)
            src = prior[g * PASS:(g + 1) * PASS, :].rearrange("(p t) c -> p t c", t=4)
            nc.sync.dma_start(out=prior_sb[j][:], in_=src[:, t:t + 2, :])

        def fetch_basis():
            for row in range(4):
                nc.sync.dma_start(
                    out=b_scales_i32.rearrange("p (g n) -> p g n", g=2)[row:P:32],
                    in_=basis_scales.bitcast(I32)[:, row:16:4, :].rearrange("g quad n -> quad g n"),
                )
            nc.sync.dma_start(
                out=b_words[:].rearrange("p g n -> p (g n)").bitcast(I32).rearrange("p (g n) -> p g n", g=2),
                in_=basis_words.bitcast(I32).rearrange("g p n -> p g n"),
            )

        fetch_w(0)
        fetch_x(0, 1)
        fetch_x(1, 1)
        fetch_x(2, 1)
        fetch_w(1)
        fetch_x(3, 1)
        fetch_w(2)
        fetch_x(4, 1)
        fetch_prior(0)
        fetch_x(5, 1)
        fetch_prior(1)
        fetch_basis()
        nc.sync.dma_start(out=depth_bf[:], in_=depth.rearrange("(g p t) -> p g t", p=P, t=4))
        fetch_prior(2)
        fetch_x(6, 2)
        nc.sync.dma_start(out=pop_raw[:], in_=pop_bytes.rearrange("(r s) k -> r s k", s=4))
        fetch_prior(3)
        nc.sync.dma_start(out=pop_sc[:], in_=pop_scale.rearrange("o (g p t) -> p (o g) t", p=P, t=4))

        def words(ap):
            return ap.bitcast(F32)

        def copy(engine, out, in_):
            if engine == "S":
                nc.scalar.copy(out=out, in_=in_)
            else:
                nc.vector.tensor_copy(out=out, in_=in_)

        def quantize(codes, scales, values):
            nc.vector.quantize_mx(out=codes.bitcast(E4M3), scales=scales, in_=values)

        def empty_turned(engine, out, bank):
            copy(
                engine,
                words(out).rearrange("p (a m u) -> p a m u", a=2, u=2),
                bank[:].rearrange("p (a u m) -> p a m u", a=2, u=2),
            )

        def interleave(engine, out, in_):
            copy(
                engine,
                out.rearrange("p (c n) t -> p c t n", n=4),
                in_.rearrange("p t (c n) -> p c t n", n=4),
            )

        x_sorted = {}
        x_grouped = {}

        def x_words(i):
            return words(x_raw[i // 2][:, K * (i % 2):K * (i % 2 + 1)])

        def x_sort(i, engine):
            tile = stage.tile([P, K // 2], F32, name="x_sorted", align_bytes=256)
            x_sorted[i] = tile
            copy(
                engine, tile[:].rearrange("m (u n) -> m u n", u=2), x_words(i).rearrange("m (n u) -> m u n", u=2)
            )

        def x_turn(first, count, only=None):
            bank = bank_of["x", first][0] if ("x", first) in bank_of else take_bank(("x", first))
            for n in only or range(count):
                i, q = divmod(first + n, K_PASSES)
                for u in range(2):
                    if i in x_sorted:
                        start = (K_PASSES * u + q) * P
                        src = x_sorted[i][:, start:start + P]
                    else:
                        src = x_words(i)[:, WORDS * q + u:WORDS * (q + 1):2]
                    col = (2 * n + u) * P
                    nc.tensor.transpose(bank[:, col:col + P], src, ident[:])

        def x_empty(first, count, engine):
            tile = stage.tile([P, 2 * PASS], BF16, name="x_grouped", bufs=6, align_bytes=256)
            x_grouped[first] = tile
            copy(
                engine,
                words(tile[:, :PASS * count]).rearrange("p (a m u) -> p a m u", a=count, u=2),
                give_bank(("x", first))[:, :WORDS * count].rearrange("p (a u m) -> p a m u", a=count, u=2),
            )

        def x_quant(first, count):
            cols = slice(P * first, P * (first + count))
            quantize(x_codes[:, cols], x_scales[:, cols], x_grouped[first][:, :PASS * count])

        def warm_up(count, lhsT, rhs):
            bank = take_bank("warm")
            for n in range(count):
                nc.tensor.matmul(out=bank[:, :rhs.shape[1]], lhsT=lhsT, rhs=rhs, start=True, stop=True)
            give_bank("warm")

        w_grouped = {}

        def w_group(h, q, engine, first, last):
            if (h, q) not in w_grouped:
                tile = stage.tile([P, BANK, 4], BF16, name="w_grouped", bufs=3, align_bytes=256)
                w_grouped[h, q] = tile
            cols = slice(first, last)
            interleave(engine, w_grouped[h, q][:, cols, :], w_raw[q][:, :, h * BANK:(h + 1) * BANK][:, :, cols])

        def w_quant(h, q, cols=slice(0, BANK)):
            values = w_grouped[h, q][:, cols, :].rearrange("p c t -> p (c t)")
            quantize(w_codes[h][q][:, cols], w_scales[h][q][:, cols], values)

        def h_passes(tiles, h, passes, cols=slice(0, BANK)):
            for q in passes:
                for i in tiles:
                    bank = take_bank(("h", i, h)) if q == 0 else bank_of["h", i, h][0]
                    first = (K_PASSES * i + q) * P
                    nc.tensor.matmul_mx(
                        out=bank[:, cols],
                        lhsT=x_codes[:, first:first + P].bitcast(E4M3),
                        lhsT_scale=x_scales[:, first:first + P],
                        rhs=w_codes[h][q][:, cols].bitcast(E4M3),
                        rhs_scale=w_scales[h][q][:, cols],
                        start=(q == 0),
                        stop=(q == K_PASSES - 1 and cols.stop == BANK),
                    )

        def h_row(i, h):
            return h_bf[i // 4][h][:, (i % 4) * BANK:(i % 4 + 1) * BANK]

        parked = {}

        def h_park(i, h):
            tile = stage.tile([P, BANK], F32, name="parked", tag="grouped", bufs=4, align_bytes=256)
            parked[i, h] = tile[:].rearrange("m (u p e) -> m u p e", u=2, e=2)
            nc.scalar.copy(
                out=parked[i, h], in_=give_bank(("h", i, h))[:].rearrange("m (p u e) -> m u p e", u=2, e=2)
            )

        def h_add(tiles, h, part=slice(0, 2)):
            for i in tiles:
                if (i, h) in parked:
                    total = parked[i, h]
                else:
                    total = give_bank(("h", i, h))[:].rearrange("m (p u e) -> m u p e", u=2, e=2)
                nc.vector.tensor_tensor(
                    out=h_row(i, h).rearrange("m (u p e) -> m u p e", u=2, e=2)[:, part],
                    in0=total[:, part],
                    in1=prior_sb[i // 2][:, i % 2, h * BANK:(h + 1) * BANK].rearrange(
                        "m (p u e) -> m u p e", u=2, e=2
                    )[:, part],
                    op=ADD,
                )

        ht_grouped = {}

        def ht_turn(i):
            bank = take_bank(("ht", i))
            for h in range(2):
                for u in range(2):
                    col = (2 * h + u) * P
                    nc.tensor.transpose(bank[:, col:col + P], words(h_row(i, h))[:, u * P:(u + 1) * P], ident[:])

        def ht_empty(i, engine):
            j, a = divmod(i, 2)
            if a == 0:
                tile = stage.tile([P, 2 * TURNED], BF16, name="ht_grouped", align_bytes=256)
                ht_grouped[j] = tile
            empty_turned(engine, ht_grouped[j][:, TURNED * a:TURNED * (a + 1)], give_bank(("ht", i)))

        def ht_quant(i, tiles):
            j, a = divmod(i, 2)
            cols = slice(2 * P * a, 2 * P * (a + tiles))
            quantize(ht_codes[j][:, cols], ht_scales[j][:, cols], ht_grouped[j][:, TURNED * a:TURNED * (a + tiles)])

        mag_rows = mag.rearrange("(g p t) f -> g t p f", p=P, t=4)
        mag_tiles = {}

        def spectrum(i, banks=range(BINS), store_every=2):
            for f in banks:
                bank = take_bank(("mag", i, f))
                for h in range(2):
                    first = P * (2 * (i % 2) + h)
                    nc.tensor.matmul_mx(
                        out=bank[:],
                        lhsT=ht_codes[i // 2][:, first:first + P].bitcast(E4M3),
                        lhsT_scale=ht_scales[i // 2][:, first:first + P],
                        rhs=b_words[:, h, 2 * BANK * f:2 * BANK * (f + 1)].bitcast(E2M1),
                        rhs_scale=b_scales[:, h, BANK * f:BANK * (f + 1)],
                        start=(h == 0),
                        stop=(h == 1),
                    )
                if f == 0:
                    tile = shared.tile([P, F], F32, name="mag_out", tag="x_mag", align_bytes=256)
                    mag_tiles[i] = tile
                nc.scalar.activation(
                    out=mag_tiles[i][:, BANK * f:BANK * (f + 1)],
                    in_=give_bank(("mag", i, f))[:],
                    func=EXP,
                    scale=depth_f[:, i:i + 1],
                )
                if (f + 1) % store_every == 0:
                    cols = slice(BANK * (f + 1 - store_every), BANK * (f + 1))
                    nc.sync.dma_start(out=mag_rows[i // 4, i % 4, :, cols], in_=mag_tiles[i][:, cols])

        h_grouped = {}

        def h_group(g, h, engine, cols=slice(0, BANK)):
            if (g, h) not in h_grouped:
                tile = stage.tile([P, BANK, 4], BF16, name="grouped", bufs=4, align_bytes=256)
                h_grouped[g, h] = tile
            interleave(engine, h_grouped[g, h][:, cols, :], h_bf[g][h][:].rearrange("p (t c) -> p t c", t=4)[:, :, cols])

        def h_quant(g, h):
            cols = slice(BANK * h, BANK * (h + 1))
            quantize(h_codes[g][:, cols], h_scales[g][:, cols], h_grouped[g, h][:].rearrange("p c t -> p (c t)"))

        pop_grouped = {}

        def pop_widen_vector(s):
            nc.vector.tensor_scalar(
                out=pop_sorted[s][:].rearrange("r (u n e) -> r n u e", u=2, e=2),
                in0=pop_raw[:, s, :].bitcast(FP8).rearrange("r (n u e) -> r n u e", u=2, e=2),
                scalar1=one[:],
                scalar2=None,
                op0=MULT,
            )

        def pop_turn(g, z):
            bank = take_bank(("pop", g, z))
            for a in range(2):
                for u in range(2):
                    first = (2 * u + g) * P
                    col = (2 * u + a) * P
                    nc.tensor.transpose(
                        bank[:, col:col + P], words(pop_sorted[2 * z + a][:])[:, first:first + P], ident[:]
                    )

        def pop_empty(g, z):
            if z == 0:
                tile = stage.tile([P, 2 * TURNED], BF16, name="grouped", bufs=4, align_bytes=256)
                pop_grouped[g] = tile
            nc.vector.tensor_tensor(
                out=pop_grouped[g][:, TURNED * z:TURNED * (z + 1)].rearrange("p (r u e) -> p r u e", u=2, e=2),
                in0=give_bank(("pop", g, z))[:].bitcast(BF16).rearrange("p (u r e) -> p r u e", u=2, e=2),
                in1=pop_sc[:, g, :].rearrange("p (u e) -> p u e", u=2).unsqueeze(1).to_broadcast([P, 2 * P, 2, 2]),
                op=MULT,
            )

        def pop_quant(g, z):
            cols = slice(2 * P * z, 2 * P * (z + 1))
            quantize(pop_codes[g][:, cols], pop_scales[g][:, cols], pop_grouped[g][:, TURNED * z:TURNED * (z + 1)])

        load_rows = load.rearrange("(r s) c -> s r c", s=4)
        load_tiles = {}

        def loading(s, h, engine, store_from):
            bank = take_bank(("load", s, h))
            cols = slice(BANK * h, BANK * (h + 1))
            for g in range(2):
                nc.tensor.matmul_mx(
                    out=bank[:],
                    lhsT=pop_codes[g][:, P * s:P * (s + 1)].bitcast(E4M3),
                    lhsT_scale=pop_scales[g][:, P * s:P * (s + 1)],
                    rhs=h_codes[g][:, cols].bitcast(E4M3),
                    rhs_scale=h_scales[g][:, cols],
                    start=(g == 0),
                    stop=(g == 1),
                )
            if s // 2 not in load_tiles:
                tile = shared.tile([P, 2 * C], F32, name="load_out", tag="w_load", bufs=K_PASSES, align_bytes=256)
                load_tiles[s // 2] = tile
            first = C * (s % 2) + BANK * h
            out = load_tiles[s // 2][:, first:first + BANK]
            copy(
                engine,
                out.rearrange("r (p u e) -> r p u e", u=2, e=2),
                give_bank(("load", s, h))[:].rearrange("r (u p e) -> r p u e", u=2, e=2),
            )
            if store_from is not None:
                cols = slice(BANK * store_from, BANK * (h + 1))
                row = load_tiles[s // 2][:, C * (s % 2):C * (s % 2 + 1)]
                nc.sync.dma_start(out=load_rows[s, :, cols], in_=row[:, cols])

        all_passes = range(K_PASSES)
        low, high = slice(0, WORDS), slice(WORDS, BANK)
        warm_up(1, ident[:], ident[:, :1].to_broadcast([P, BANK]))
        warm_up(2, w_raw[0][:, 0, :P], w_raw[0][:, 0, :BANK])
        w_group(0, 0, "V", 0, 336)
        w_group(0, 0, "S", 336, 512)
        x_turn(0, 2)
        x_turn(2, 2)
        x_turn(4, 2)
        w_group(1, 0, "V", 0, 336)
        w_group(1, 0, "S", 336, 512)
        w_quant(0, 0)
        x_empty(0, 2, "S")
        warm_up(1, w_raw[0][:, 0, :P], w_raw[0][:, 0, :BANK])
        x_turn(6, 1)
        x_turn(7, 2)
        w_quant(1, 0)
        x_empty(2, 2, "S")
        x_quant(0, 2)
        x_empty(4, 2, "S")
        h_passes((0,), 0, (0,))
        h_passes((0,), 1, (0,))
        x_quant(2, 2)
        x_empty(6, 1, "S")
        h_passes((1,), 0, (0,))
        h_passes((1,), 1, (0,))
        x_empty(7, 2, "S")
        x_quant(4, 2)
        x_quant(6, 1)
        h_passes((2,), 0, (0,))
        h_passes((2,), 1, (0,))
        x_turn(9, 2)
        x_turn(11, 1)
        w_group(0, 1, "V", 0, 160)
        w_group(0, 1, "S", 160, 256)
        w_group(0, 1, "V", 256, 416)
        w_group(0, 1, "S", 416, 512)
        w_quant(0, 1, low)
        x_quant(7, 2)
        h_passes((0, 1, 2), 0, (1,), low)
        w_quant(0, 1, high)
        h_passes((0, 1, 2), 0, (1,), high)
        w_group(1, 1, "S", 0, 224)
        w_group(1, 1, "V", 224, 256)
        w_group(1, 1, "V", 256, 512)
        x_empty(9, 2, "S")
        x_empty(11, 1, "S")
        w_quant(1, 1, low)
        h_passes((0, 1, 2), 1, (1,), low)
        w_quant(1, 1, high)
        h_passes((0, 1, 2), 1, (1,), high)
        x_quant(9, 2)
        h_passes((3,), 0, (0, 1))
        h_passes((3,), 1, (0, 1))
        w_group(0, 2, "S", 0, 192)
        w_group(0, 2, "V", 192, 256)
        x_quant(11, 1)
        w_group(0, 2, "V", 256, 512)
        w_group(1, 2, "S", 0, 256)
        w_quant(0, 2, low)
        h_passes(range(4), 0, (2,), low)
        w_quant(0, 2, high)
        h_passes(range(4), 0, (2,), high)
        w_group(1, 2, "V", 256, 512)
        w_quant(1, 2, low)
        h_passes(range(4), 1, (2,), low)
        w_quant(1, 2, high)
        h_passes(range(4), 1, (2,), high)
        x_sort(4, "S")
        x_sort(5, "S")
        h_add((0, 1), 0)
        h_park(2, 0)
        h_park(3, 0)
        x_turn(12, 1)
        x_turn(13, 2)
        h_add((0, 1), 1)
        x_turn(15, 2)
        x_turn(17, 1)
        x_empty(12, 1, "S")
        ht_turn(0)
        ht_turn(1)
        x_empty(13, 2, "S")
        x_quant(12, 1)
        h_add((2,), 1)
        x_empty(15, 2, "S")
        x_quant(13, 2)
        x_empty(17, 1, "S")
        for q in all_passes:
            for h in range(2):
                h_passes((4,), h, (q,))
        h_add((3,), 1)
        x_quant(15, 2)
        ht_empty(0, "S")
        ht_empty(1, "S")
        x_quant(17, 1)
        h_add((2,), 0)
        h_passes((5,), 0, all_passes)
        ht_quant(0, 1)
        h_add((3,), 0)
        h_passes((5,), 1, all_passes)
        ht_quant(1, 1)
        h_group(0, 0, "S", low)
        h_group(0, 0, "V", high)
        nc.vector.tensor_copy(out=depth_f[:], in_=depth_bf[:].rearrange("p g t -> p (g t)"))
        spectrum(0, store_every=BINS)
        h_add((4,), 0)
        h_add((4,), 1)
        h_add((5,), 0)
        h_add((5,), 1)
        spectrum(1, banks=(0, 1))
        x_sort(6, "V")
        x_sort(7, "V")
        for i in (2, 3):
            ht_turn(i)
            ht_empty(i, "V")
        ht_turn(4)
        ht_empty(4, "S")
        ht_turn(5)
        ht_empty(5, "S")
        for n in (18, 20, 22):
            x_turn(n, 2)
        ht_quant(2, 1)
        x_empty(18, 2, "V")
        x_empty(20, 2, "S")
        ht_quant(3, 1)
        x_empty(22, 2, "V")
        spectrum(1, banks=(2, 3))
        spectrum(2, store_every=BINS)
        x_quant(18, 2)
        x_quant(20, 2)
        x_quant(22, 2)
        h_passes((6,), 0, all_passes)
        ht_quant(4, 2)
        h_quant(0, 0)
        pop_widen_vector(0)
        h_group(0, 1, "V", high)
        h_add((6,), 0)
        spectrum(3, store_every=BINS)
        h_passes((6,), 1, all_passes)
        pop_widen_vector(1)
        pop_widen_vector(2)
        h_add((6,), 1)
        h_passes((7,), 0, all_passes)
        h_group(0, 1, "S", low)
        h_add((7,), 0)
        pop_widen_vector(3)
        spectrum(4)
        h_group(1, 0, "V")
        h_quant(0, 1)
        h_quant(1, 0)
        spectrum(5, banks=(0, 1))
        h_passes((7,), 1, all_passes)
        ht_turn(6)
        ht_empty(6, "S")
        h_add((7,), 1)
        for z in range(2):
            for g in range(2):
                pop_turn(g, z)
        ht_turn(7)
        h_group(1, 1, "S", slice(0, 192))
        ht_empty(7, "S")
        pop_empty(0, 0)
        ht_quant(6, 1)
        spectrum(5, banks=(2, 3), store_every=1)
        pop_empty(1, 0)
        ht_quant(7, 1)
        spectrum(6, store_every=1)
        pop_quant(0, 0)
        pop_quant(1, 0)
        pop_empty(0, 1)
        pop_empty(1, 1)
        spectrum(7, store_every=1)
        pop_quant(0, 1)
        pop_quant(1, 1)
        h_group(1, 1, "V", slice(192, BANK))
        loading(0, 0, "S", 0)
        loading(1, 0, "S", 0)
        h_quant(1, 1)
        loading(2, 0, "S", 0)
        loading(3, 0, "V", 0)
        for s in range(4):
            loading(s, 1, "V" if s % 2 else "S", 1)
